import numpy as np, ml_dtypes
CORES = [48,51,52,55]
N = 4
BF = ml_dtypes.bfloat16
def gentries(a):
    return np.ascontiguousarray(a.reshape(8, 16, -1).transpose(0, 2, 1)).reshape(8, -1)
def gtable(e):
    e = np.asarray(e); return np.ascontiguousarray(e.reshape(8, -1, 16).transpose(0, 2, 1)).reshape(128, -1).astype(np.int32)
V, WN, M, S, RO, LIM, PEN, T0 = 4096, 2048, 256, 4, 2, 24, 37, 34816
H = WN // 2
def parts(rng):
    return rng.integers(0, 256, (N, 8, 16, V)), rng.integers(0, V, (N, 8, 16, WN)), rng.integers(0, V, (N, 8, M)), rng.integers(0, 256, (N, 8, 16, M))
def pack(X, O, v, z):
    return {"tracks": np.ascontiguousarray(X.reshape(N, 128, V)).astype(np.float32).astype(BF),
            "nb": np.ascontiguousarray((O[..., :H] + V * O[..., H:]).reshape(N, 128, H)).astype(np.int32),
            "v": np.stack([gtable(a) for a in v]), "z": np.ascontiguousarray(z.reshape(N, 128, M)).astype(np.float32).astype(BF)}
def bits(b):
    return 255 * ((np.asarray(b)[..., None] >> (15 - np.arange(16))) & 1)
def tune(b, goal):
    t = bits(b); t = t - LIM * (t > 0); need = int((goal - np.add.reduce((2 * np.arange(16) + 1) * t)) % V)
    for p in range(15, -1, -1):
        d = min(LIM, need // (2 * p + 1)); t[p] += d; need -= d * (2 * p + 1)
    return t
def ladder(z):
    t = np.tile(np.where(np.abs(z - 128) > 64, 128, 0), (3, 1)); t[:, 0] = z[0]
    for j in (1, 2, 3): t[j - 1, 4 - j] = z[4 - j] + (LIM + j) * (1 if z[4 - j] < 128 else -1)
    return t
def setup_inputs(rng):
    X, O, v, z = parts(rng)
    few = np.take_along_axis(rng.integers(0, V, (N, 8, 16)), rng.integers(0, 16, (N, 8, M)), 2)
    return pack(X, O, np.where(rng.random((N, 8, M)) < 0.25, few, v), z)
def uneven(rng, n):
    a = np.minimum((np.exp2(8 * rng.random((N, 8, 1, n))) * rng.random((N, 8, 16, n))).astype(np.int64), 255)
    return np.where(rng.random(a.shape) < 0.5, 255 - a, a)
def setup_inputs_spread(rng):
    O = np.minimum((V * rng.random((N, 8, 16, WN)) ** 3).astype(np.int64), V - 1); v = np.minimum((V * rng.random((N, 8, M)) ** 2).astype(np.int64), V - 1)
    return pack(uneven(rng, V), O, v, uneven(rng, M))
def setup_inputs_ends(rng):
    X, O, v, z = parts(rng)
    X = 255 * rng.integers(0, 2, X.shape); z = 255 * rng.integers(0, 2, z.shape)
    e = (V - 1) * rng.integers(0, 2, (N, 8, 16, H)); keep = rng.random((N, 8, 16, H)) < 0.75
    keep[..., 0] = True; keep[..., H - 1] = True; e[:, :, 14, H - 1] = V - 1; e[:, :, 15, H - 1] = 0; e[:, :, 14, 0] = 0; e[:, :, 15, 0] = V - 1
    O = np.concatenate([np.where(keep, e, O[..., :H]), np.where(keep, e, O[..., H:])], axis=3)
    v = np.where(rng.random(v.shape) < 0.75, (V - 1) * rng.integers(0, 2, v.shape), v)
    X[:, 1::2, :, V - 1] = X[:, 1::2, :, 0]
    z[..., M // 2:M // 2 + 8] = 255
    v[:, :, M - 2:] = V - 1; z[..., M - 1] = X[..., V - 1]; z[..., M - 2] = 255 - X[..., V - 1]
    v[:, :, :2] = 0; z[..., 0] = X[..., 0]; z[..., 1] = 255 - X[..., 0]
    return pack(X, O, v, z)
def setup_inputs_ties(rng):
    X, O, v, z = parts(rng)
    B = np.broadcast_to(rng.integers(60, 196, (1, 8, 16, 6)), (N, 8, 16, 6)); jog = np.array([LIM, LIM + 1, LIM + 2, LIM + 3, LIM + 4, -LIM, -LIM - 1, -LIM - 2])
    X = np.take_along_axis(B, np.broadcast_to(rng.integers(0, 6, (N, 8, 1, V)), X.shape), 3)
    X = np.where((rng.random((N, 8, 1, V)) < 0.5) & (rng.random(X.shape) < 0.15), X + rng.choice(jog, X.shape), X)
    z = np.take_along_axis(B, np.broadcast_to(rng.integers(0, 6, (N, 8, 1, M)), z.shape), 3)
    z = np.where(rng.random(z.shape) < 0.3, z + rng.choice(jog, z.shape), z)
    O[:, ::2] = np.tile(O[:, ::2, :4], (1, 1, 4, 1))
    return pack(X, O, v, z)
def calm(rng, X, O, v, z, g, low):
    for r in range(N):
        t = rng.integers(0, 256, 16); B = rng.permutation(V)[:5]; f, n, L = int(B[0]), int(B[1]), B[2:]
        w = rng.permutation(np.setdiff1d(np.arange(WN), np.array([f & (WN - 1)])))[:2]; go, end = int(w[0]), int(w[1])
        X[r, g][:, f] = t; X[r, g][:, n] = np.where(np.abs(t - 128) > 64, 128, 0); X[r, g][:, L] = ladder(t).T
        O[r, g][:, go] = f; O[r, g][:, end] = n; O[r, g][:, f & (WN - 1)] = L[rng.permutation(16) % 3]
        stay = np.ones(M, bool); z[r, g] = t[:, None]
        if r in low: stay = np.isin(np.arange(M), rng.permutation(M)[:low[r]])
        else: z[r, g][1:] = rng.integers(0, 256, (15, M))
        v[r, g] = np.where(stay, end, go) + WN * rng.integers(0, V // WN, M)
def setup_inputs_corners(rng):
    X, O, v, z = parts(rng); C = min(M // 4, WN // (4 * N)); own = 1 + np.arange(3 * N * C).reshape(N, 3, C); top = 3 * N * C + 1
    O[..., 0] = rng.choice(np.array([0, V - 1]), (N, 8, 16)); O[..., WN - 1] = rng.choice(np.array([0, V - 1]), (N, 8, 16))
    for r in range(N):
        for g in range(8):
            o = rng.permutation(M); rest = o[3 * C:]
            v[r, g, rest[::2]] = rng.choice(np.array([0, V - 1]), len(rest[::2]))
            for j in range(3):
                E = own[r, j]; ln = o[j * C:(j + 1) * C]; b = rng.integers(0, 65536, C); d = rng.integers(1, 1000, C)
                v[r, g, ln] = E + WN * rng.integers(0, V // WN, C); z[r, g][:, ln] = bits(b).T
                for s in range((S, 1, 2)[j]):
                    q = (r + s) % N
                    t = 65535 - (S - 1 - s) * d if j == 0 else np.full(C, T0 + j - 1)
                    b = b ^ (65535 - t); X[q, g][:, E] = bits(b).T
                    if j == 0:
                        O[q, g][:, E] = rng.integers(top, V, (16, C)); O[q, g][rng.integers(0, 16, C), E] = E
                    else: O[q, g][:, E] = E
    two = rng.permutation(8)[:2]; few = rng.permutation(4)
    for i in range(2): calm(rng, X, O, v, z, int(two[i]), {(i + 2 * j) % N: int(few[(i * (N // 2) + j) % 4]) for j in range(N // 2)})
    return pack(X, O, v, z)
def apart(rng, X, O, v, z, g, q, b):
    K = (S - 1) * M; E = rng.permutation(WN - 1)[:K]; E[K - 1] = WN - 1
    B = E + WN * rng.integers(0, V // WN, K); B[K - 1] = V - 1; B2 = (B[:M] + WN) % V
    left = int(np.setdiff1d(np.arange(WN), E)[0]); X[:, g, :, left] = 128
    for r in range(N):
        k = rng.integers(0, 16, K); k[K - 1] = 15
        X[r, g][:, B] = bits(int(b[r]))[:, None]; O[r, g][:, E] = left; O[r, g][k, E] = B
        if r == q:
            X[r, g][:, B2] = bits(65535 - int(b[q]))[:, None]; O[r, g][(k[:M] + 1 + rng.integers(0, 15, M)) % 16, E[:M]] = B2
    for s in range(1, S):
        r = (q - s) % N; v[r, g] = B[(s - 1) * M:s * M]
        for i in range(M): z[r, g, :, i] = tune(int(b[r]) ^ (65534 - T0), int(rng.integers(1, V)))
    v[q, g] = B2; z[q, g] = bits(65535 - int(b[q]))[:, None]
def setup_inputs_crowd(rng):
    X, O, v, z = parts(rng)
    v = np.take_along_axis(rng.integers(0, V, (N, 8, 3)), rng.integers(0, 3, (N, 8, M)), 2)
    o = rng.permutation(8)
    for i in range(7):
        g = int(o[i]); q = int(rng.integers(0, N)); a = int((V - 1, 0, WN, rng.integers(1, V - 1), V - 1, rng.integers(1, V - 1), 0)[i]); first = q - S + (2 if i < 2 else 1)
        t = np.sort(T0 + 2 + rng.permutation(65534 - T0)[:S - 1]); b = rng.integers(0, 65536, N)
        if i in (2, 3): t[S - 2] = t[S - 3]
        if i >= 4: t[S - 2] = 65535
        for j in range(1, S): b[(first + j) % N] = b[(first + j - 1) % N] ^ (65535 - int(t[j - 1]))
        b = b ^ (int(b[q]) ^ int(rng.integers(1, 65535)))
        if i == 6:
            apart(rng, X, O, v, z, g, q, b); continue
        for r in range(N): X[r, g, :, a] = bits(int(b[r]))
        O[:, g, :, a & (WN - 1)] = a
        if i == 0: X[:, g, :, 0] = 128; O[:, g, :15, a & (WN - 1)] = 0
        v[:, g] = (a + WN * rng.integers(0, V // WN, (N, M))) % V
        for r in range(N):
            m = T0 + 1
            if i in (2, 3) and r == q: m = T0
            if i in (2, 3) and r == (q - 1) % N: m = int(t[S - 2])
            if i >= 4 and r == q: m = 65535
            z[r, g] = tune(int(b[r]) ^ (65535 - m), V - 1)[:, None]
        if i in (2, 3):
            e = (a + 1 + np.arange(3)) % V
            X[q, g][:, e] = ladder(z[q, g, :, 0]).T; O[q, g, :, (a - 1) & (WN - 1)] = e[rng.permutation(16) % 3]
        if i == 2:
            y = tune(int(b[q]) ^ (65535 - T0), V - 2); z[q, g, :, 1::2] = y[:, None]
            f = (a + 4) % V; nx = (q + 1) % N; x = np.full(16, 128); x[[0, 4, 15]] = y[[0, 4, 15]]
            X[q, g, :, f] = x; O[q, g, :, (a - 2) & (WN - 1)] = f
            X[nx, g][:, e] = ladder(x).T; O[nx, g, :, f & (WN - 1)] = e[rng.permutation(16) % 3]
        if i == 1: z[q, g, :, M - 1] = bits(65535 - int(b[q]))
        if i == 3: z[q, g, :, M - 1] = bits(int(b[q]))
        if i == 5: z[q, g, :, M - max(1, S * M - 1024):] = bits(65535 - int(b[q]))[:, None]
    return pack(X, O, v, z)
def check_inputs(d):
    bad = []
    for k, hi in (("tracks", 255), ("nb", V * V - 1), ("v", V - 1), ("z", 255)):
        a = np.asarray(d[k]).astype(np.float64)
        if not np.all((a >= 0) & (a <= hi) & (a == np.floor(a))): bad.append("range of " + k)
    return bad
def reference(tracks, nb, v, z):
    X = np.ascontiguousarray(tracks.astype(np.float32).astype(np.int16).reshape(N, 8, 16, V).transpose(0, 1, 3, 2))
    a = nb.astype(np.int64).reshape(N, 8, 16, H)
    O = np.ascontiguousarray(np.concatenate([a & (V - 1), a // V], axis=3).transpose(0, 1, 3, 2))
    bo = np.stack([gentries(e) for e in v]).astype(np.int64)
    tr = np.ascontiguousarray(z.astype(np.float32).astype(np.int16).reshape(N, 8, 16, M).transpose(0, 1, 3, 2))
    r = np.arange(N)[:, None, None]; g = np.arange(8)[None, :, None]
    two = (1 << (15 - np.arange(16))).astype(np.int32); odd = 2 * np.arange(16) + 1
    settled = np.zeros((N, 8), np.int64)
    for rnd in range(RO):
        u = np.add.reduce(tr * odd, axis=-1) & (V - 1)
        vs, zs, mark, live, c, trail = bo, tr, np.full((N, 8, M), T0), np.ones((N, 8, M), bool), np.zeros((N, 8, M), np.int64), []
        for s in range(S):
            q = (r + s) % N; w = vs & (WN - 1)
            P = O[q, g, w]
            x = X[q[..., None], g[..., None], P]
            near = np.abs(x - zs[:, :, :, None, :]) <= LIM + (settled[q, g] & 3)[..., None, None]
            T = np.add.reduce(np.where(near, two, 0), axis=-1)
            k = np.argmax(T, axis=-1); best = np.max(T, axis=-1)
            go = live & (best > mark)
            nv = np.take_along_axis(P, k[..., None], 3)[..., 0]; nz = np.take_along_axis(x, k[..., None, None], 3)[:, :, :, 0]
            trail.append((w, k, nv))
            vs = np.where(go, nv, vs); zs = np.where(go[..., None], nz, zs); mark = np.where(go, best, mark); c = c + go; live = go
            if s == 0: z1 = zs
        hit = np.zeros((N, 8, V), bool); more = np.zeros((N, 8, WN, 16), np.int64); settled = np.zeros((N, 8), np.int64)
        G = np.broadcast_to(g, (N, 8, M))
        for s in range(S):
            w, k, nv = trail[s]; Q = np.broadcast_to((r + s) % N, (N, 8, M))
            e = c == s + 1; hit[Q[e], G[e], nv[e]] = True
            e = c > s + 1; np.add.at(more, (Q[e], G[e], w[e], k[e]), u[e])
            e = (c == s) if s < S - 1 else (c >= s)
            settled = settled + np.roll(np.add.reduce(e.astype(np.int64), axis=2), s, axis=0)
        X = np.where(hit[..., None], np.maximum(X - PEN, 0), X).astype(np.int16); O = (O + more) & (V - 1)
        bo = np.where(c > 0, vs, (bo + u) & (V - 1)); tr = np.where((c > 0)[..., None], (tr + z1) >> 1, tr).astype(np.int16)
    o = O.transpose(0, 1, 3, 2)
    return {"yx": np.ascontiguousarray(X.transpose(0, 1, 3, 2)).reshape(N, 128, V).astype(np.float32).astype(BF),
            "yn": np.ascontiguousarray(o[..., :H] + V * o[..., H:]).reshape(N, 128, H).astype(np.float32),
            "yv": np.stack([gtable(e) for e in bo]).astype(np.float32),
            "yz": np.ascontiguousarray(tr.transpose(0, 1, 3, 2)).reshape(N, 128, M).astype(np.float32).astype(BF)}

@@ -1,0 +1,613 @@
+from concourse.bass import DstId, RemoteDMATransfer
+from concourse.mybir import AluOpType as A, AxisListType, ActivationFunctionType as F
+
+BIG = float(2 ** 23)
+CF = float(3 * 2 ** 28)
+CB = float(3 * 2 ** 12)
+C2 = float(3 * 2 ** 23)
+C0 = 192.0
+S0 = 1.3046875
+PARAM = {"sv": ("00100001", "10101000", "11111100", "11101110"), "vg": ("01000100", "00011010", "00000000", "00000000"),
+         "pS": 1, "mS": 1, "gS": 1, "dS": 2, "wS": 0, "both": 0, "hold": 0.2, "lift": 1.0, "spare": 2, "nt": 2, "ahead": 3000.0,
+         "cyc": 1.04, "pe": 0.52, "ga": 1.56, "sc": 3.8, "lat": 70.0, "rem": 2500.0, "bw": 250.0}
+NS = 20
+
+SCRATCH = {
+    "X0": ("sbuf", [128, 4352], "bfloat16"), "X1": ("sbuf", [128, 4352], "bfloat16"), "X2": ("sbuf", [128, 4352], "bfloat16"),
+    "O0": ("sbuf", [128, 2048], "float32"), "O1": ("sbuf", [128, 2304], "float32"), "O2": ("sbuf", [128, 2304], "float32"),
+    "nbi": ("sbuf", [128, 1024], "int32"), "nbt": ("sbuf", [128, 2048], "int32"), "pk": ("sbuf", [128, 1024], "float32"),
+    "vi": ("sbuf", [128, 16], "int32"), "v0": ("sbuf", [128, 16], "float32"),
+    "zr": ("sbuf", [128, 2, 256], "bfloat16"), "zs": ("sbuf", [128, 2, 128], "float32"),
+    "LF": ("sbuf", [128, 12, 16], "float32"), "LB": ("sbuf", [128, 12, 16], "float32"), "LV": ("sbuf", [128, 4, 16], "float32"),
+    "LU": ("sbuf", [128, 4, 16], "float32"), "US": ("sbuf", [128, 2, 16], "float32"), "OB": ("sbuf", [128, 16, 32], "float32"),
+    "ui": ("sbuf", [128, 4, 16], "int32"), "vri": ("sbuf", [128, 8, 8], "int32"),
+    "sm": ("sbuf", [128, 8 * NS, 16], "float32"), "su": ("sbuf", [128, 8 * 5, 16], "uint16"),
+    "P16": ("sbuf", [128, 3, 128], "uint16"), "Pf": ("sbuf", [128, 3, 128], "float32"), "Pm": ("sbuf", [128, 2, 128], "float16"),
+    "OZ": ("sbuf", [128, 16, 128], "bfloat16"), "LZ": ("sbuf", [128, 12, 128], "bfloat16"),
+    "zT": ("sbuf", [128, 2, 128], "bfloat16"), "xg": ("sbuf", [128, 8, 512], "bfloat16"), "lv": ("sbuf", [128, 8, 512], "bfloat16"),
+    "near": ("sbuf", [128, 16, 256], "bfloat16"), "key": ("sbuf", [128, 2, 128], "float32"),
+    "nvs": ("sbuf", [128, 2, 128], "float32"), "nvr": ("sbuf", [128, 6, 128], "uint16"), "wr": ("sbuf", [128, 2, 128], "uint16"),
+    "wf": ("sbuf", [128, 2, 128], "float32"), "yo": ("sbuf", [128, 4, 256], "float32"),
+    "eqp": ("sbuf", [128, 32, 128], "bfloat16"), "eqe": ("sbuf", [128, 48, 128], "float16"), "lh": ("sbuf", [128, 16, 128], "float16"),
+    "pv": ("sbuf", [128, 6, 128], "bfloat16"), "cs": ("sbuf", [128, 2, 128], "float32"), "nw": ("sbuf", [128, 4, 128], "int32"),
+    "cnt": ("sbuf", [128, 96], "float32"), "col": ("sbuf", [128, 64], "float32"), "coli": ("sbuf", [128, 16], "int32"),
+    "colb": ("sbuf", [128, 8], "bfloat16"),
+    "iof": ("sbuf", [128, 144], "float32"), "cm": ("sbuf", [128, 256], "float32"), "jg": ("sbuf", [128, 128], "float32"),
+    "i2k": ("sbuf", [128, 2048], "float32"),
+    "ident": ("sbuf", [128, 128], "bfloat16"), "E": ("sbuf", [128, 2048], "bfloat16"),
+    "Z": ("sbuf", [128, 144], "bfloat16"), "Zu": ("sbuf", [128, 144], "bfloat16"), "BO": ("sbuf", [128, 128], "float32"),
+    "Wl": ("sbuf", [128, 8, 128], "bfloat16"), "pw": ("sbuf", [128, 128], "float32"),
+    "thr": ("sbuf", [128, 128], "bfloat16"), "offd": ("sbuf", [128, 128], "bfloat16"),
+    "ta": ("sbuf", [128, 10, 128], "float32"), "eye": ("sbuf", [128, 32], "bfloat16"), "iK": ("sbuf", [128, 128], "bfloat16"),
+    "d0T": ("sbuf", [128, 128], "float32"), "d0N": ("sbuf", [128, 256], "float32"), "dum": ("sbuf", [128, 32], "float32"),
+    "dgb": ("sbuf", [128, 2, 128], "bfloat16"), "BOh": ("sbuf", [128, 128], "bfloat16"),
+    "pd0": ("psum", [128, 512], "float32"), "pd1": ("psum", [128, 512], "float32"), "pd2": ("psum", [128, 512], "float32"),
+    "pT": ("psum", [128, 512], "float32"), "pz": ("psum", [128, 512], "float32"), "pS": ("psum", [128, 512], "float32"),
+    "pC": ("psum", [128, 512], "float32"), "pN": ("psum", [128, 512], "float32"),
+}
+PSUM = ("pd0", "pd1", "pd2", "pT", "pz", "pS", "pC", "pN")
+SEMAPHORES = (["cV", "cS", "cP", "cG", "sent"] + ["d%d" % i for i in range(20)] + ["f%d" % i for i in range(16)]
+              + ["t%d" % i for i in range(16)] + ["b%d" % i for i in range(16)] + ["u%d" % i for i in range(4)])
+ORDER = {}
+
+
+def make_ops(g, core, T, topo, rank, banks):
+    pr = PARAM
+    uses = [0]
+
+    def bank():
+        uses[0] += 1
+        name = "#%d" % uses[0]
+        return T[banks.get(name, PSUM[0])], name
+
+    cyc, pe = pr["cyc"], pr["pe"]
+    V, S, PE = g.vector, g.scalar, g.tensor
+    ops = []
+    ndma = [0]
+    lift = [0.0]
+    ahead = [0.0]
+
+    def op(eng, fn, cost, r, w, sems=None):
+        ops.append({"e": eng, "fn": fn, "c": cost, "r": list(r), "w": list(w), "sems": sems, "lift": lift[0], "first": ahead[0]})
+
+    def vc(n, c=1.0):
+        return max(64.0, n * c) * cyc
+
+    def ts(out, in0, s1, o0, s2, o1, n, r, w, c=1.0):
+        if o1 is None:
+            op("V", lambda: [V.tensor_scalar(out, in0, s1, None, o0)], vc(n, c), r, w)
+        else:
+            op("V", lambda: [V.tensor_scalar(out, in0, s1, s2, o0, o1)], vc(n, c), r, w)
+
+    def tt(out, a, b, o, n, r, w, c=2.0):
+        op("V", lambda: [V.tensor_tensor(out, a, b, o)], vc(n, c), r, w)
+
+    def cp(out, a, n, r, w, c=1.0):
+        op("V", lambda: [V.tensor_copy(out, a)], vc(n, c), r, w)
+
+    def vx(fn, n, r, w, per):
+        op("V", lambda: [fn()], 62.0 + n * per * cyc, r, w)
+
+    def scan(out, d0, d1, o0, o1, n, r, w, init=0.0):
+        op("V", lambda: [V.tensor_tensor_scan(out, d0, d1, init, o0, o1)], vc(n), r, w)
+
+    def ms(ap, val, n, w):
+        op("V", lambda: [V.memset(ap, val)], vc(n), [], w)
+
+    def act(out, in_, f, n, r, w, bias=None, scale=None, ind=False):
+        kw = {}
+        if bias is not None:
+            kw["bias"] = bias
+        if scale is not None:
+            kw["scale"] = scale
+        op("S", lambda: [S.activation(out, in_, f, **kw)], (80.0 + n * pr["ga"] * cyc) if ind else (vc(n) + 30.0), r, w)
+
+    def mm(out, pairs, n, r, w, passes=0):
+        def fn():
+            return [PE.matmul(out, l, x, i == 0, i == len(pairs) - 1) for i, (l, x) in enumerate(pairs)]
+        op("P", fn, (passes or len(pairs)) * max(64, n) * pe + 30.0, r, w)
+
+    def iota(out, pat, base, cm_, n, w, fl=True):
+        if fl:
+            op("G", lambda: [g.iota(out, pat, base, cm_, allow_small_or_imprecise_dtypes=True)], 160.0 + 2 * n * cyc, [], w)
+        else:
+            op("G", lambda: [g.iota(out, pat, base, cm_)], 160.0 + 2 * n * cyc, [], w)
+
+    def dma(out, in_, nbytes, r, w):
+        name = "d%d" % ndma[0]
+        ndma[0] += 1
+        op("Y", lambda: [g.sync.dma_start(out, in_)], nbytes / pr["bw"], r, w, {"": name})
+
+    def send(trs, r):
+        n = len(trs)
+        made, sems = [], {}
+        for i, (step, src, dst, sem, name) in enumerate(trs):
+            to = T.cores[(rank + step) % len(T.cores)]
+            en = topo.engines(core, to)
+            part = en[i * len(en) // n:(i + 1) * len(en) // n]
+            rid, pid, _se = topo.addr(to)
+            made.append((rid, pid, sum(1 << e for e in part), src, dst, sem))
+            sems[name] = (sem, len(part))
+
+        def fn():
+            if n == 1:
+                rid, pid, mask, src, dst, sem = made[0]
+                g.remote_dma(dst, src, T.sem[sem], T.sem.sent, pid, rid, mask)
+            else:
+                g.remote_dma_fused([RemoteDMATransfer(dst_ids=[DstId(rid=rid, pnc=pid)], dma_engine_mask=mask, remote_sem=T.sem[sem],
+                                                      src=src, dst=dst) for rid, pid, mask, src, dst, sem in made], local_sem=T.sem.sent)
+            return []
+        op("R", fn, 500.0, r, [t[4] for t in trs], sems)
+
+    X = [T.X0, T.X1, T.X2]
+    O = [T.O0, T.O1, T.O2]
+    col = lambda i: T.col[:, i:i + 1]
+    ta = lambda i: T.ta[:, i, :]
+
+    ahead[0] = 1e6
+    for c in range(2):
+        dma(T.nbi[:, 512 * c:512 * c + 512], T.nb[:, 512 * c:512 * c + 512], 262144, [], ["nbi%d" % c])
+    ahead[0] = 5e5
+    dma(T.vi[:], T.v[:], 30000, [], ["vi"])
+    dma(T.X0[:, 4096:4352], T.z[:], 65536, [], ["X0d"])
+    ahead[0] = 0.0
+    dma(T.X0[:, 0:4096], T.tracks[:], 1048576, [], ["X0"])
+    dma(T.X1[:, 0:4096], T.tracks[:], 1048576, [], ["X1"])
+
+    iota(T.coli[:, 0:1], [[0, 1]], 0, 1, 1, ["pi"], False)
+    iota(T.iof[:], [[1, 144]], 0, 0, 144, ["iof"])
+    iota(T.cm[:], [[0, 16], [1, 16]], 0, 0, 256, ["cm"])
+    iota(T.jg[:], [[16, 8], [0, 16]], 0, 0, 128, ["jg"])
+    iota(T.dum[:, 0:16], [[16, 16]], 4096, 0, 16, ["dumA"])
+    iota(T.dum[:, 16:32], [[16, 16]], 2048, 0, 16, ["dumB"])
+    iota(T.i2k[:], [[1, 2048]], 0, 0, 2048, ["i2k"])
+    cm = T.cm[:, 0:128]
+    cp(col(0), T.coli[:, 0:1], 1, ["pi"], ["c0"])
+    ts(T.coli[:, 4:5], T.coli[:, 0:1], 15, A.bitwise_and, None, None, 1, ["pi"], ["ai"])
+    cp(col(1), T.coli[:, 4:5], 1, ["ai"], ["c1"])
+    tt(col(2), col(0), col(1), A.subtract, 1, ["c0", "c1"], ["c2"])
+    act(col(3), col(2), F.Identity, 1, ["c2"], ["c3"], bias=15.0)
+    act(col(4), col(1), F.Identity, 1, ["c1"], ["c4"], bias=15.0, scale=-1.0)
+    act(col(5), col(1), F.Identity, 1, ["c1"], ["c5"], bias=1.0, scale=2.0)
+    ts(T.ident[:], T.iof[:, 0:128], col(0), A.is_equal, None, None, 128, ["iof", "c0"], ["ident"])
+    act(T.dgb[:, 0, :], T.ident[:], F.Copy, 128, ["ident"], ["dgb0"], scale=S0)
+    for k in range(16):
+        act(T.E[:, k:2048:16], T.ident[:], F.Copy, 128, ["ident"], ["E%d" % k], scale=-1.0)
+    EK = ["E%d" % k for k in range(16)]
+    ms(ta(0), 0.5, 128, ["ta0"])
+    ms(ta(1), 0.0, 128, ["ta1"])
+    scan(T.pw[:], ta(0), ta(1), A.mult, A.add, 128, ["ta0", "ta1"], ["pw"], float(2 ** 64))
+    ts(ta(2), cm, col(1), A.is_equal, None, None, 128, ["cm", "c1"], ["ta2"])
+    tt(ta(3), ta(2), T.pw[:], A.mult, 128, ["ta2", "pw"], ["ta3"])
+    op("V", lambda: [V.tensor_reduce(col(7), T.ta[:, 3, 0:16], AxisListType.X, A.add)], vc(16), ["ta3"], ["c7"])
+    act(col(8), col(7), F.Copy, 1, ["c7"], ["c8"], scale=float(2.0 ** -42))
+    ts(T.Z[:], T.iof[:], col(3), A.is_equal, col(8), A.mult, 144, ["iof", "c3", "c8"], ["Z"])
+    ts(T.Zu[:], T.iof[:], col(3), A.is_equal, col(5), A.mult, 144, ["iof", "c3", "c5"], ["Zu"])
+    ts(T.BO[:], T.jg[:], col(2), A.is_equal, None, None, 128, ["jg", "c2"], ["BO"])
+    act(T.Wl[:, 0, :], T.BO[:], F.Copy, 128, ["BO", "c7"], ["Wl0"], scale=col(7))
+    for b in range(1, 8):
+        act(T.Wl[:, b, :], T.Wl[:, 0, :], F.Copy, 128, ["Wl0"], ["Wl%d" % b], scale=float(2.0 ** (-16 * b)))
+    WL = ["Wl%d" % b for b in range(8)]
+    ts(ta(4), cm, col(1), A.not_equal, -1e29, A.mult, 128, ["cm", "c1"], ["ta4"])
+    act(T.offd[:], ta(4), F.Identity, 128, ["ta4"], ["offd"], bias=2048.0)
+    act(T.BOh[:], T.BO[:], F.Copy, 128, ["BO"], ["BOh"])
+    act(ta(5), ta(3), F.Copy, 128, ["ta3"], ["ta5"], scale=-2.5)
+    tt(T.thr[:], ta(4), ta(5), A.add, 128, ["ta4", "ta5"], ["thr"])
+    ts(T.eye[:], T.iof[:, 0:32], col(4), A.is_equal, None, None, 32, ["iof", "c4"], ["eye"])
+    act(ta(6), cm, F.Identity, 128, ["cm"], ["ta6"], bias=51.0, scale=-1.0)
+    tt(ta(7), ta(6), T.BO[:], A.mult, 128, ["ta6", "BO"], ["ta7"])
+    act(T.iK[:], ta(7), F.Identity, 128, ["ta7"], ["iK"], bias=-100.0)
+    ts(ta(8), cm, 0.0, A.is_equal, -BIG - 1.0, A.mult, 128, ["cm"], ["ta8"])
+    act(T.d0T[:], ta(8), F.Identity, 128, ["ta8"], ["d0T"], bias=1.0)
+    ts(T.d0N[:], T.cm[:], 0.0, A.is_equal, -9e29, A.mult, 256, ["cm"], ["d0N"])
+    ts(T.dum[:], T.dum[:], col(1), A.add, None, None, 32, ["dumA", "dumB", "c1"], ["dumA", "dumB", "dum"])
+    for W, wk, c in ((T.X1, "X1d", 4096), (T.X2, "X2d", 4096), (T.O1, "O1d", 2048), (T.O2, "O2d", 2048)):
+        act(W[:, c:c + 256], T.cm[:], F.Copy, 256, ["cm"], [wk])
+
+    for c in range(2):
+        for hi in range(2):
+            a = 1024 * hi + 512 * c
+            ts(T.nbt[:, a:a + 512], T.nbi[:, 512 * c:512 * c + 512], 12 if hi else 4095, A.logical_shift_right if hi else A.bitwise_and,
+               None, None, 512, ["nbi%d" % c], ["nbt%d" % a])
+            cp(T.O0[:, a:a + 512], T.nbt[:, a:a + 512], 512, ["nbt%d" % a], ["O0/%d" % a])
+    OK = [["O0/%d" % a for a in range(0, 2048, 512)], ["O1"]]
+    dma(T.O1[:, 0:2048], T.O0[:, 0:2048], 1048576, OK[0], ["O1"])
+    cp(T.v0[:], T.vi[:], 16, ["vi"], ["v0"])
+
+    chunk = [0]
+    sml = lambda st, i, hs: T.sm[:, NS * st + i, 8 * hs[0]:8 * hs[-1] + 8]
+    sul = lambda st, i, hs: T.su[:, 5 * st + i, 8 * hs[0]:8 * hs[-1] + 8]
+    ks = lambda n, st, hs: ["%s/%d" % (n, 2 * st + h) for h in hs]
+
+    def first(st, hs, i, eq, ek, key, kn, d0, on):
+        n, c0 = len(hs), 128 * hs[0]
+        ps, pn = bank()
+        pairs = []
+        for h in hs:
+            e0, names = ek(h)
+            mm(ps[:, 128 * h:128 * h + 128], [(T.Wl[:, b, :], eq[:, e0 + b, :]) for b in range(8)] + [(T.ident[:], T.thr[:])], 128,
+               WL + [x for h_ in hs for x in ek(h_)[1]] + ["ident", "thr"], [pn])
+        yi = 2 * i + st % 2
+        yk = ["yo%d/%d" % (yi, h) for h in hs]
+        scan(T.yo[:, yi, c0:c0 + 128 * n], T.d0N[:, 0:128 * n], ps[:, c0:c0 + 128 * n], A.add, A.max, 128 * n, ["d0N", pn], yk)
+        sm = lambda j: sml(st, 10 + 3 * i + j, hs)
+        k = lambda x: ks("%s%d" % (x, i), st, hs)
+        ends = T.yo[:, yi, c0 + 15:c0 + 128 * n:16]
+        if pr["dS"] == 1 or (pr["dS"] == 2 and i == 1 and st % 4 > 1):
+            act(sm(0), ends, F.Sign, 8, yk, k("d"))
+        else:
+            ts(sm(0), ends, 0.0, A.is_gt, None, None, 8, yk, k("d"))
+        tt(sm(1), sm(0), T.dum[:, d0 + 8 * hs[0]:d0 + 8 * hs[-1] + 8], A.mult, 8, k("d") + ["dum"], k("e"))
+        tt(sm(2), sm(1), sml(st, key, hs), A.max, 8, k("e") + ks(kn, st, hs), k("o"))
+        cp(sul(st, 3 + i, hs), sm(2), 8, k("o"), ks(on, st, hs))
+
+    def station(rd, s, h):
+        st = 4 * rd + s
+        U = 2 * st + h
+        k = lambda n: "%s/%d" % (n, U)
+        Xg, Og, xk, ok = X[rd], O[rd], "X%d" % rd, OK[rd]
+        sm = lambda i: sml(st, i, [h])
+        su = lambda i: sul(st, i, [h])
+        ob = lambda a, b: T.OB[:, U, a - 128:b - 128] if a else T.OZ[:, U, :]
+        y = U % 6
+        dm = T.dum[:, 8 * h:8 * h + 8]
+        if s == 0:
+            v, vk = (T.v0[:, 8 * h:8 * h + 8], "v0") if rd == 0 else (T.LV[:, h, 0:8], "LV/%d" % h)
+            z, zk = (T.X0[:, 4096 + 128 * h:4224 + 128 * h], "X0d") if rd == 0 else (T.zr[:, 0, 128 * h:128 * h + 128], "zr0/%d" % h)
+        else:
+            li = 6 * rd + 2 * (s - 1) + h
+            v, vk, z, zk = T.LF[:, li, 0:8], k("LL"), T.LZ[:, li, :], k("LF")
+        ts(sm(0), v, 2048.0, A.is_ge, -2048.0, A.mult, 8, [vk], [k("s0")])
+        tt(sm(7), v, sm(0), A.add, 8, [vk, k("s0")], [k("wf")])
+        cp(su(0), sm(7), 8, [k("wf")], [k("w")])
+        p3, u2 = U % 3, U % 2
+        act(T.Pf[:, p3, :], Og[:, 0:2048].indirect(su(0)), F.Identity, 128, ok + [k("w")], ["Pf%d" % p3], ind=True, bias=-2048.0)
+        if pr["pS"]:
+            ts(T.P16[:, p3, :], T.Pf[:, p3, :], 2048.0, A.add, None, None, 128, ["Pf%d" % p3], ["P16%d" % p3])
+        else:
+            vx(lambda: V.tensor_copy(T.P16[:, p3, :], Og[:, 0:2048].indirect(su(0))), 128, ok + [k("w")], ["P16%d" % p3], pr["ga"])
+        ps, pn = bank()
+        mm(ps[:, 0:128], [(z, T.dgb[:, rd, :])], 128, [zk, "dgb%d" % rd], [pn])
+        act(T.zT[:, u2, :], ps[:, 0:128], F.Identity, 128, [pn], ["zT%d" % u2], bias=-C0)
+        for c in range(4):
+            n = chunk[0]
+            chunk[0] += 1
+            xb = n % 8
+            ps, pk_ = bank()
+            win = Xg[:, 0:4096].indirect(T.P16[:, p3, 32 * c:32 * c + 32])
+            xo = T.xg[:, xb, :]
+            if pr["vg"][s][4 * h + c] == "1":
+                vx(lambda xo=xo, win=win: V.tensor_copy(xo, win), 512, [xk, "P16%d" % p3], ["xg%d" % xb], pr["ga"])
+            else:
+                act(xo, win, F.Copy, 512, [xk, "P16%d" % p3], ["xg%d" % xb], ind=True)
+            mm(ps[:], [(T.dgb[:, rd, :], xo), (T.zT[:, u2, :], T.E[:, 512 * c:512 * c + 512])], 512,
+               ["dgb%d" % rd, "xg%d" % xb, "zT%d" % u2] + EK, [pk_])
+            no, nk = T.near[:, 8 * u2 + 2 * c:8 * u2 + 2 * c + 2, :], "near%d/%d" % (u2, c)
+            if pr["sv"][s][4 * h + c] == "1":
+                act(T.lv[:, xb, :], ps[:], F.Identity, 512, [pk_], ["lv%d" % xb], bias=CB - C0)
+                ts(no, T.lv[:, xb, :], CB, A.is_equal, None, None, 512, ["lv%d" % xb], [nk], 0.5)
+            else:
+                ts(no, ps[:], CF - C0, A.add, CF, A.is_equal, 512, [pk_], [nk])
+        ps, pn = bank()
+        nt = pr["nt"]
+        for c in range(nt):
+            w_ = 8 // nt
+            mm(ps[:, 16 * w_ * c:16 * w_ * (c + 1)],
+               [(T.Z[:, 15 - a:143 - a], T.near[:, 8 * u2 + w_ * c:8 * u2 + w_ * (c + 1), 16 * a:16 * a + 16]) for a in range(16)], 16 * w_,
+               ["Z"] + ["near%d/%d" % (u2, c_) for c_ in range(4 * c // nt, 4 * (c + 1) // nt)], [pn])
+        scan(T.key[:, u2, :], T.d0T[:], ps[:, 0:128], A.add, A.max, 128, ["d0T", pn], ["key%d" % u2])
+        key, kk = T.key[:, u2, 15:128:16], "key%d" % u2
+        ts(sm(1), key, CF, A.add, CF - 64.0, A.subtract, 8, [kk], [k("q")])
+        if s == 0:
+            ts(sm(2), key, 64.0 * 34816 + 64.0, A.max, None, None, 8, [kk], [k("G")])
+        else:
+            tt(sm(2), key, T.LF[:, li, 8:16], A.max, 8, [kk, k("LL")], [k("G")])
+        tt(sm(3), sm(2), sm(1), A.subtract, 8, [k("G"), k("q")], [k("r")])
+        ts(su(1), sm(3), -48.0, A.min, 64.0, A.add, 8, [k("r")], [k("kl")])
+        vx(lambda: V.tensor_tensor(T.Pm[:, u2, :], T.eye[:, 0:32].indirect(su(1)), T.Pf[:, p3, :], A.mult), 128,
+           ["eye", k("kl"), "Pf%d" % p3], ["Pm%d" % u2], pr["ga"])
+        if pr["mS"]:
+            act(ob(144, 152), sm(3), F.Relu, 8, [k("r")], [k("m")], bias=BIG, scale=BIG / 32)
+        else:
+            ts(ob(144, 152), sm(3), 0.0, A.is_ge, BIG, A.mult, 8, [k("r")], [k("m")])
+        tt(sm(8), dm, ob(144, 152), A.min, 8, ["dum", k("m")], [k("c16")])
+        ps, pn = bank()
+        mm(ps[:, 0:128], [(T.ident[:], T.offd[:]), (T.BOh[:], T.Pm[:, u2, :])], 128, ["BOh", "Pm%d" % u2, "ident", "offd"], [pn])
+        scan(T.nvs[:, u2, :], T.d0N[:, 0:128], ps[:, 0:128], A.add, A.max, 128, ["d0N", pn], ["nvs%d" % u2])
+        ps, pn = bank()
+        mm(ps[:, 0:128], [(T.BOh[:], T.Pm[:, u2, :])], 128, ["BOh", "Pm%d" % u2], [pn])
+        ts(T.nvr[:, y, :], ps[:, 0:128], 2048.0, A.add, None, None, 128, [pn], ["nvr%d" % y])
+        nvd = sm(9)
+        tt(nvd, T.nvs[:, u2, 15:128:16], sm(8), A.max, 8, ["nvs%d" % u2, k("c16")], [k("nv")])
+        cp(su(2), nvd, 8, [k("nv")], [k("nu")])
+        if s < 3:
+            act(ob(0, 128), Xg[:, 0:4352].indirect(su(2)), F.Copy, 128, [xk, xk + "d", k("nu")], [k("nz")], ind=True)
+            act(T.pv[:, y, :], ob(0, 128), F.Relu, 128, [k("nz")], ["pv%d" % y], bias=-37.0)
+        else:
+            act(T.pv[:, y, :], Xg[:, 0:4352].indirect(su(2)), F.Relu, 128, [xk, xk + "d", k("nu")], ["pv%d" % y], bias=-37.0, ind=True)
+        if pr["gS"]:
+            act(sm(4), sm(3), F.Relu, 8, [k("r")], [k("gb")], bias=-16 * BIG, scale=-BIG / 2)
+        else:
+            ts(sm(4), sm(3), 0.0, A.is_lt, BIG, A.mult, 8, [k("r")], [k("gb")])
+        if s == 0:
+            vi_ = 4 * rd + 2 * h
+            tt(T.vri[:, vi_, :], v, T.US[:, rd, 8 * h:8 * h + 8], A.add, 8, [vk, "US%d" % rd], [k("vr0")])
+            ts(T.vri[:, vi_ + 1, :], T.vri[:, vi_, :], 4095, A.bitwise_and, None, None, 8, [k("vr0")], [k("vr")])
+            tt(sm(5), T.vri[:, vi_ + 1, :], sm(4), A.add, 8, [k("vr"), k("gb")], [k("t")])
+        else:
+            tt(sm(5), v, sm(4), A.add, 8, [vk, k("gb")], [k("t")])
+        tt(ob(128, 136), nvd, sm(5), A.min, 8, [k("nv"), k("t")], [k("v")])
+        tt(ob(136, 144), sm(1), ob(144, 152), A.max, 8, [k("q"), k("m")], [k("M")])
+        if s > 0:
+            tt(ob(152, 160), dm, sm(4), A.min, 8, ["dum", k("gb")], [k("fb")])
+            back = (-1, ob(144, 160), T.LB[:, li, :], "b%d" % U, "LB/%d" % (U - 2))
+        if s < 3:
+            lo = 6 * rd + 2 * s + h
+            on = (1, ob(128, 144), T.LF[:, lo, :], "f%d" % U, "LL/%d" % (U + 2))
+            send([on, back] if s > 0 else [on], [k("v"), k("M")] + ([k("m"), k("fb")] if s > 0 else []))
+            send([(1, ob(0, 128), T.LZ[:, lo, :], "t%d" % U, "LF/%d" % (U + 2))], [k("nz")])
+        else:
+            send([(1, ob(128, 144), T.LV[:, 2 * rd + h, :], "f%d" % U, "LV/%d" % (2 * rd + h)), back], [k("v"), k("M"), k("m"), k("fb")])
+        if s == 0:
+            tt(T.zs[:, h, :], z, ob(0, 128), A.add, 128, [zk, k("nz")], ["zs%d" % h])
+            ts(T.zs[:, h, :], T.zs[:, h, :], -0.5, A.add, C2, A.add, 128, ["zs%d" % h], ["zs%d" % h])
+            act(T.zr[:, rd, 128 * h:128 * h + 128], T.zs[:, h, :], F.Identity, 128, ["zs%d" % h], ["zr%d/%d" % (rd, h)], bias=-C2 / 2, scale=0.5)
+        if s < 3:
+            lift[0] = pr["lift"]
+            if pr["wS"]:
+                act(T.wf[:, u2, :], T.i2k[:, 0:2048].indirect(su(0)), F.Copy, 128, ["i2k", k("w")], ["wf%d" % u2], ind=True)
+                cp(T.wr[:, u2, :], T.wf[:, u2, :], 128, ["wf%d" % u2], ["wr%d" % u2])
+            else:
+                vx(lambda: V.tensor_copy(T.wr[:, u2, :], T.i2k[:, 0:2048].indirect(su(0))), 128, ["i2k", k("w")], ["wr%d" % u2], pr["ga"])
+            for b in range(8):
+                ts(T.eqe[:, 8 * y + b, :], T.wr[:, u2, :], T.sm[:, NS * st + 7, 8 * h + b:8 * h + b + 1], A.is_equal, None, None, 128,
+                   ["wr%d" % u2, k("wf")], ["eqe%d/%d" % (y, b)], 0.5)
+            if h == 1:
+                ek = lambda h_: (8 * ((2 * st + h_) % 6), ["eqe%d/%d" % ((2 * st + h_) % 6, b) for b in range(8)])
+                first(st, [0, 1], 0, T.eqe, ek, 7, "wf", 16, "oe")
+            lift[0] = 0.0
+
+    def landed(rd, s, hs, a):
+        li = 6 * rd + 2 * s
+        return T.LB[:, li + hs[0], a:a + 8] if len(hs) == 1 else T.LB[:, li:li + 2, a:a + 8]
+
+    def penalty(rd, s, hs):
+        st = 4 * rd + s
+        ki, kn = 9, "nv"
+        e4 = lambda h: (2 * st + h) % 4
+        if s < 3:
+            tt(sml(st, 16, hs), sml(st, 9, hs), landed(rd, s, hs, 8), A.max, 8, ks("nv", st, hs) + ks("LB", st, hs), ks("pk", st, hs))
+            ki, kn = 16, "pk"
+        for h in hs:
+            y = (2 * st + h) % 6
+            for b in range(8):
+                ts(T.eqp[:, 8 * e4(h) + b, :], T.nvr[:, y, :], T.sm[:, NS * st + ki, 8 * h + b:8 * h + b + 1], A.is_equal, None, None, 128,
+                   ["nvr%d" % y] + ks(kn, st, [h]), ["eqp%d/%d" % (e4(h), b)], 0.5)
+        first(st, hs, 1, T.eqp, lambda h: (8 * e4(h), ["eqp%d/%d" % (e4(h), b) for b in range(8)]), ki, kn, 0, "op")
+        wk = "X%d" % (rd + 1)
+        for h in hs:
+            y = (2 * st + h) % 6
+            vx(lambda h=h, y=y: V.tensor_copy(X[rd + 1][:, 0:4352].indirect(sul(st, 4, [h])), T.pv[:, y, :]), 128,
+               ks("op", st, [h]) + ["pv%d" % y], [wk, wk + "d"], pr["sc"])
+
+    def exonerate(rd, s, hs):
+        st = 4 * rd + s
+        tt(sml(st, 6, hs), sml(st, 3, hs), landed(rd, s, hs, 0), A.add, 8, ks("r", st, hs) + ks("LB", st, hs), ks("kx", st, hs))
+        uk = "US%d" % rd if s == 0 else "LU/%d" % (2 * rd + s - 1)
+        wk, W = "O%d" % (rd + 1), O[rd + 1]
+        for h in hs:
+            y = (2 * st + h) % 6
+            for b in range(8):
+                c = 8 * h + b
+                u = T.US[:, rd, c:c + 1] if s == 0 else T.LU[:, 2 * rd + s - 1, c:c + 1]
+                ts(T.lh[:, c, :], T.iK[:], T.sm[:, NS * st + 6, c:c + 1], A.is_equal, u, A.mult, 128, ["iK", uk] + ks("kx", st, [h]), ["lh%d" % c], 0.5)
+            off, oe = sul(st, 3, [h]), ks("oe", st, [h])
+            act(T.cs[:, h, :], W[:, 0:2304].indirect(off), F.Copy, 128, [wk, wk + "d"] + oe, ["cs%d" % h], ind=True)
+            ps, pn = bank()
+            mm(ps[:, 0:128], [(T.lh[:, 8 * h + b, :], T.eqe[:, 8 * y + b, :]) for b in range(8)], 128,
+               ["lh%d" % (8 * h + b) for b in range(8)] + ["eqe%d/%d" % (y, b) for b in range(8)] + oe, [pn])
+            tt(T.nw[:, 2 * h, :], ps[:, 0:128], T.cs[:, h, :], A.add, 128, [pn, "cs%d" % h], ["nw%d" % h], 1.0)
+            ts(T.nw[:, 2 * h + 1, :], T.nw[:, 2 * h, :], 4095, A.bitwise_and, None, None, 128, ["nw%d" % h], ["nx%d" % h])
+            vx(lambda h=h, off=off: V.tensor_copy(W[:, 0:2304].indirect(off), T.nw[:, 2 * h + 1, :]), 128, oe + ["nx%d" % h], [wk, wk + "d"], pr["sc"])
+
+    def code(rd):
+        zk = ["X0d"] if rd == 0 else ["zr0/0", "zr0/1"]
+        col16 = lambda a: T.X0[:, 4096 + a:4352:16] if rd == 0 else T.zr[:, 0, a:256:16]
+        ps, pn = bank()
+        mm(ps[:, 0:16], [(T.Zu[:, 15 - a:143 - a], col16(a)) for a in range(16)], 16, ["Zu"] + zk, [pn])
+        ts(T.ui[:, 2 * rd, :], ps[:, 0:16], 2048.0, A.add, None, None, 16, [pn], ["ui%d" % rd])
+        ts(T.ui[:, 2 * rd + 1, :], T.ui[:, 2 * rd, :], 4095, A.bitwise_and, None, None, 16, ["ui%d" % rd], ["uj%d" % rd])
+        ts(T.US[:, rd, :], T.ui[:, 2 * rd + 1, :], -2048.0, A.add, None, None, 16, ["uj%d" % rd], ["US%d" % rd])
+        send([(i + 1, T.US[:, rd, :], T.LU[:, 2 * rd + i, :], "u%d" % (2 * rd + i), "LU/%d" % (2 * rd + i)) for i in range(2)], ["US%d" % rd])
+
+    def nearness():
+        ts(T.cnt[:, 0:48], T.LF[:, 0:6, 8:16], BIG, A.is_lt, None, None, 48, ["LL/%d" % U for U in range(2, 8)], ["cnt0"])
+        ts(T.cnt[:, 48:96], T.OB[:, 0:6, 16:24], 1.0, A.is_lt, -1.0, A.mult, 48, ["m/%d" % U for U in range(6)], ["cnt1"])
+        ms(T.ta[:, 9, 0:96], -1e6, 96, ["ta9"])
+        scan(T.ta[:, 0, 0:96], T.cnt[:], T.ta[:, 9, 0:96], A.add, A.max, 96, ["cnt0", "cnt1", "ta9"], ["ta0"])
+        ps, pn = bank()
+        mm(ps[:, 0:2], [(T.BO[:], T.ta[:, 0, 94:96])], 2, ["BO", "ta0"], [pn], 4)
+        cp(T.coli[:, 8:9], ps[:, 1:2], 1, [pn], ["A0"])
+        ts(T.coli[:, 12:13], T.coli[:, 8:9], 3, A.bitwise_and, None, None, 1, ["A0"], ["A1"])
+        ts(col(12), T.coli[:, 12:13], 2.0 / 64, A.mult, 49.0 / 64, A.add, 1, ["A1"], ["A2"])
+        op("V", lambda: [V.reciprocal(col(16), col(12))], 250.0, ["A2"], ["A3"])
+        cp(T.colb[:, 0:1], col(16), 1, ["A3"], ["A4"])
+        cp(col(20), T.colb[:, 0:1], 1, ["A4"], ["A5"])
+        act(T.dgb[:, 1, :], T.ident[:], F.Copy, 128, ["ident", "A5"], ["dgb1"], scale=col(20))
+
+    code(0)
+    for rd in range(2):
+        for s in range(4):
+            for h in range(2):
+                ahead[0] = pr["ahead"] * (1 - h)
+                station(rd, s, h)
+                ahead[0] = 0.0
+                lift[0] = pr["lift"]
+                if s == 3:
+                    penalty(rd, 3, [h])
+                if s > 0 and (s > pr["both"] or h == 1):
+                    hs = [h] if s > pr["both"] else [0, 1]
+                    penalty(rd, s - 1, hs)
+                    exonerate(rd, s - 1, hs)
+                lift[0] = 0.0
+            if rd == 0 and s == 0:
+                code(1)
+        if rd == 0:
+            nearness()
+            act(T.X1[:, 4096:4352], T.zr[:, 0, :], F.Copy, 256, ["zr0/0", "zr0/1"], ["X1d"])
+            dma(T.X2[:, 0:4096], T.X1[:, 0:4096], 1048576, ["X1"], ["X2"])
+            dma(T.O2[:, 0:2048], T.O1[:, 0:2048], 1048576, ["O1"], ["O2"])
+    dma(T.yz[:], T.zr[:, 1, :], 65536, ["zr1/0", "zr1/1"], ["yz"])
+    for h in range(2):
+        dma(T.yv[:, 8 * h:8 * h + 8], T.LV[:, 2 + h, 0:8], 30000, ["LV/%d" % (2 + h)], ["yv%d" % h])
+    dma(T.yx[:], T.X2[:, 0:4096], 1048576, ["X2"], ["yx"])
+    for c in range(2):
+        ps, pk_ = bank()
+        act(ps[:], T.O2[:, 1024 + 512 * c:1536 + 512 * c], F.Copy, 512, ["O2"], [pk_], scale=4096.0)
+        tt(T.pk[:, 512 * c:512 * c + 512], ps[:], T.O2[:, 512 * c:512 * c + 512], A.add, 512, [pk_, "O2"], ["pk%d" % c], 1.0)
+        dma(T.yn[:, 512 * c:512 * c + 512], T.pk[:, 512 * c:512 * c + 512], 262144, ["pk%d" % c], ["yn%d" % c])
+    return ops
+
+
+def depend(ops, order, banks):
+    last, readers, deps = {}, {}, {}
+    for i in order:
+        o = ops[i]
+        d = {}
+        rs = [banks.get(x, x) for x in o["r"]]
+        ws = [banks.get(x, x) for x in o["w"]]
+        for x in rs:
+            if x in last:
+                d[(last[x], x)] = 1
+        for x in ws:
+            if x in last:
+                d[(last[x], x)] = 1
+            for j in readers.get(x, []):
+                d[(j, x)] = 1
+        for x in rs:
+            readers.setdefault(x, []).append(i)
+        for x in ws:
+            last[x] = i
+            readers[x] = []
+        deps[i] = [e for e in d if e[0] != i]
+    return deps
+
+
+def queue(o):
+    return "G" if o["e"] == "R" else o["e"]
+
+
+def after(o):
+    return PARAM["rem"] if o["e"] == "R" else (2000.0 if o["e"] == "Y" else PARAM["lat"])
+
+
+def arrange(ops, deps):
+    n = len(ops)
+    way = [0.0] * n
+    succ = [set() for _ in range(n)]
+    for i in range(n):
+        for j, _x in deps[i]:
+            succ[j].add(i)
+    for i in range(n - 1, -1, -1):
+        way[i] = ops[i]["c"] + after(ops[i]) + max([way[j] for j in succ[i]] + [0.0])
+    rank_ = [way[i] + (ops[i]["lift"] or ops[i]["first"]) for i in range(n)]
+    left = [len(set(j for j, _x in deps[i])) for i in range(n)]
+    ready = [0.0] * n
+    free = {q: 0.0 for q in "VSPGY"}
+    pool = [i for i in range(n) if left[i] == 0]
+    order, end = [], 0.0
+    use = [([x for x in o["r"] + o["w"] if x[0] == "#"] + [None])[0] for o in ops]
+    open_ = {}
+    for x in use:
+        open_[x] = open_.get(x, 0) + 1
+    banks, idle = {}, {b: 0.0 for b in PSUM}
+
+    def start(i):
+        t = max(ready[i], free[queue(ops[i])])
+        if use[i] is not None and use[i] not in banks:
+            if len(idle) <= (PARAM["spare"] if ops[i]["lift"] else 0):
+                return 1e18
+            t = max(t, min(idle.values()))
+        return t
+    while pool:
+        best = min(pool, key=lambda i: (start(i), -rank_[i]))
+        q = queue(ops[best])
+        soon = start(best) + PARAM["hold"] * ops[best]["c"]
+        assert soon < 1e17
+        for i in pool:
+            if queue(ops[i]) == q and rank_[i] > rank_[best] and start(i) < soon:
+                best = i
+        t0 = start(best)
+        pool.remove(best)
+        order.append(best)
+        free[q] = t0 + ops[best]["c"]
+        done = free[q] + after(ops[best])
+        ops[best]["t"] = t0
+        x = use[best]
+        if x is not None:
+            if x not in banks:
+                banks[x] = min(idle, key=lambda b: idle[b])
+                idle.pop(banks[x])
+            open_[x] -= 1
+            if open_[x] == 0:
+                idle[banks[x]] = done
+        end = max(end, done)
+        for j in succ[best]:
+            ready[j] = max(ready[j], done)
+            left[j] -= 1
+            if left[j] == 0:
+                pool.append(j)
+    return order, banks, end
+
+
+def rank_program(g, core, T, topo):
+    rank = T.rank_of(core)
+    if rank is None:
+        return
+    if "o" not in ORDER:
+        ops = make_ops(g, core, T, topo, rank, {})
+        ORDER["o"], ORDER["banks"], ORDER["end"] = arrange(ops, depend(ops, range(len(ops)), {}))
+    ops = make_ops(g, core, T, topo, rank, ORDER["banks"])
+    deps = depend(ops, ORDER["o"], ORDER["banks"])
+    Q = {"V": g.vector, "S": g.scalar, "P": g.tensor, "G": g, "Y": g.sync}
+    known = {q: {} for q in Q}
+    count = {}
+    mark = {}
+    for i in ORDER["o"]:
+        o = ops[i]
+        q = queue(o)
+        need = {}
+        for j, x in deps[i]:
+            if ops[j]["e"] == "R":
+                sem, val = ops[j]["sems"][x]
+                seen = {}
+            else:
+                sem, val, seen = mark[j]
+            if val > need.get(sem, (0, None))[0]:
+                need[sem] = (val, seen)
+        for sem in sorted(need, key=lambda s_: -sum(need[s_][1].values())):
+            val, seen = need[sem]
+            if known[q].get(sem, 0) < val:
+                Q[q].wait_ge(T.sem[sem], val)
+                known[q][sem] = val
+                for s_, v_ in seen.items():
+                    if known[q].get(s_, 0) < v_:
+                        known[q][s_] = v_
+        made = o["fn"]()
+        if o["e"] == "R":
+            for sem, val in o["sems"].values():
+                count[sem] = val
+                count["sent"] = count.get("sent", 0) + val
+        elif o["e"] == "Y":
+            made[0].then_inc(T.sem[o["sems"][""]], 16)
+            count[o["sems"][""]] = 16
+            mark[i] = (o["sems"][""], 16, dict(known[q]))
+        else:
+            sem = "c" + q
+            for m in made:
+                m.then_inc(T.sem[sem], 1)
+            count[sem] = count.get(sem, 0) + len(made)
+            mark[i] = (sem, count[sem], dict(known[q]))
+    for sem, val in count.items():
+        if max(known[q].get(sem, 0) for q in known) < val:
+            g.sync.wait_ge(T.sem[sem], val)

@@ -8,13 +8,17 @@ C2 = float(3 * 2 ** 23)
 C0 = 192.0
 S0 = 1.3046875
 PARAM = {"sv": ("00100001", "10101000", "11111100", "11101110"), "vg": ("01000100", "00011010", "00000000", "00000000"),
-         "pS": 1, "mS": 1, "gS": 1, "dS": 2, "wS": 0, "both": 0, "hold": 0.2, "lift": 1.0, "spare": 2, "nt": 2, "ahead": 3000.0,
-         "cyc": 1.04, "pe": 0.52, "ga": 1.56, "sc": 3.8, "lat": 70.0, "rem": 2500.0, "bw": 250.0}
+         "pS": 1, "mS": 1, "gS": 1, "dS": 2, "wS": 0, "both": 0, "hold": 0.2, "lift": 1.0, "spare": 2, "nt": 2,
+         "ahead": (3000.0, 3000.0, 3000.0, 3000.0), "eS": (0, 0, 0, 0, 4, 0, 0, 8),
+         "cyc": 1.04, "pe": 0.52, "ga": 1.56, "sc": 3.8, "lat": 170.0, "rem": 2500.0, "fix": 0.0, "bw": 250.0}
+PARAM.update({'lat': 230.0, 'cyc': 0.9, 'pe': 0.45, 'rem': 2300.0, 'pS': 0, 'mS': 0, 'gS': 1, 'dS': 2, 'lift': 2000.0, 'fix': 10.0,
+              'sv': ('00100001', '11001111', '00000000', '11100001'), 'eS': (0, 0, 0, 0, 4, 0, 0, 4),
+              'ahead': (1000.0, 1000.0, 3000.0, 1000.0), 'vg': ('00100100', '00011010', '00000000', '10001000')})
 NS = 20
 
 SCRATCH = {
     "X0": ("sbuf", [128, 4352], "bfloat16"), "X1": ("sbuf", [128, 4352], "bfloat16"), "X2": ("sbuf", [128, 4352], "bfloat16"),
-    "O0": ("sbuf", [128, 2048], "float32"), "O1": ("sbuf", [128, 2304], "float32"), "O2": ("sbuf", [128, 2304], "float32"),
+    "O0": ("sbuf", [128, 4096], "float32"), "O1": ("sbuf", [128, 4352], "float32"), "O2": ("sbuf", [128, 4352], "float32"),
     "nbi": ("sbuf", [128, 1024], "int32"), "nbt": ("sbuf", [128, 2048], "int32"), "pk": ("sbuf", [128, 1024], "float32"),
     "vi": ("sbuf", [128, 16], "int32"), "v0": ("sbuf", [128, 16], "float32"),
     "zr": ("sbuf", [128, 2, 256], "bfloat16"), "zs": ("sbuf", [128, 2, 128], "float32"),
@@ -27,13 +31,14 @@ SCRATCH = {
     "zT": ("sbuf", [128, 2, 128], "bfloat16"), "xg": ("sbuf", [128, 8, 512], "bfloat16"), "lv": ("sbuf", [128, 8, 512], "bfloat16"),
     "near": ("sbuf", [128, 16, 256], "bfloat16"), "key": ("sbuf", [128, 2, 128], "float32"),
     "nvs": ("sbuf", [128, 2, 128], "float32"), "nvr": ("sbuf", [128, 6, 128], "uint16"), "wr": ("sbuf", [128, 2, 128], "uint16"),
+    "nvf": ("sbuf", [128, 4, 128], "float32"), "ab": ("sbuf", [128, 4, 128], "float32"),
     "wf": ("sbuf", [128, 2, 128], "float32"), "yo": ("sbuf", [128, 4, 256], "float32"),
     "eqp": ("sbuf", [128, 32, 128], "bfloat16"), "eqe": ("sbuf", [128, 48, 128], "float16"), "lh": ("sbuf", [128, 16, 128], "float16"),
     "pv": ("sbuf", [128, 6, 128], "bfloat16"), "cs": ("sbuf", [128, 2, 128], "float32"), "nw": ("sbuf", [128, 4, 128], "int32"),
     "cnt": ("sbuf", [128, 96], "float32"), "col": ("sbuf", [128, 64], "float32"), "coli": ("sbuf", [128, 16], "int32"),
     "colb": ("sbuf", [128, 8], "bfloat16"),
     "iof": ("sbuf", [128, 144], "float32"), "cm": ("sbuf", [128, 256], "float32"), "jg": ("sbuf", [128, 128], "float32"),
-    "i2k": ("sbuf", [128, 2048], "float32"),
+    "i2k": ("sbuf", [128, 4096], "float32"),
     "ident": ("sbuf", [128, 128], "bfloat16"), "E": ("sbuf", [128, 2048], "bfloat16"),
     "Z": ("sbuf", [128, 144], "bfloat16"), "Zu": ("sbuf", [128, 144], "bfloat16"), "BO": ("sbuf", [128, 128], "float32"),
     "Wl": ("sbuf", [128, 8, 128], "bfloat16"), "pw": ("sbuf", [128, 128], "float32"),
@@ -71,7 +76,7 @@ def make_ops(g, core, T, topo, rank, banks):
         ops.append({"e": eng, "fn": fn, "c": cost, "r": list(r), "w": list(w), "sems": sems, "lift": lift[0], "first": ahead[0]})
 
     def vc(n, c=1.0):
-        return max(64.0, n * c) * cyc
+        return max(64.0, pr["fix"] + n * c) * cyc
 
     def ts(out, in0, s1, o0, s2, o1, n, r, w, c=1.0):
         if o1 is None:
@@ -152,7 +157,7 @@ def make_ops(g, core, T, topo, rank, banks):
     dma(T.X0[:, 4096:4352], T.z[:], 65536, [], ["X0d"])
     ahead[0] = 0.0
     dma(T.X0[:, 0:4096], T.tracks[:], 1048576, [], ["X0"])
-    dma(T.X1[:, 0:4096], T.tracks[:], 1048576, [], ["X1"])
+    dma(T.X1[:, 0:4096], T.tracks[:], 1048576, ["X0"], ["X1"])
 
     iota(T.coli[:, 0:1], [[0, 1]], 0, 1, 1, ["pi"], False)
     iota(T.iof[:], [[1, 144]], 0, 0, 144, ["iof"])
@@ -160,7 +165,8 @@ def make_ops(g, core, T, topo, rank, banks):
     iota(T.jg[:], [[16, 8], [0, 16]], 0, 0, 128, ["jg"])
     iota(T.dum[:, 0:16], [[16, 16]], 4096, 0, 16, ["dumA"])
     iota(T.dum[:, 16:32], [[16, 16]], 2048, 0, 16, ["dumB"])
-    iota(T.i2k[:], [[1, 2048]], 0, 0, 2048, ["i2k"])
+    iota(T.i2k[:, 0:2048], [[1, 2048]], 0, 0, 2048, ["i2a"])
+    dma(T.i2k[:, 2048:4096], T.i2k[:, 0:2048], 1048576, ["i2a"], ["i2k"])
     cm = T.cm[:, 0:128]
     cp(col(0), T.coli[:, 0:1], 1, ["pi"], ["c0"])
     ts(T.coli[:, 4:5], T.coli[:, 0:1], 15, A.bitwise_and, None, None, 1, ["pi"], ["ai"])
@@ -201,7 +207,7 @@ def make_ops(g, core, T, topo, rank, banks):
     act(T.d0T[:], ta(8), F.Identity, 128, ["ta8"], ["d0T"], bias=1.0)
     ts(T.d0N[:], T.cm[:], 0.0, A.is_equal, -9e29, A.mult, 256, ["cm"], ["d0N"])
     ts(T.dum[:], T.dum[:], col(1), A.add, None, None, 32, ["dumA", "dumB", "c1"], ["dumA", "dumB", "dum"])
-    for W, wk, c in ((T.X1, "X1d", 4096), (T.X2, "X2d", 4096), (T.O1, "O1d", 2048), (T.O2, "O2d", 2048)):
+    for W, wk, c in ((T.X1, "X1d", 4096), (T.X2, "X2d", 4096), (T.O1, "O1d", 4096), (T.O2, "O2d", 4096)):
         act(W[:, c:c + 256], T.cm[:], F.Copy, 256, ["cm"], [wk])
 
     for c in range(2):
@@ -209,9 +215,10 @@ def make_ops(g, core, T, topo, rank, banks):
             a = 1024 * hi + 512 * c
             ts(T.nbt[:, a:a + 512], T.nbi[:, 512 * c:512 * c + 512], 12 if hi else 4095, A.logical_shift_right if hi else A.bitwise_and,
                None, None, 512, ["nbi%d" % c], ["nbt%d" % a])
-            cp(T.O0[:, a:a + 512], T.nbt[:, a:a + 512], 512, ["nbt%d" % a], ["O0/%d" % a])
+            cp(T.O0[:, 2048 + a:2560 + a], T.nbt[:, a:a + 512], 512, ["nbt%d" % a], ["O0/%d" % a])
     OK = [["O0/%d" % a for a in range(0, 2048, 512)], ["O1"]]
-    dma(T.O1[:, 0:2048], T.O0[:, 0:2048], 1048576, OK[0], ["O1"])
+    dma(T.O0[:, 0:2048], T.O0[:, 2048:4096], 1048576, OK[0], ["O0t"])
+    dma(T.O1[:, 2048:4096], T.O0[:, 2048:4096], 1048576, OK[0], ["O1"])
     cp(T.v0[:], T.vi[:], 16, ["vi"], ["v0"])
 
     chunk = [0]
@@ -257,15 +264,21 @@ def make_ops(g, core, T, topo, rank, banks):
         else:
             li = 6 * rd + 2 * (s - 1) + h
             v, vk, z, zk = T.LF[:, li, 0:8], k("LL"), T.LZ[:, li, :], k("LF")
-        ts(sm(0), v, 2048.0, A.is_ge, -2048.0, A.mult, 8, [vk], [k("s0")])
-        tt(sm(7), v, sm(0), A.add, 8, [vk, k("s0")], [k("wf")])
-        cp(su(0), sm(7), 8, [k("wf")], [k("w")])
+        if s < 3:
+            ts(sm(0), v, 2048.0, A.is_ge, -2048.0, A.mult, 8, [vk], [k("s0")])
+            tt(sm(7), v, sm(0), A.add, 8, [vk, k("s0")], [k("wf")])
+        if s == 0:
+            cp(su(0), sm(7), 8, [k("wf")], [k("w")])
+            ow, iw, ik = Og[:, 2048:4096], T.i2k[:, 0:2048], ["i2a"]
+        else:
+            cp(su(0), v, 8, [vk], [k("w")])
+            ow, iw, ik, ok = Og[:, 0:4096], T.i2k[:, 0:4096], ["i2a", "i2k"], ok + ["O%dt" % rd]
         p3, u2 = U % 3, U % 2
-        act(T.Pf[:, p3, :], Og[:, 0:2048].indirect(su(0)), F.Identity, 128, ok + [k("w")], ["Pf%d" % p3], ind=True, bias=-2048.0)
+        act(T.Pf[:, p3, :], ow.indirect(su(0)), F.Identity, 128, ok + [k("w")], ["Pf%d" % p3], ind=True, bias=-2048.0)
         if pr["pS"]:
             ts(T.P16[:, p3, :], T.Pf[:, p3, :], 2048.0, A.add, None, None, 128, ["Pf%d" % p3], ["P16%d" % p3])
         else:
-            vx(lambda: V.tensor_copy(T.P16[:, p3, :], Og[:, 0:2048].indirect(su(0))), 128, ok + [k("w")], ["P16%d" % p3], pr["ga"])
+            vx(lambda: V.tensor_copy(T.P16[:, p3, :], ow.indirect(su(0))), 128, ok + [k("w")], ["P16%d" % p3], pr["ga"])
         ps, pn = bank()
         mm(ps[:, 0:128], [(z, T.dgb[:, rd, :])], 128, [zk, "dgb%d" % rd], [pn])
         act(T.zT[:, u2, :], ps[:, 0:128], F.Identity, 128, [pn], ["zT%d" % u2], bias=-C0)
@@ -316,7 +329,13 @@ def make_ops(g, core, T, topo, rank, banks):
         scan(T.nvs[:, u2, :], T.d0N[:, 0:128], ps[:, 0:128], A.add, A.max, 128, ["d0N", pn], ["nvs%d" % u2])
         ps, pn = bank()
         mm(ps[:, 0:128], [(T.BOh[:], T.Pm[:, u2, :])], 128, ["BOh", "Pm%d" % u2], [pn])
-        ts(T.nvr[:, y, :], ps[:, 0:128], 2048.0, A.add, None, None, 128, [pn], ["nvr%d" % y])
+        if pr["eS"][2 * s + h] < 8:
+            ts(T.nvr[:, y, :], ps[:, 0:128], 2048.0, A.add, None, None, 128, [pn], ["nvr%d" % y])
+        if pr["eS"][2 * s + h] > 0:
+            if pr["eS"][2 * s + h] < 8:
+                ps, pn = bank()
+                mm(ps[:, 0:128], [(T.BOh[:], T.Pm[:, u2, :])], 128, ["BOh", "Pm%d" % u2], [pn])
+            act(T.nvf[:, y % 4, :], ps[:, 0:128], F.Identity, 128, [pn], ["nvf%d" % (y % 4)], bias=2048.0)
         nvd = sm(9)
         tt(nvd, T.nvs[:, u2, 15:128:16], sm(8), A.max, 8, ["nvs%d" % u2, k("c16")], [k("nv")])
         cp(su(2), nvd, 8, [k("nv")], [k("nu")])
@@ -355,10 +374,10 @@ def make_ops(g, core, T, topo, rank, banks):
         if s < 3:
             lift[0] = pr["lift"]
             if pr["wS"]:
-                act(T.wf[:, u2, :], T.i2k[:, 0:2048].indirect(su(0)), F.Copy, 128, ["i2k", k("w")], ["wf%d" % u2], ind=True)
+                act(T.wf[:, u2, :], iw.indirect(su(0)), F.Copy, 128, ik + [k("w")], ["wf%d" % u2], ind=True)
                 cp(T.wr[:, u2, :], T.wf[:, u2, :], 128, ["wf%d" % u2], ["wr%d" % u2])
             else:
-                vx(lambda: V.tensor_copy(T.wr[:, u2, :], T.i2k[:, 0:2048].indirect(su(0))), 128, ["i2k", k("w")], ["wr%d" % u2], pr["ga"])
+                vx(lambda: V.tensor_copy(T.wr[:, u2, :], iw.indirect(su(0))), 128, ik + [k("w")], ["wr%d" % u2], pr["ga"])
             for b in range(8):
                 ts(T.eqe[:, 8 * y + b, :], T.wr[:, u2, :], T.sm[:, NS * st + 7, 8 * h + b:8 * h + b + 1], A.is_equal, None, None, 128,
                    ["wr%d" % u2, k("wf")], ["eqe%d/%d" % (y, b)], 0.5)
@@ -380,7 +399,11 @@ def make_ops(g, core, T, topo, rank, banks):
             ki, kn = 16, "pk"
         for h in hs:
             y = (2 * st + h) % 6
-            for b in range(8):
+            for b in range(pr["eS"][2 * s + h]):
+                kc, ab = T.sm[:, NS * st + ki, 8 * h + b:8 * h + b + 1], T.ab[:, b % 4, :]
+                act(ab, T.nvf[:, y % 4, :], F.Abs, 128, ["nvf%d" % (y % 4)] + ks(kn, st, [h]), ["ab%d" % (b % 4)], bias=kc, scale=-1.0)
+                act(T.eqp[:, 8 * e4(h) + b, :], ab, F.Relu, 128, ["ab%d" % (b % 4)], ["eqp%d/%d" % (e4(h), b)], bias=1.0, scale=-1.0)
+            for b in range(pr["eS"][2 * s + h], 8):
                 ts(T.eqp[:, 8 * e4(h) + b, :], T.nvr[:, y, :], T.sm[:, NS * st + ki, 8 * h + b:8 * h + b + 1], A.is_equal, None, None, 128,
                    ["nvr%d" % y] + ks(kn, st, [h]), ["eqp%d/%d" % (e4(h), b)], 0.5)
         first(st, hs, 1, T.eqp, lambda h: (8 * e4(h), ["eqp%d/%d" % (e4(h), b) for b in range(8)]), ki, kn, 0, "op")
@@ -402,13 +425,13 @@ def make_ops(g, core, T, topo, rank, banks):
                 u = T.US[:, rd, c:c + 1] if s == 0 else T.LU[:, 2 * rd + s - 1, c:c + 1]
                 ts(T.lh[:, c, :], T.iK[:], T.sm[:, NS * st + 6, c:c + 1], A.is_equal, u, A.mult, 128, ["iK", uk] + ks("kx", st, [h]), ["lh%d" % c], 0.5)
             off, oe = sul(st, 3, [h]), ks("oe", st, [h])
-            act(T.cs[:, h, :], W[:, 0:2304].indirect(off), F.Copy, 128, [wk, wk + "d"] + oe, ["cs%d" % h], ind=True)
+            act(T.cs[:, h, :], W[:, 2048:4352].indirect(off), F.Copy, 128, [wk, wk + "d"] + oe, ["cs%d" % h], ind=True)
             ps, pn = bank()
             mm(ps[:, 0:128], [(T.lh[:, 8 * h + b, :], T.eqe[:, 8 * y + b, :]) for b in range(8)], 128,
                ["lh%d" % (8 * h + b) for b in range(8)] + ["eqe%d/%d" % (y, b) for b in range(8)] + oe, [pn])
             tt(T.nw[:, 2 * h, :], ps[:, 0:128], T.cs[:, h, :], A.add, 128, [pn, "cs%d" % h], ["nw%d" % h], 1.0)
             ts(T.nw[:, 2 * h + 1, :], T.nw[:, 2 * h, :], 4095, A.bitwise_and, None, None, 128, ["nw%d" % h], ["nx%d" % h])
-            vx(lambda h=h, off=off: V.tensor_copy(W[:, 0:2304].indirect(off), T.nw[:, 2 * h + 1, :]), 128, oe + ["nx%d" % h], [wk, wk + "d"], pr["sc"])
+            vx(lambda h=h, off=off: V.tensor_copy(W[:, 2048:4352].indirect(off), T.nw[:, 2 * h + 1, :]), 128, oe + ["nx%d" % h], [wk, wk + "d"], pr["sc"])
 
     def code(rd):
         zk = ["X0d"] if rd == 0 else ["zr0/0", "zr0/1"]
@@ -439,7 +462,7 @@ def make_ops(g, core, T, topo, rank, banks):
     for rd in range(2):
         for s in range(4):
             for h in range(2):
-                ahead[0] = pr["ahead"] * (1 - h)
+                ahead[0] = pr["ahead"][s] * (1 - h)
                 station(rd, s, h)
                 ahead[0] = 0.0
                 lift[0] = pr["lift"]
@@ -456,15 +479,16 @@ def make_ops(g, core, T, topo, rank, banks):
             nearness()
             act(T.X1[:, 4096:4352], T.zr[:, 0, :], F.Copy, 256, ["zr0/0", "zr0/1"], ["X1d"])
             dma(T.X2[:, 0:4096], T.X1[:, 0:4096], 1048576, ["X1"], ["X2"])
-            dma(T.O2[:, 0:2048], T.O1[:, 0:2048], 1048576, ["O1"], ["O2"])
+            dma(T.O1[:, 0:2048], T.O1[:, 2048:4096], 1048576, ["O1"], ["O1t"])
+            dma(T.O2[:, 2048:4096], T.O1[:, 2048:4096], 1048576, ["O1"], ["O2"])
     dma(T.yz[:], T.zr[:, 1, :], 65536, ["zr1/0", "zr1/1"], ["yz"])
     for h in range(2):
         dma(T.yv[:, 8 * h:8 * h + 8], T.LV[:, 2 + h, 0:8], 30000, ["LV/%d" % (2 + h)], ["yv%d" % h])
     dma(T.yx[:], T.X2[:, 0:4096], 1048576, ["X2"], ["yx"])
     for c in range(2):
         ps, pk_ = bank()
-        act(ps[:], T.O2[:, 1024 + 512 * c:1536 + 512 * c], F.Copy, 512, ["O2"], [pk_], scale=4096.0)
-        tt(T.pk[:, 512 * c:512 * c + 512], ps[:], T.O2[:, 512 * c:512 * c + 512], A.add, 512, [pk_, "O2"], ["pk%d" % c], 1.0)
+        act(ps[:], T.O2[:, 3072 + 512 * c:3584 + 512 * c], F.Copy, 512, ["O2"], [pk_], scale=4096.0)
+        tt(T.pk[:, 512 * c:512 * c + 512], ps[:], T.O2[:, 2048 + 512 * c:2560 + 512 * c], A.add, 512, [pk_, "O2"], ["pk%d" % c], 1.0)
         dma(T.yn[:, 512 * c:512 * c + 512], T.pk[:, 512 * c:512 * c + 512], 262144, ["pk%d" % c], ["yn%d" % c])
     return ops
 

@@ -8,12 +8,19 @@ C2 = float(3 * 2 ** 23)
 C0 = 192.0
 S0 = 1.3046875
 PARAM = {"sv": ("00100001", "10101000", "11111100", "11101110"), "vg": ("01000100", "00011010", "00000000", "00000000"),
-         "pS": 1, "mS": 1, "gS": 1, "dS": 2, "wS": 0, "both": 0, "hold": 0.2, "lift": 1.0, "spare": 2, "nt": 2,
+         "pS": 1, "mS": 1, "gS": 1, "dS": 2, "wS": 0, "both": 0, "hold": 0.2, "holdP": 0.5, "holdS": 0.2, "last": 1.0, "lift": 1.0, "spare": 2, "nt": 2,
          "ahead": (3000.0, 3000.0, 3000.0, 3000.0), "eS": (0, 0, 0, 0, 4, 0, 0, 8),
          "cyc": 1.04, "pe": 0.52, "ga": 1.56, "sc": 3.8, "lat": 170.0, "rem": 2500.0, "fix": 0.0, "bw": 250.0}
 PARAM.update({'lat': 230.0, 'cyc': 0.9, 'pe': 0.45, 'rem': 2300.0, 'pS': 0, 'mS': 0, 'gS': 1, 'dS': 2, 'lift': 2000.0, 'fix': 10.0,
               'sv': ('00100001', '11001111', '00000000', '11100001'), 'eS': (0, 0, 0, 0, 4, 0, 0, 4),
               'ahead': (1000.0, 1000.0, 3000.0, 1000.0), 'vg': ('00100100', '00011010', '00000000', '10001000')})
+PARAM.update({'lat': 250.0, 'eS': (0, 0, 0, 8, 2, 0, 8, 4), 'lift': 1000.0, 'ahead': (2000.0, 1000.0, 6000.0, 1000.0),
+              'sv': ('10101010', '01001111', '00000000', '00010001'), 'fix': 0.0, 'holdS': 0.8, 'tie': 0.0, 'mix': 0})
+PARAM.update({'vg': ('01100110', '10000100', '01000100', '00000000'), 'sv': ('00000100', '10000001', '10101110', '01100110'),
+              'ahead': (2000.0, 3000.0, 2000.0, 1000.0), 'rem': 2000.0, 'holdS': 0.3, 'eS': (0, 0, 0, 4, 4, 0, 0, 4),
+              'lift': -1500.0, 'mS': 1, 'lat': 230.0})
+PARAM.update({'sv': ('00100100', '00000001', '10101110', '01100110'), 'vg': ('00010110', '10000100', '01000100', '00000000'),
+              'ahead': (4000.0, 3000.0, 2000.0, 1000.0), 'lift': 1.0, 'eS': (0, 0, 0, 2, 4, 0, 0, 4)})
 NS = 20
 
 SCRATCH = {
@@ -26,12 +33,13 @@ SCRATCH = {
     "LU": ("sbuf", [128, 4, 16], "float32"), "US": ("sbuf", [128, 2, 16], "float32"), "OB": ("sbuf", [128, 16, 32], "float32"),
     "ui": ("sbuf", [128, 4, 16], "int32"), "vri": ("sbuf", [128, 8, 8], "int32"),
     "sm": ("sbuf", [128, 8 * NS, 16], "float32"), "su": ("sbuf", [128, 8 * 5, 16], "uint16"),
-    "P16": ("sbuf", [128, 3, 128], "uint16"), "Pf": ("sbuf", [128, 3, 128], "float32"), "Pm": ("sbuf", [128, 2, 128], "float16"),
+    "P16": ("sbuf", [128, 3, 128], "uint16"), "Pf": ("sbuf", [128, 3, 128], "float32"), "Pm": ("sbuf", [128, 2, 128], "float32"),
     "OZ": ("sbuf", [128, 16, 128], "bfloat16"), "LZ": ("sbuf", [128, 12, 128], "bfloat16"),
-    "zT": ("sbuf", [128, 2, 128], "bfloat16"), "xg": ("sbuf", [128, 8, 512], "bfloat16"), "lv": ("sbuf", [128, 8, 512], "bfloat16"),
+    "zT": ("sbuf", [128, 2, 128], "bfloat16"), "xg": ("sbuf", [128, 4096], "bfloat16"), "cx": ("sbuf", [128, 8], "float32"),
+    "sq": ("sbuf", [128, 4, 8], "uint16"), "zq": ("sbuf", [128, 2, 128], "bfloat16"), "lv": ("sbuf", [128, 8, 512], "bfloat16"),
     "near": ("sbuf", [128, 16, 256], "bfloat16"), "key": ("sbuf", [128, 2, 128], "float32"),
     "nvs": ("sbuf", [128, 2, 128], "float32"), "nvr": ("sbuf", [128, 6, 128], "uint16"), "wr": ("sbuf", [128, 2, 128], "uint16"),
-    "nvf": ("sbuf", [128, 4, 128], "float32"), "ab": ("sbuf", [128, 4, 128], "float32"),
+    "nvf": ("sbuf", [128, 6, 128], "float32"), "ab": ("sbuf", [128, 4, 128], "float32"),
     "wf": ("sbuf", [128, 2, 128], "float32"), "yo": ("sbuf", [128, 4, 256], "float32"),
     "eqp": ("sbuf", [128, 32, 128], "bfloat16"), "eqe": ("sbuf", [128, 48, 128], "float16"), "lh": ("sbuf", [128, 16, 128], "float16"),
     "pv": ("sbuf", [128, 6, 128], "bfloat16"), "cs": ("sbuf", [128, 2, 128], "float32"), "nw": ("sbuf", [128, 4, 128], "int32"),
@@ -45,7 +53,7 @@ SCRATCH = {
     "thr": ("sbuf", [128, 128], "bfloat16"), "offd": ("sbuf", [128, 128], "bfloat16"),
     "ta": ("sbuf", [128, 10, 128], "float32"), "eye": ("sbuf", [128, 32], "bfloat16"), "iK": ("sbuf", [128, 128], "bfloat16"),
     "d0T": ("sbuf", [128, 128], "float32"), "d0N": ("sbuf", [128, 256], "float32"), "dum": ("sbuf", [128, 32], "float32"),
-    "dgb": ("sbuf", [128, 2, 128], "bfloat16"), "BOh": ("sbuf", [128, 128], "bfloat16"),
+    "dgb": ("sbuf", [128, 2, 128], "bfloat16"), "tw": ("sbuf", [128, 4, 128], "float32"),
     "pd0": ("psum", [128, 512], "float32"), "pd1": ("psum", [128, 512], "float32"), "pd2": ("psum", [128, 512], "float32"),
     "pT": ("psum", [128, 512], "float32"), "pz": ("psum", [128, 512], "float32"), "pS": ("psum", [128, 512], "float32"),
     "pC": ("psum", [128, 512], "float32"), "pN": ("psum", [128, 512], "float32"),
@@ -190,23 +198,30 @@ def make_ops(g, core, T, topo, rank, banks):
     ts(T.Z[:], T.iof[:], col(3), A.is_equal, col(8), A.mult, 144, ["iof", "c3", "c8"], ["Z"])
     ts(T.Zu[:], T.iof[:], col(3), A.is_equal, col(5), A.mult, 144, ["iof", "c3", "c5"], ["Zu"])
     ts(T.BO[:], T.jg[:], col(2), A.is_equal, None, None, 128, ["jg", "c2"], ["BO"])
-    act(T.Wl[:, 0, :], T.BO[:], F.Copy, 128, ["BO", "c7"], ["Wl0"], scale=col(7))
+    ms(T.tw[:, 0, :], float(2.0 ** -0.75), 128, ["tw0"])
+    scan(T.tw[:, 1, :], T.tw[:, 0, :], ta(1), A.mult, A.add, 128, ["tw0", "ta1"], ["tw1"], float(2 ** 90))
+    act(T.tw[:, 0, :], ta(2), F.Copy, 128, ["ta2"], ["tw0"], scale=float(2 ** 22))
+    tt(T.tw[:, 2, :], T.tw[:, 0, :], T.tw[:, 1, :], A.mult, 128, ["tw0", "tw1"], ["tw2"])
+    op("V", lambda: [V.tensor_reduce(col(9), T.tw[:, 2, 0:16], AxisListType.X, A.add)], vc(16), ["tw2"], ["c9"])
+    act(T.Wl[:, 0, :], T.BO[:], F.Copy, 128, ["BO", "c9"], ["Wl0"], scale=col(9))
     for b in range(1, 8):
-        act(T.Wl[:, b, :], T.Wl[:, 0, :], F.Copy, 128, ["Wl0"], ["Wl%d" % b], scale=float(2.0 ** (-16 * b)))
+        act(T.Wl[:, b, :], T.Wl[:, 0, :], F.Copy, 128, ["Wl0"], ["Wl%d" % b], scale=float(2.0 ** (-12 * b)))
     WL = ["Wl%d" % b for b in range(8)]
     ts(ta(4), cm, col(1), A.not_equal, -1e29, A.mult, 128, ["cm", "c1"], ["ta4"])
-    act(T.offd[:], ta(4), F.Identity, 128, ["ta4"], ["offd"], bias=2048.0)
-    act(T.BOh[:], T.BO[:], F.Copy, 128, ["BO"], ["BOh"])
-    act(ta(5), ta(3), F.Copy, 128, ["ta3"], ["ta5"], scale=-2.5)
-    tt(T.thr[:], ta(4), ta(5), A.add, 128, ["ta4", "ta5"], ["thr"])
+    act(T.offd[:], ta(4), F.Identity, 128, ["ta4"], ["offd"], bias=8192.0)
+    act(ta(5), T.tw[:, 2, :], F.Copy, 128, ["tw2"], ["ta5"], scale=-2.575)
+    act(T.tw[:, 3, :], ta(4), F.Copy, 128, ["ta4"], ["tw3"], scale=2e8)
+    tt(T.thr[:], T.tw[:, 3, :], ta(5), A.add, 128, ["tw3", "ta5"], ["thr"])
     ts(T.eye[:], T.iof[:, 0:32], col(4), A.is_equal, None, None, 32, ["iof", "c4"], ["eye"])
     act(ta(6), cm, F.Identity, 128, ["cm"], ["ta6"], bias=51.0, scale=-1.0)
     tt(ta(7), ta(6), T.BO[:], A.mult, 128, ["ta6", "BO"], ["ta7"])
     act(T.iK[:], ta(7), F.Identity, 128, ["ta7"], ["iK"], bias=-100.0)
     ts(ta(8), cm, 0.0, A.is_equal, -BIG - 1.0, A.mult, 128, ["cm"], ["ta8"])
     act(T.d0T[:], ta(8), F.Identity, 128, ["ta8"], ["d0T"], bias=1.0)
-    ts(T.d0N[:], T.cm[:], 0.0, A.is_equal, -9e29, A.mult, 256, ["cm"], ["d0N"])
+    ts(T.d0N[:], T.cm[:], 0.0, A.is_equal, -1e29, A.mult, 256, ["cm"], ["d0N"])
+    act(T.d0N[:], T.d0N[:], F.Copy, 256, ["d0N"], ["d0N"], scale=1e9)
     ts(T.dum[:], T.dum[:], col(1), A.add, None, None, 32, ["dumA", "dumB", "c1"], ["dumA", "dumB", "dum"])
+    act(T.cx[:], T.dum[:, 0:8], F.Identity, 8, ["dum"], ["cx"], bias=-65585.0, scale=16.0)
     for W, wk, c in ((T.X1, "X1d", 4096), (T.X2, "X2d", 4096), (T.O1, "O1d", 4096), (T.O2, "O2d", 4096)):
         act(W[:, c:c + 256], T.cm[:], F.Copy, 256, ["cm"], [wk])
 
@@ -240,11 +255,7 @@ def make_ops(g, core, T, topo, rank, banks):
         sm = lambda j: sml(st, 10 + 3 * i + j, hs)
         k = lambda x: ks("%s%d" % (x, i), st, hs)
         ends = T.yo[:, yi, c0 + 15:c0 + 128 * n:16]
-        if pr["dS"] == 1 or (pr["dS"] == 2 and i == 1 and st % 4 > 1):
-            act(sm(0), ends, F.Sign, 8, yk, k("d"))
-        else:
-            ts(sm(0), ends, 0.0, A.is_gt, None, None, 8, yk, k("d"))
-        tt(sm(1), sm(0), T.dum[:, d0 + 8 * hs[0]:d0 + 8 * hs[-1] + 8], A.mult, 8, k("d") + ["dum"], k("e"))
+        tt(sm(1), ends, T.dum[:, d0 + 8 * hs[0]:d0 + 8 * hs[-1] + 8], A.min, 8, yk + ["dum"], k("e"))
         tt(sm(2), sm(1), sml(st, key, hs), A.max, 8, k("e") + ks(kn, st, hs), k("o"))
         cp(sul(st, 3 + i, hs), sm(2), 8, k("o"), ks(on, st, hs))
 
@@ -274,9 +285,9 @@ def make_ops(g, core, T, topo, rank, banks):
             cp(su(0), v, 8, [vk], [k("w")])
             ow, iw, ik, ok = Og[:, 0:4096], T.i2k[:, 0:4096], ["i2a", "i2k"], ok + ["O%dt" % rd]
         p3, u2 = U % 3, U % 2
-        act(T.Pf[:, p3, :], ow.indirect(su(0)), F.Identity, 128, ok + [k("w")], ["Pf%d" % p3], ind=True, bias=-2048.0)
+        act(T.Pf[:, p3, :], ow.indirect(su(0)), F.Identity, 128, ok + [k("w")], ["Pf%d" % p3], ind=True, bias=-8192.0)
         if pr["pS"]:
-            ts(T.P16[:, p3, :], T.Pf[:, p3, :], 2048.0, A.add, None, None, 128, ["Pf%d" % p3], ["P16%d" % p3])
+            ts(T.P16[:, p3, :], T.Pf[:, p3, :], 8192.0, A.add, None, None, 128, ["Pf%d" % p3], ["P16%d" % p3])
         else:
             vx(lambda: V.tensor_copy(T.P16[:, p3, :], ow.indirect(su(0))), 128, ok + [k("w")], ["P16%d" % p3], pr["ga"])
         ps, pn = bank()
@@ -288,7 +299,7 @@ def make_ops(g, core, T, topo, rank, banks):
             xb = n % 8
             ps, pk_ = bank()
             win = Xg[:, 0:4096].indirect(T.P16[:, p3, 32 * c:32 * c + 32])
-            xo = T.xg[:, xb, :]
+            xo = T.xg[:, 512 * xb:512 * xb + 512]
             if pr["vg"][s][4 * h + c] == "1":
                 vx(lambda xo=xo, win=win: V.tensor_copy(xo, win), 512, [xk, "P16%d" % p3], ["xg%d" % xb], pr["ga"])
             else:
@@ -323,27 +334,35 @@ def make_ops(g, core, T, topo, rank, banks):
             act(ob(144, 152), sm(3), F.Relu, 8, [k("r")], [k("m")], bias=BIG, scale=BIG / 32)
         else:
             ts(ob(144, 152), sm(3), 0.0, A.is_ge, BIG, A.mult, 8, [k("r")], [k("m")])
-        tt(sm(8), dm, ob(144, 152), A.min, 8, ["dum", k("m")], [k("c16")])
         ps, pn = bank()
-        mm(ps[:, 0:128], [(T.ident[:], T.offd[:]), (T.BOh[:], T.Pm[:, u2, :])], 128, ["BOh", "Pm%d" % u2, "ident", "offd"], [pn])
+        mm(ps[:, 0:128], [(T.ident[:], T.offd[:]), (T.BO[:], T.Pm[:, u2, :])], 128, ["BO", "Pm%d" % u2, "ident", "offd"], [pn], 5)
         scan(T.nvs[:, u2, :], T.d0N[:, 0:128], ps[:, 0:128], A.add, A.max, 128, ["d0N", pn], ["nvs%d" % u2])
         ps, pn = bank()
-        mm(ps[:, 0:128], [(T.BOh[:], T.Pm[:, u2, :])], 128, ["BOh", "Pm%d" % u2], [pn])
+        mm(ps[:, 0:128], [(T.BO[:], T.Pm[:, u2, :])], 128, ["BO", "Pm%d" % u2], [pn], 4)
         if pr["eS"][2 * s + h] < 8:
-            ts(T.nvr[:, y, :], ps[:, 0:128], 2048.0, A.add, None, None, 128, [pn], ["nvr%d" % y])
+            ts(T.nvr[:, y, :], ps[:, 0:128], 8192.0, A.add, None, None, 128, [pn], ["nvr%d" % y])
         if pr["eS"][2 * s + h] > 0:
             if pr["eS"][2 * s + h] < 8:
                 ps, pn = bank()
-                mm(ps[:, 0:128], [(T.BOh[:], T.Pm[:, u2, :])], 128, ["BOh", "Pm%d" % u2], [pn])
-            act(T.nvf[:, y % 4, :], ps[:, 0:128], F.Identity, 128, [pn], ["nvf%d" % (y % 4)], bias=2048.0)
+                mm(ps[:, 0:128], [(T.BO[:], T.Pm[:, u2, :])], 128, ["BO", "Pm%d" % u2], [pn], 4)
+            act(T.nvf[:, y, :], ps[:, 0:128], F.Identity, 128, [pn], ["nvf%d" % y], bias=8192.0)
         nvd = sm(9)
-        tt(nvd, T.nvs[:, u2, 15:128:16], sm(8), A.max, 8, ["nvs%d" % u2, k("c16")], [k("nv")])
-        cp(su(2), nvd, 8, [k("nv")], [k("nu")])
+        tt(nvd, T.nvs[:, u2, 15:128:16], dm, A.min, 8, ["nvs%d" % u2, "dum"], [k("nv")])
+        if s == 0:
+            cp(T.sq[:, 2 * rd + h, :], nvd, 8, [k("nv")], [k("n0")])
+            act(T.zq[:, h, :], Xg[:, 0:4352].indirect(T.sq[:, 2 * rd + h, :]), F.Copy, 128, [xk, xk + "d", k("n0")], ["zq%d" % h], ind=True)
+        if s == 3:
+            cp(su(2), nvd, 8, [k("nv")], [k("nu")])
+            zw, zwk = Xg[:, 0:4352], [xk, xk + "d", k("nu")]
+        else:
+            tt(sm(8), T.cx[:], sm(3), A.subtract, 8, ["cx", k("r")], [k("xo")])
+            cp(su(2), sm(8), 8, [k("xo")], [k("nu")])
+            zw, zwk = T.xg[:, 2048 * u2:2048 * u2 + 2048], ["xg%d" % (4 * u2 + c) for c in range(4)] + [k("nu")]
         if s < 3:
-            act(ob(0, 128), Xg[:, 0:4352].indirect(su(2)), F.Copy, 128, [xk, xk + "d", k("nu")], [k("nz")], ind=True)
+            act(ob(0, 128), zw.indirect(su(2)), F.Copy, 128, zwk, [k("nz")], ind=True)
             act(T.pv[:, y, :], ob(0, 128), F.Relu, 128, [k("nz")], ["pv%d" % y], bias=-37.0)
         else:
-            act(T.pv[:, y, :], Xg[:, 0:4352].indirect(su(2)), F.Relu, 128, [xk, xk + "d", k("nu")], ["pv%d" % y], bias=-37.0, ind=True)
+            act(T.pv[:, y, :], zw.indirect(su(2)), F.Relu, 128, zwk, ["pv%d" % y], bias=-37.0, ind=True)
         if pr["gS"]:
             act(sm(4), sm(3), F.Relu, 8, [k("r")], [k("gb")], bias=-16 * BIG, scale=-BIG / 2)
         else:
@@ -355,7 +374,7 @@ def make_ops(g, core, T, topo, rank, banks):
             tt(sm(5), T.vri[:, vi_ + 1, :], sm(4), A.add, 8, [k("vr"), k("gb")], [k("t")])
         else:
             tt(sm(5), v, sm(4), A.add, 8, [vk, k("gb")], [k("t")])
-        tt(ob(128, 136), nvd, sm(5), A.min, 8, [k("nv"), k("t")], [k("v")])
+        tt(ob(128, 136), T.nvs[:, u2, 15:128:16], sm(5), A.min, 8, ["nvs%d" % u2, k("t")], [k("v")])
         tt(ob(136, 144), sm(1), ob(144, 152), A.max, 8, [k("q"), k("m")], [k("M")])
         if s > 0:
             tt(ob(152, 160), dm, sm(4), A.min, 8, ["dum", k("gb")], [k("fb")])
@@ -368,7 +387,7 @@ def make_ops(g, core, T, topo, rank, banks):
         else:
             send([(1, ob(128, 144), T.LV[:, 2 * rd + h, :], "f%d" % U, "LV/%d" % (2 * rd + h)), back], [k("v"), k("M"), k("m"), k("fb")])
         if s == 0:
-            tt(T.zs[:, h, :], z, ob(0, 128), A.add, 128, [zk, k("nz")], ["zs%d" % h])
+            tt(T.zs[:, h, :], z, T.zq[:, h, :], A.add, 128, [zk, "zq%d" % h], ["zs%d" % h])
             ts(T.zs[:, h, :], T.zs[:, h, :], -0.5, A.add, C2, A.add, 128, ["zs%d" % h], ["zs%d" % h])
             act(T.zr[:, rd, 128 * h:128 * h + 128], T.zs[:, h, :], F.Identity, 128, ["zs%d" % h], ["zr%d/%d" % (rd, h)], bias=-C2 / 2, scale=0.5)
         if s < 3:
@@ -401,7 +420,7 @@ def make_ops(g, core, T, topo, rank, banks):
             y = (2 * st + h) % 6
             for b in range(pr["eS"][2 * s + h]):
                 kc, ab = T.sm[:, NS * st + ki, 8 * h + b:8 * h + b + 1], T.ab[:, b % 4, :]
-                act(ab, T.nvf[:, y % 4, :], F.Abs, 128, ["nvf%d" % (y % 4)] + ks(kn, st, [h]), ["ab%d" % (b % 4)], bias=kc, scale=-1.0)
+                act(ab, T.nvf[:, y, :], F.Abs, 128, ["nvf%d" % y] + ks(kn, st, [h]), ["ab%d" % (b % 4)], bias=kc, scale=-1.0)
                 act(T.eqp[:, 8 * e4(h) + b, :], ab, F.Relu, 128, ["ab%d" % (b % 4)], ["eqp%d/%d" % (e4(h), b)], bias=1.0, scale=-1.0)
             for b in range(pr["eS"][2 * s + h], 8):
                 ts(T.eqp[:, 8 * e4(h) + b, :], T.nvr[:, y, :], T.sm[:, NS * st + ki, 8 * h + b:8 * h + b + 1], A.is_equal, None, None, 128,
@@ -471,6 +490,7 @@ def make_ops(g, core, T, topo, rank, banks):
                 if s > 0 and (s > pr["both"] or h == 1):
                     hs = [h] if s > pr["both"] else [0, 1]
                     penalty(rd, s - 1, hs)
+                    lift[0] = pr["lift"] + (pr["last"] if rd == 1 and s == 3 else 0.0)
                     exonerate(rd, s - 1, hs)
                 lift[0] = 0.0
             if rd == 0 and s == 0:
@@ -535,6 +555,7 @@ def arrange(ops, deps):
     for i in range(n - 1, -1, -1):
         way[i] = ops[i]["c"] + after(ops[i]) + max([way[j] for j in succ[i]] + [0.0])
     rank_ = [way[i] + (ops[i]["lift"] or ops[i]["first"]) for i in range(n)]
+    rank_ = [x + PARAM["tie"] * ((i * 7919 + PARAM["mix"]) * (i + PARAM["mix"]) % 1009) / 1009.0 for i, x in enumerate(rank_)]
     left = [len(set(j for j, _x in deps[i])) for i in range(n)]
     ready = [0.0] * n
     free = {q: 0.0 for q in "VSPGY"}
@@ -556,7 +577,7 @@ def arrange(ops, deps):
     while pool:
         best = min(pool, key=lambda i: (start(i), -rank_[i]))
         q = queue(ops[best])
-        soon = start(best) + PARAM["hold"] * ops[best]["c"]
+        soon = start(best) + PARAM["hold" + (q if q in "PS" else "")] * ops[best]["c"]
         assert soon < 1e17
         for i in pool:
             if queue(ops[i]) == q and rank_[i] > rank_[best] and start(i) < soon:

@@ -5,62 +5,62 @@ BIG = float(2 ** 23)
 CF = float(3 * 2 ** 28)
 CB = float(3 * 2 ** 12)
 C2 = float(3 * 2 ** 23)
+CM = float(3 * 2 ** 34)
 C0 = 192.0
 S0 = 1.3046875
-PARAM = {"sv": ("00100001", "10101000", "11111100", "11101110"), "vg": ("01000100", "00011010", "00000000", "00000000"),
-         "pS": 1, "mS": 1, "gS": 1, "dS": 2, "wS": 0, "both": 0, "hold": 0.2, "holdP": 0.5, "holdS": 0.2, "last": 1.0, "lift": 1.0, "spare": 2, "nt": 2,
-         "ahead": (3000.0, 3000.0, 3000.0, 3000.0), "eS": (0, 0, 0, 0, 4, 0, 0, 8),
-         "cyc": 1.04, "pe": 0.52, "ga": 1.56, "sc": 3.8, "lat": 170.0, "rem": 2500.0, "fix": 0.0, "bw": 250.0}
-PARAM.update({'lat': 230.0, 'cyc': 0.9, 'pe': 0.45, 'rem': 2300.0, 'pS': 0, 'mS': 0, 'gS': 1, 'dS': 2, 'lift': 2000.0, 'fix': 10.0,
-              'sv': ('00100001', '11001111', '00000000', '11100001'), 'eS': (0, 0, 0, 0, 4, 0, 0, 4),
-              'ahead': (1000.0, 1000.0, 3000.0, 1000.0), 'vg': ('00100100', '00011010', '00000000', '10001000')})
-PARAM.update({'lat': 250.0, 'eS': (0, 0, 0, 8, 2, 0, 8, 4), 'lift': 1000.0, 'ahead': (2000.0, 1000.0, 6000.0, 1000.0),
-              'sv': ('10101010', '01001111', '00000000', '00010001'), 'fix': 0.0, 'holdS': 0.8, 'tie': 0.0, 'mix': 0})
-PARAM.update({'vg': ('01100110', '10000100', '01000100', '00000000'), 'sv': ('00000100', '10000001', '10101110', '01100110'),
-              'ahead': (2000.0, 3000.0, 2000.0, 1000.0), 'rem': 2000.0, 'holdS': 0.3, 'eS': (0, 0, 0, 4, 4, 0, 0, 4),
-              'lift': -1500.0, 'mS': 1, 'lat': 230.0})
-PARAM.update({'sv': ('00100100', '00000001', '10101110', '01100110'), 'vg': ('00010110', '10000100', '01000100', '00000000'),
-              'ahead': (4000.0, 3000.0, 2000.0, 1000.0), 'lift': 1.0, 'eS': (0, 0, 0, 2, 4, 0, 0, 4)})
-NS = 20
+M0 = 64.0 * 34816
+XO, SP, ST, WN = 2048, 6144, 6400, 7168
+PARAM = {"sv": ("00000000", "00000000", "00000000", "00000000"), "vg": ("00000000", "00000000", "00000000", "00000000"),
+         "kS": "00000000", "hS": "00000000", "pS": "0000", "both": 0, "hold": 0.2, "holdP": 0.5, "holdS": 0.3, "lift": 1.0, "spare": 2, "nt": 2,
+         "ahead": (2000.0, 2000.0, 2000.0, 1000.0),
+         "cyc": 0.9, "pe": 0.45, "ga": 1.56, "sc": 3.8, "lat": 200.0, "rem": 1800.0, "bw": 250.0, "dma": 1800.0, "iss": 600.0}
+PARAM.update({'sv': ('0000000000', '0000000000', '1000010000', '1000011000'), 'vg': ('1000001000', '1000010000', '0000000000', '0000000100'),
+              'kS': '01001101', 'ch': ((2, 2, 2, 1, 1),) * 4, 'mV': '0001', 'zV': '000000',
+              'hS': '00010010', 'holdS': 0.6, 'spare': 0, 'ahead': (1000.0, 4000.0, 1000.0, 0.0), 'lat': 150.0})
+PARAM.update({'sv': ('0011010000', '0000000000', '1000010100', '1001011100'), 'vg': ('1000101000', '1000010010', '0000100000', '0001000100'), 'kS': '00001101', 'hS': '20010010', 'pS': '0000', 'both': 0, 'hold': 0.5, 'holdP': 0.5, 'holdS': 0.6, 'lift': 1.0, 'spare': 1, 'nt': 2, 'ahead': (1000.0, 2000.0, 3000.0, 0.0), 'cyc': 0.83, 'lat': 200.0, 'rem': 2000.0, 'ch': ((2, 2, 1, 2, 1), (2, 2, 2, 1, 1), (2, 2, 1, 2, 1), (2, 2, 2, 1, 1)), 'mV': '1000', 'zV': '100011'})
+PARAM.update({'sv': ('0000000000', '0000001001', '1100111000', '1110011110'), 'vg': ('1000010000', '1000010000', '1000000001', '0000010000'), 'kS': '10111111', 'hS': '10110200', 'pS': '0000', 'both': 0, 'hold': 0.5, 'holdP': 0.5, 'holdS': 0.6, 'lift': 1.0, 'spare': 0, 'nt': 2, 'ahead': (2000.0, 2000.0, 4000.0, 0.0), 'cyc': 0.83, 'lat': 200.0, 'rem': 2000.0, 'ch': ((2, 2, 2, 1, 1), (2, 2, 1, 2, 1), (1, 1, 2, 2, 2), (2, 2, 1, 2, 1)), 'mV': '0000', 'zV': '001111', 'turns': 2, 'keep': 0.0, 'back': 0})
+NS = 12
 
 SCRATCH = {
-    "X0": ("sbuf", [128, 4352], "bfloat16"), "X1": ("sbuf", [128, 4352], "bfloat16"), "X2": ("sbuf", [128, 4352], "bfloat16"),
-    "O0": ("sbuf", [128, 4096], "float32"), "O1": ("sbuf", [128, 4352], "float32"), "O2": ("sbuf", [128, 4352], "float32"),
+    "X0": ("sbuf", [128, 4352], "bfloat16"), "O0": ("sbuf", [128, 4096], "float32"),
+    "W1": ("sbuf", [128, 2048 + WN], "float32"), "W2": ("sbuf", [128, WN], "float32"),
     "nbi": ("sbuf", [128, 1024], "int32"), "nbt": ("sbuf", [128, 2048], "int32"), "pk": ("sbuf", [128, 1024], "float32"),
-    "vi": ("sbuf", [128, 16], "int32"), "v0": ("sbuf", [128, 16], "float32"),
+    "vi": ("sbuf", [128, 16], "int32"), "v0": ("sbuf", [128, 16], "int32"), "vf": ("sbuf", [128, 16], "float32"),
     "zr": ("sbuf", [128, 2, 256], "bfloat16"), "zs": ("sbuf", [128, 2, 128], "float32"),
-    "LF": ("sbuf", [128, 12, 16], "float32"), "LB": ("sbuf", [128, 12, 16], "float32"), "LV": ("sbuf", [128, 4, 16], "float32"),
-    "LU": ("sbuf", [128, 4, 16], "float32"), "US": ("sbuf", [128, 2, 16], "float32"), "OB": ("sbuf", [128, 16, 32], "float32"),
-    "ui": ("sbuf", [128, 4, 16], "int32"), "vri": ("sbuf", [128, 8, 8], "int32"),
-    "sm": ("sbuf", [128, 8 * NS, 16], "float32"), "su": ("sbuf", [128, 8 * 5, 16], "uint16"),
-    "P16": ("sbuf", [128, 3, 128], "uint16"), "Pf": ("sbuf", [128, 3, 128], "float32"), "Pm": ("sbuf", [128, 2, 128], "float32"),
-    "OZ": ("sbuf", [128, 16, 128], "bfloat16"), "LZ": ("sbuf", [128, 12, 128], "bfloat16"),
+    "LF": ("sbuf", [128, 12, 16], "int32"), "LB": ("sbuf", [128, 12, 32], "bfloat16"), "LV": ("sbuf", [128, 4, 16], "int32"),
+    "LN": ("sbuf", [128, 12, 8], "uint16"), "ON": ("sbuf", [128, 12, 8], "uint16"), "m1": ("sbuf", [128, 16, 8], "bfloat16"),
+    "idB": ("sbuf", [128, 128], "bfloat16"), "OM": ("sbuf", [128, 16, 32], "bfloat16"),
+    "LU": ("sbuf", [128, 4, 16], "float32"), "US": ("sbuf", [128, 2, 16], "float32"), "OB": ("sbuf", [128, 16, 16], "int32"),
+    "ui": ("sbuf", [128, 4, 16], "int32"), "vr": ("sbuf", [128, 12, 8], "int32"), "wI": ("sbuf", [128, 8, 16], "int32"),
+    "sm": ("sbuf", [128, 8 * NS, 16], "float32"), "su": ("sbuf", [128, 8 * 6, 16], "uint16"),
+    "P16": ("sbuf", [128, 3, 128], "uint16"), "Pf": ("sbuf", [128, 3, 128], "float32"), "Pm": ("sbuf", [128, 2, 128], "float16"),
+    "OZ": ("sbuf", [128, 12, 128], "bfloat16"), "LZ": ("sbuf", [128, 12, 128], "bfloat16"),
     "zT": ("sbuf", [128, 2, 128], "bfloat16"), "xg": ("sbuf", [128, 4096], "bfloat16"), "cx": ("sbuf", [128, 8], "float32"),
-    "sq": ("sbuf", [128, 4, 8], "uint16"), "zq": ("sbuf", [128, 2, 128], "bfloat16"), "lv": ("sbuf", [128, 8, 512], "bfloat16"),
-    "near": ("sbuf", [128, 16, 256], "bfloat16"), "key": ("sbuf", [128, 2, 128], "float32"),
-    "nvs": ("sbuf", [128, 2, 128], "float32"), "nvr": ("sbuf", [128, 6, 128], "uint16"), "wr": ("sbuf", [128, 2, 128], "uint16"),
-    "nvf": ("sbuf", [128, 6, 128], "float32"), "ab": ("sbuf", [128, 4, 128], "float32"),
-    "wf": ("sbuf", [128, 2, 128], "float32"), "yo": ("sbuf", [128, 4, 256], "float32"),
-    "eqp": ("sbuf", [128, 32, 128], "bfloat16"), "eqe": ("sbuf", [128, 48, 128], "float16"), "lh": ("sbuf", [128, 16, 128], "float16"),
-    "pv": ("sbuf", [128, 6, 128], "bfloat16"), "cs": ("sbuf", [128, 2, 128], "float32"), "nw": ("sbuf", [128, 4, 128], "int32"),
+    "zq": ("sbuf", [128, 2, 128], "bfloat16"), "lv": ("sbuf", [128, 4, 512], "bfloat16"),
+    "near": ("sbuf", [128, 16, 16, 17], "bfloat16"), "key": ("sbuf", [128, 4, 136], "float32"),
+    "kr": ("sbuf", [128, 4, 128], "uint16"), "kf": ("sbuf", [128, 4, 128], "float32"), "D": ("sbuf", [128, 6 * 136], "float32"), "yo": ("sbuf", [128, 2, 272], "float32"),
+    "eq": ("sbuf", [128, 32, 8, 17], "float16"), "lh": ("sbuf", [128, 16, 128], "float16"),
+    "cs": ("sbuf", [128, 2, 128], "float32"), "ys": ("sbuf", [128, 2, 128], "float32"), "hs": ("sbuf", [128, 2, 128], "float32"),
     "cnt": ("sbuf", [128, 96], "float32"), "col": ("sbuf", [128, 64], "float32"), "coli": ("sbuf", [128, 16], "int32"),
     "colb": ("sbuf", [128, 8], "bfloat16"),
     "iof": ("sbuf", [128, 144], "float32"), "cm": ("sbuf", [128, 256], "float32"), "jg": ("sbuf", [128, 128], "float32"),
-    "i2k": ("sbuf", [128, 4096], "float32"),
-    "ident": ("sbuf", [128, 128], "bfloat16"), "E": ("sbuf", [128, 2048], "bfloat16"),
-    "Z": ("sbuf", [128, 144], "bfloat16"), "Zu": ("sbuf", [128, 144], "bfloat16"), "BO": ("sbuf", [128, 128], "float32"),
-    "Wl": ("sbuf", [128, 8, 128], "bfloat16"), "pw": ("sbuf", [128, 128], "float32"),
-    "thr": ("sbuf", [128, 128], "bfloat16"), "offd": ("sbuf", [128, 128], "bfloat16"),
-    "ta": ("sbuf", [128, 10, 128], "float32"), "eye": ("sbuf", [128, 32], "bfloat16"), "iK": ("sbuf", [128, 128], "bfloat16"),
-    "d0T": ("sbuf", [128, 128], "float32"), "d0N": ("sbuf", [128, 256], "float32"), "dum": ("sbuf", [128, 32], "float32"),
-    "dgb": ("sbuf", [128, 2, 128], "bfloat16"), "tw": ("sbuf", [128, 4, 128], "float32"),
+    "i2k": ("sbuf", [128, ST], "float32"),
+    "ident": ("sbuf", [128, 128], "bfloat16"), "identF": ("sbuf", [128, 128], "float32"), "E": ("sbuf", [128, 2048], "bfloat16"),
+    "eye": ("sbuf", [128, 2048], "bfloat16"), "iK": ("sbuf", [128, 8, 128], "float16"),
+    "Z": ("sbuf", [128, 144], "bfloat16"), "Zu": ("sbuf", [128, 144], "bfloat16"), "Z1": ("sbuf", [128, 144], "float16"),
+    "BO": ("sbuf", [128, 128], "float32"), "Wl": ("sbuf", [128, 8, 128], "bfloat16"), "pw": ("sbuf", [128, 128], "float32"),
+    "thr": ("sbuf", [128, 8, 17], "bfloat16"), "half": ("sbuf", [128, 136], "bfloat16"),
+    "ta": ("sbuf", [128, 8, 128], "float32"), "d0T": ("sbuf", [128, 2, 136], "float32"),
+    "dum": ("sbuf", [128, 16], "float32"), "stg": ("sbuf", [128, 48], "float32"),
+    "dgb": ("sbuf", [128, 2, 128], "bfloat16"), "tw": ("sbuf", [128, 3, 128], "float32"),
     "pd0": ("psum", [128, 512], "float32"), "pd1": ("psum", [128, 512], "float32"), "pd2": ("psum", [128, 512], "float32"),
-    "pT": ("psum", [128, 512], "float32"), "pz": ("psum", [128, 512], "float32"), "pS": ("psum", [128, 512], "float32"),
-    "pC": ("psum", [128, 512], "float32"), "pN": ("psum", [128, 512], "float32"),
+    "pd3": ("psum", [128, 512], "float32"), "pd4": ("psum", [128, 512], "float32"), "pd5": ("psum", [128, 512], "float32"),
+    "pd6": ("psum", [128, 512], "float32"), "pd7": ("psum", [128, 512], "float32"),
 }
-PSUM = ("pd0", "pd1", "pd2", "pT", "pz", "pS", "pC", "pN")
-SEMAPHORES = (["cV", "cS", "cP", "cG", "sent"] + ["d%d" % i for i in range(20)] + ["f%d" % i for i in range(16)]
-              + ["t%d" % i for i in range(16)] + ["b%d" % i for i in range(16)] + ["u%d" % i for i in range(4)])
+PSUM = tuple("pd%d" % i for i in range(8))
+SEMAPHORES = (["cV", "cS", "cP", "cG", "sent"] + ["d%d" % i for i in range(30)] + ["f%d" % i for i in range(16)]
+              + ["t%d" % i for i in range(16)] + ["b%d" % i for i in range(16)] + ["n%d" % i for i in range(16)]
+              + ["u%d" % i for i in range(4)])
 ORDER = {}
 
 
@@ -73,7 +73,6 @@ def make_ops(g, core, T, topo, rank, banks):
         name = "#%d" % uses[0]
         return T[banks.get(name, PSUM[0])], name
 
-    cyc, pe = pr["cyc"], pr["pe"]
     V, S, PE = g.vector, g.scalar, g.tensor
     ops = []
     ndma = [0]
@@ -81,31 +80,25 @@ def make_ops(g, core, T, topo, rank, banks):
     ahead = [0.0]
 
     def op(eng, fn, cost, r, w, sems=None):
-        ops.append({"e": eng, "fn": fn, "c": cost, "r": list(r), "w": list(w), "sems": sems, "lift": lift[0], "first": ahead[0]})
+        ops.append({"e": eng, "fn": fn, "k": cost, "r": list(r), "w": list(w), "sems": sems, "lift": lift[0], "first": ahead[0]})
 
-    def vc(n, c=1.0):
-        return max(64.0, pr["fix"] + n * c) * cyc
-
-    def ts(out, in0, s1, o0, s2, o1, n, r, w, c=1.0):
+    def ts(out, in0, s1, o0, s2, o1, n, r, w, c=1.0, kind="v"):
         if o1 is None:
-            op("V", lambda: [V.tensor_scalar(out, in0, s1, None, o0)], vc(n, c), r, w)
+            op("V", lambda: [V.tensor_scalar(out, in0, s1, None, o0)], (kind, n * c), r, w)
         else:
-            op("V", lambda: [V.tensor_scalar(out, in0, s1, s2, o0, o1)], vc(n, c), r, w)
+            op("V", lambda: [V.tensor_scalar(out, in0, s1, s2, o0, o1)], (kind, n * c), r, w)
 
-    def tt(out, a, b, o, n, r, w, c=2.0):
-        op("V", lambda: [V.tensor_tensor(out, a, b, o)], vc(n, c), r, w)
+    def tt(out, a, b, o, n, r, w, c=2.0, kind="v"):
+        op("V", lambda: [V.tensor_tensor(out, a, b, o)], (kind, n * c), r, w)
 
-    def cp(out, a, n, r, w, c=1.0):
-        op("V", lambda: [V.tensor_copy(out, a)], vc(n, c), r, w)
-
-    def vx(fn, n, r, w, per):
-        op("V", lambda: [fn()], 62.0 + n * per * cyc, r, w)
+    def cp(out, a, n, r, w, c=1.0, kind="v"):
+        op("V", lambda: [V.tensor_copy(out, a)], (kind, n * c), r, w)
 
     def scan(out, d0, d1, o0, o1, n, r, w, init=0.0):
-        op("V", lambda: [V.tensor_tensor_scan(out, d0, d1, init, o0, o1)], vc(n), r, w)
+        op("V", lambda: [V.tensor_tensor_scan(out, d0, d1, init, o0, o1)], ("v", n), r, w)
 
     def ms(ap, val, n, w):
-        op("V", lambda: [V.memset(ap, val)], vc(n), [], w)
+        op("V", lambda: [V.memset(ap, val)], ("v", n), [], w)
 
     def act(out, in_, f, n, r, w, bias=None, scale=None, ind=False):
         kw = {}
@@ -113,31 +106,35 @@ def make_ops(g, core, T, topo, rank, banks):
             kw["bias"] = bias
         if scale is not None:
             kw["scale"] = scale
-        op("S", lambda: [S.activation(out, in_, f, **kw)], (80.0 + n * pr["ga"] * cyc) if ind else (vc(n) + 30.0), r, w)
+        op("S", lambda: [S.activation(out, in_, f, **kw)], ("sg" if ind else "s", n), r, w)
 
-    def mm(out, pairs, n, r, w, passes=0):
+    def mm(out, pairs, n, r, w, passes=0, first=True, last=True):
         def fn():
-            return [PE.matmul(out, l, x, i == 0, i == len(pairs) - 1) for i, (l, x) in enumerate(pairs)]
-        op("P", fn, (passes or len(pairs)) * max(64, n) * pe + 30.0, r, w)
+            return [PE.matmul(out, l, x, first and i == 0, last and i == len(pairs) - 1) for i, (l, x) in enumerate(pairs)]
+        op("P", fn, ("p", (passes or len(pairs)) * max(64, n)), r, w)
 
     def iota(out, pat, base, cm_, n, w, fl=True):
         if fl:
-            op("G", lambda: [g.iota(out, pat, base, cm_, allow_small_or_imprecise_dtypes=True)], 160.0 + 2 * n * cyc, [], w)
+            op("G", lambda: [g.iota(out, pat, base, cm_, allow_small_or_imprecise_dtypes=True)], ("g", n), [], w)
         else:
-            op("G", lambda: [g.iota(out, pat, base, cm_)], 160.0 + 2 * n * cyc, [], w)
+            op("G", lambda: [g.iota(out, pat, base, cm_)], ("g", n), [], w)
 
-    def dma(out, in_, nbytes, r, w):
+    def dma(out, in_, nbytes, r, w, cast=False):
         name = "d%d" % ndma[0]
         ndma[0] += 1
-        op("Y", lambda: [g.sync.dma_start(out, in_)], nbytes / pr["bw"], r, w, {"": name})
+        if cast:
+            op("C", lambda: [g.dma_start(out, in_)], ("c", nbytes), r, w, {"": name})
+        else:
+            op("Y", lambda: [g.sync.dma_start(out, in_)], ("y", nbytes), r, w, {"": name})
 
     def send(trs, r):
         n = len(trs)
+        cuts = {1: (0, 4), 2: (0, 2, 4), 3: (0, 2, 3, 4)}[n]
         made, sems = [], {}
         for i, (step, src, dst, sem, name) in enumerate(trs):
             to = T.cores[(rank + step) % len(T.cores)]
             en = topo.engines(core, to)
-            part = en[i * len(en) // n:(i + 1) * len(en) // n]
+            part = en[cuts[i] * len(en) // 4:cuts[i + 1] * len(en) // 4]
             rid, pid, _se = topo.addr(to)
             made.append((rid, pid, sum(1 << e for e in part), src, dst, sem))
             sems[name] = (sem, len(part))
@@ -150,10 +147,9 @@ def make_ops(g, core, T, topo, rank, banks):
                 g.remote_dma_fused([RemoteDMATransfer(dst_ids=[DstId(rid=rid, pnc=pid)], dma_engine_mask=mask, remote_sem=T.sem[sem],
                                                       src=src, dst=dst) for rid, pid, mask, src, dst, sem in made], local_sem=T.sem.sent)
             return []
-        op("R", fn, 500.0, r, [t[4] for t in trs], sems)
+        op("R", fn, ("r", n), r, [t[4] for t in trs], sems)
 
-    X = [T.X0, T.X1, T.X2]
-    O = [T.O0, T.O1, T.O2]
+    W = lambda rd, a, b: T.W1[:, 2048 + a:2048 + b] if rd == 0 else T.W2[:, a:b]
     col = lambda i: T.col[:, i:i + 1]
     ta = lambda i: T.ta[:, i, :]
 
@@ -163,27 +159,27 @@ def make_ops(g, core, T, topo, rank, banks):
     ahead[0] = 5e5
     dma(T.vi[:], T.v[:], 30000, [], ["vi"])
     dma(T.X0[:, 4096:4352], T.z[:], 65536, [], ["X0d"])
-    ahead[0] = 0.0
     dma(T.X0[:, 0:4096], T.tracks[:], 1048576, [], ["X0"])
-    dma(T.X1[:, 0:4096], T.tracks[:], 1048576, ["X0"], ["X1"])
+    ahead[0] = 0.0
 
     iota(T.coli[:, 0:1], [[0, 1]], 0, 1, 1, ["pi"], False)
     iota(T.iof[:], [[1, 144]], 0, 0, 144, ["iof"])
     iota(T.cm[:], [[0, 16], [1, 16]], 0, 0, 256, ["cm"])
     iota(T.jg[:], [[16, 8], [0, 16]], 0, 0, 128, ["jg"])
-    iota(T.dum[:, 0:16], [[16, 16]], 4096, 0, 16, ["dumA"])
-    iota(T.dum[:, 16:32], [[16, 16]], 2048, 0, 16, ["dumB"])
-    iota(T.i2k[:, 0:2048], [[1, 2048]], 0, 0, 2048, ["i2a"])
-    dma(T.i2k[:, 2048:4096], T.i2k[:, 0:2048], 1048576, ["i2a"], ["i2k"])
+    iota(T.stg[:], [[16, 48]], ST, 0, 48, ["stg"])
+    for c in range(8):
+        iota(T.i2k[:, 800 * c:800 * c + 800], [[1, 800]], 800 * c, 0, 800, ["i2k%d" % c])
+    IK = ["i2k%d" % c for c in range(8)]
     cm = T.cm[:, 0:128]
     cp(col(0), T.coli[:, 0:1], 1, ["pi"], ["c0"])
     ts(T.coli[:, 4:5], T.coli[:, 0:1], 15, A.bitwise_and, None, None, 1, ["pi"], ["ai"])
     cp(col(1), T.coli[:, 4:5], 1, ["ai"], ["c1"])
     tt(col(2), col(0), col(1), A.subtract, 1, ["c0", "c1"], ["c2"])
     act(col(3), col(2), F.Identity, 1, ["c2"], ["c3"], bias=15.0)
-    act(col(4), col(1), F.Identity, 1, ["c1"], ["c4"], bias=15.0, scale=-1.0)
+    act(col(4), col(1), F.Identity, 1, ["c1"], ["c4"], bias=4096.0, scale=16.0)
     act(col(5), col(1), F.Identity, 1, ["c1"], ["c5"], bias=1.0, scale=2.0)
     ts(T.ident[:], T.iof[:, 0:128], col(0), A.is_equal, None, None, 128, ["iof", "c0"], ["ident"])
+    act(T.identF[:], T.ident[:], F.Copy, 128, ["ident"], ["identF"])
     act(T.dgb[:, 0, :], T.ident[:], F.Copy, 128, ["ident"], ["dgb0"], scale=S0)
     for k in range(16):
         act(T.E[:, k:2048:16], T.ident[:], F.Copy, 128, ["ident"], ["E%d" % k], scale=-1.0)
@@ -193,264 +189,268 @@ def make_ops(g, core, T, topo, rank, banks):
     scan(T.pw[:], ta(0), ta(1), A.mult, A.add, 128, ["ta0", "ta1"], ["pw"], float(2 ** 64))
     ts(ta(2), cm, col(1), A.is_equal, None, None, 128, ["cm", "c1"], ["ta2"])
     tt(ta(3), ta(2), T.pw[:], A.mult, 128, ["ta2", "pw"], ["ta3"])
-    op("V", lambda: [V.tensor_reduce(col(7), T.ta[:, 3, 0:16], AxisListType.X, A.add)], vc(16), ["ta3"], ["c7"])
+    op("V", lambda: [V.tensor_reduce(col(7), T.ta[:, 3, 0:16], AxisListType.X, A.add)], ("v", 16), ["ta3"], ["c7"])
     act(col(8), col(7), F.Copy, 1, ["c7"], ["c8"], scale=float(2.0 ** -42))
     ts(T.Z[:], T.iof[:], col(3), A.is_equal, col(8), A.mult, 144, ["iof", "c3", "c8"], ["Z"])
     ts(T.Zu[:], T.iof[:], col(3), A.is_equal, col(5), A.mult, 144, ["iof", "c3", "c5"], ["Zu"])
+    ts(T.Z1[:], T.iof[:], col(3), A.is_equal, None, None, 144, ["iof", "c3"], ["Z1"])
     ts(T.BO[:], T.jg[:], col(2), A.is_equal, None, None, 128, ["jg", "c2"], ["BO"])
+    for c in range(16):
+        act(T.eye[:, 128 * c:128 * c + 128], ta(2), F.Copy, 128, ["ta2"], ["eye%d" % c])
+    EYE = ["eye%d" % c for c in range(16)]
     ms(T.tw[:, 0, :], float(2.0 ** -0.75), 128, ["tw0"])
     scan(T.tw[:, 1, :], T.tw[:, 0, :], ta(1), A.mult, A.add, 128, ["tw0", "ta1"], ["tw1"], float(2 ** 90))
-    act(T.tw[:, 0, :], ta(2), F.Copy, 128, ["ta2"], ["tw0"], scale=float(2 ** 22))
+    act(T.tw[:, 0, :], ta(2), F.Copy, 128, ["ta2"], ["tw0"], scale=float(2 ** 26))
     tt(T.tw[:, 2, :], T.tw[:, 0, :], T.tw[:, 1, :], A.mult, 128, ["tw0", "tw1"], ["tw2"])
-    op("V", lambda: [V.tensor_reduce(col(9), T.tw[:, 2, 0:16], AxisListType.X, A.add)], vc(16), ["tw2"], ["c9"])
+    op("V", lambda: [V.tensor_reduce(col(9), T.tw[:, 2, 0:16], AxisListType.X, A.add)], ("v", 16), ["tw2"], ["c9"])
     act(T.Wl[:, 0, :], T.BO[:], F.Copy, 128, ["BO", "c9"], ["Wl0"], scale=col(9))
     for b in range(1, 8):
         act(T.Wl[:, b, :], T.Wl[:, 0, :], F.Copy, 128, ["Wl0"], ["Wl%d" % b], scale=float(2.0 ** (-12 * b)))
     WL = ["Wl%d" % b for b in range(8)]
-    ts(ta(4), cm, col(1), A.not_equal, -1e29, A.mult, 128, ["cm", "c1"], ["ta4"])
-    act(T.offd[:], ta(4), F.Identity, 128, ["ta4"], ["offd"], bias=8192.0)
+    ts(ta(4), cm, col(1), A.not_equal, 1e29, A.mult, 128, ["cm", "c1"], ["ta4"])
     act(ta(5), T.tw[:, 2, :], F.Copy, 128, ["tw2"], ["ta5"], scale=-2.575)
-    act(T.tw[:, 3, :], ta(4), F.Copy, 128, ["ta4"], ["tw3"], scale=2e8)
-    tt(T.thr[:], T.tw[:, 3, :], ta(5), A.add, 128, ["tw3", "ta5"], ["thr"])
-    ts(T.eye[:], T.iof[:, 0:32], col(4), A.is_equal, None, None, 32, ["iof", "c4"], ["eye"])
-    act(ta(6), cm, F.Identity, 128, ["cm"], ["ta6"], bias=51.0, scale=-1.0)
+    ms(T.thr[:], 1e29, 68, ["thr"])
+    tt(T.thr[:, :, 0:16], ta(4), ta(5), A.add, 128, ["ta4", "ta5", "thr"], ["thr"])
+    act(ta(6), cm, F.Identity, 128, ["cm", "c4"], ["ta6"], bias=col(4))
     tt(ta(7), ta(6), T.BO[:], A.mult, 128, ["ta6", "BO"], ["ta7"])
-    act(T.iK[:], ta(7), F.Identity, 128, ["ta7"], ["iK"], bias=-100.0)
-    ts(ta(8), cm, 0.0, A.is_equal, -BIG - 1.0, A.mult, 128, ["cm"], ["ta8"])
-    act(T.d0T[:], ta(8), F.Identity, 128, ["ta8"], ["d0T"], bias=1.0)
-    ts(T.d0N[:], T.cm[:], 0.0, A.is_equal, -1e29, A.mult, 256, ["cm"], ["d0N"])
-    act(T.d0N[:], T.d0N[:], F.Copy, 256, ["d0N"], ["d0N"], scale=1e9)
-    ts(T.dum[:], T.dum[:], col(1), A.add, None, None, 32, ["dumA", "dumB", "c1"], ["dumA", "dumB", "dum"])
-    act(T.cx[:], T.dum[:, 0:8], F.Identity, 8, ["dum"], ["cx"], bias=-65585.0, scale=16.0)
-    for W, wk, c in ((T.X1, "X1d", 4096), (T.X2, "X2d", 4096), (T.O1, "O1d", 4096), (T.O2, "O2d", 4096)):
-        act(W[:, c:c + 256], T.cm[:], F.Copy, 256, ["cm"], [wk])
+    for b in range(8):
+        ts(T.iK[:, b, :], ta(7), 256.0 * b - 4096.0, A.add, None, None, 128, ["ta7"], ["iK%d" % b])
+    ts(T.stg[:], T.stg[:], col(1), A.add, None, None, 48, ["stg", "c1"], ["stg"])
+    act(T.dum[:], T.stg[:, 0:16], F.Identity, 16, ["stg"], ["dum"], bias=float(SP - ST))
+    for i in range(2):
+        ms(T.d0T[:, i, :], float(i), 136, ["d0T%d" % i])
+        ms(T.d0T[:, i, 0:136:17], -BIG, 8, ["d0T%d" % i])
+    act(T.d0T[:, 1, 16:136:17], T.stg[:, 0:8], F.Identity, 8, ["stg"], ["d0T1"], bias=16.0 * ST - 15.0, scale=-16.0)
+    ms(T.near[:, :, :, 16:17], -1.0, 128, ["nearz"])
+    act(T.idB[:], T.ident[:], F.Copy, 128, ["ident"], ["idB"], scale=BIG)
+    DK = ["D%d" % i for i in range(6)]
+    ms(T.D[:], -1e29, 816, DK)
+    for i in range(3):
+        act(T.D[:, 272 * i:272 * i + 272:17], T.dum[:], F.Copy, 16, ["dum"], DK[2 * i:2 * i + 2])
+    EQ = ["eq%d/%d" % (e, b) for e in range(4) for b in range(8)]
+    ts(T.eq[:, :, :, 16:17], T.cm[:], 0.0, A.mult, None, None, 256, ["cm"], ["eqz"])
+    ms(T.half[:, 0:128], -0.5, 64, ["half"])
+    ms(T.half[:, 128:136], 4096.0, 8, ["c4k"])
+    ms(T.OM[:], 0.0, 256, ["OM"])
+    for rd in range(2):
+        for c in range(4):
+            act(W(rd, SP + 256 * c, SP + 256 * c + 256), T.cm[:], F.Copy, 256, ["cm"],
+                ["W%dd" % rd] if c == 0 else ["W%ds%d" % (rd, y) for y in (2 * c - 2, 2 * c - 1)])
 
     for c in range(2):
         for hi in range(2):
             a = 1024 * hi + 512 * c
             ts(T.nbt[:, a:a + 512], T.nbi[:, 512 * c:512 * c + 512], 12 if hi else 4095, A.logical_shift_right if hi else A.bitwise_and,
                None, None, 512, ["nbi%d" % c], ["nbt%d" % a])
-            cp(T.O0[:, 2048 + a:2560 + a], T.nbt[:, a:a + 512], 512, ["nbt%d" % a], ["O0/%d" % a])
-    OK = [["O0/%d" % a for a in range(0, 2048, 512)], ["O1"]]
-    dma(T.O0[:, 0:2048], T.O0[:, 2048:4096], 1048576, OK[0], ["O0t"])
-    dma(T.O1[:, 2048:4096], T.O0[:, 2048:4096], 1048576, OK[0], ["O1"])
-    cp(T.v0[:], T.vi[:], 16, ["vi"], ["v0"])
+            ts(T.O0[:, 2048 + a:2560 + a], T.nbt[:, a:a + 512], -2048.0, A.add, None, None, 512, ["nbt%d" % a], ["O0/%d" % a])
+    OK = [["O0/%d" % a for a in range(0, 2048, 512)], ["W0o"]]
+    dma(T.O0[:, 0:2048], T.O0[:, 2048:4096], 1048576, OK[0] + ["X0"], ["O0t"])
+    ts(T.v0[:], T.vi[:], 2048.0, A.add, None, None, 16, ["vi"], ["v0"])
 
     chunk = [0]
     sml = lambda st, i, hs: T.sm[:, NS * st + i, 8 * hs[0]:8 * hs[-1] + 8]
-    sul = lambda st, i, hs: T.su[:, 5 * st + i, 8 * hs[0]:8 * hs[-1] + 8]
+    sul = lambda st, i, hs: T.su[:, 6 * st + i, 8 * hs[0]:8 * hs[-1] + 8]
     ks = lambda n, st, hs: ["%s/%d" % (n, 2 * st + h) for h in hs]
-
-    def first(st, hs, i, eq, ek, key, kn, d0, on):
-        n, c0 = len(hs), 128 * hs[0]
-        ps, pn = bank()
-        pairs = []
-        for h in hs:
-            e0, names = ek(h)
-            mm(ps[:, 128 * h:128 * h + 128], [(T.Wl[:, b, :], eq[:, e0 + b, :]) for b in range(8)] + [(T.ident[:], T.thr[:])], 128,
-               WL + [x for h_ in hs for x in ek(h_)[1]] + ["ident", "thr"], [pn])
-        yi = 2 * i + st % 2
-        yk = ["yo%d/%d" % (yi, h) for h in hs]
-        scan(T.yo[:, yi, c0:c0 + 128 * n], T.d0N[:, 0:128 * n], ps[:, c0:c0 + 128 * n], A.add, A.max, 128 * n, ["d0N", pn], yk)
-        sm = lambda j: sml(st, 10 + 3 * i + j, hs)
-        k = lambda x: ks("%s%d" % (x, i), st, hs)
-        ends = T.yo[:, yi, c0 + 15:c0 + 128 * n:16]
-        tt(sm(1), ends, T.dum[:, d0 + 8 * hs[0]:d0 + 8 * hs[-1] + 8], A.min, 8, yk + ["dum"], k("e"))
-        tt(sm(2), sm(1), sml(st, key, hs), A.max, 8, k("e") + ks(kn, st, hs), k("o"))
-        cp(sul(st, 3 + i, hs), sm(2), 8, k("o"), ks(on, st, hs))
+    slot = lambda st, h: (4 if st % 4 == 3 else 2 * (st % 2)) + h
+    keys = lambda st, hs: T.D[:, 136 * slot(st, hs[0]) + 16:136 * slot(st, hs[-1]) + 136:17]
 
     def station(rd, s, h):
         st = 4 * rd + s
         U = 2 * st + h
         k = lambda n: "%s/%d" % (n, U)
-        Xg, Og, xk, ok = X[rd], O[rd], "X%d" % rd, OK[rd]
         sm = lambda i: sml(st, i, [h])
         su = lambda i: sul(st, i, [h])
-        ob = lambda a, b: T.OB[:, U, a - 128:b - 128] if a else T.OZ[:, U, :]
-        y = U % 6
+        y, p3, u2 = U % 6, U % 3, U % 2
+        lo = 6 * rd + 2 * s + h
+        li = lo - 2
+        Xg = lambda n: T.X0[:, 0:n] if rd == 0 else W(0, XO, XO + n)
+        xk, xd = (["X0"], ["X0d"]) if rd == 0 else (["W0x"], ["W0d"])
         dm = T.dum[:, 8 * h:8 * h + 8]
+        wI = T.wI[:, st, 8 * h:8 * h + 8]
         if s == 0:
             v, vk = (T.v0[:, 8 * h:8 * h + 8], "v0") if rd == 0 else (T.LV[:, h, 0:8], "LV/%d" % h)
             z, zk = (T.X0[:, 4096 + 128 * h:4224 + 128 * h], "X0d") if rd == 0 else (T.zr[:, 0, 128 * h:128 * h + 128], "zr0/%d" % h)
         else:
-            li = 6 * rd + 2 * (s - 1) + h
             v, vk, z, zk = T.LF[:, li, 0:8], k("LL"), T.LZ[:, li, :], k("LF")
         if s < 3:
-            ts(sm(0), v, 2048.0, A.is_ge, -2048.0, A.mult, 8, [vk], [k("s0")])
-            tt(sm(7), v, sm(0), A.add, 8, [vk, k("s0")], [k("wf")])
+            ts(wI, v, 2047, A.bitwise_and, None, None, 8, [vk], [k("w")])
         if s == 0:
-            cp(su(0), sm(7), 8, [k("wf")], [k("w")])
-            ow, iw, ik = Og[:, 2048:4096], T.i2k[:, 0:2048], ["i2a"]
+            cp(su(0), wI, 8, [k("w")], [k("w16")])
+            ow = (T.O0[:, 2048:4096] if rd == 0 else W(0, 0, XO)).indirect(su(0))
+            ok = OK[rd] + [k("w16")]
         else:
-            cp(su(0), v, 8, [vk], [k("w")])
-            ow, iw, ik, ok = Og[:, 0:4096], T.i2k[:, 0:4096], ["i2a", "i2k"], ok + ["O%dt" % rd]
-        p3, u2 = U % 3, U % 2
-        act(T.Pf[:, p3, :], ow.indirect(su(0)), F.Identity, 128, ok + [k("w")], ["Pf%d" % p3], ind=True, bias=-8192.0)
-        if pr["pS"]:
-            ts(T.P16[:, p3, :], T.Pf[:, p3, :], 8192.0, A.add, None, None, 128, ["Pf%d" % p3], ["P16%d" % p3])
+            ow = (T.O0 if rd == 0 else T.W1)[:, 0:4096].indirect(T.LN[:, li, 0:8])
+            ok = OK[rd] + ["O%dt" % rd, k("LN")]
+        act(T.Pf[:, p3, :], ow, F.Copy, 128, ok, ["Pf%d" % p3], ind=True)
+        if pr["pS"][s] == "1":
+            ts(T.P16[:, p3, :], T.Pf[:, p3, :], 2048.0, A.add, None, None, 128, ["Pf%d" % p3], ["P16%d" % p3])
         else:
-            vx(lambda: V.tensor_copy(T.P16[:, p3, :], ow.indirect(su(0))), 128, ok + [k("w")], ["P16%d" % p3], pr["ga"])
+            ts(T.P16[:, p3, :], ow, 2048.0, A.add, None, None, 128, ok, ["P16%d" % p3], kind="vg")
         ps, pn = bank()
         mm(ps[:, 0:128], [(z, T.dgb[:, rd, :])], 128, [zk, "dgb%d" % rd], [pn])
         act(T.zT[:, u2, :], ps[:, 0:128], F.Identity, 128, [pn], ["zT%d" % u2], bias=-C0)
-        for c in range(4):
-            n = chunk[0]
-            chunk[0] += 1
-            xb = n % 8
+        c0 = 0
+        for c, n in enumerate(pr["ch"][s]):
+            a, b = 256 * c0, 256 * (c0 + n)
+            xn = ["xg%d" % (8 * u2 + i) for i in range(c0, c0 + n)]
             ps, pk_ = bank()
-            win = Xg[:, 0:4096].indirect(T.P16[:, p3, 32 * c:32 * c + 32])
-            xo = T.xg[:, 512 * xb:512 * xb + 512]
-            if pr["vg"][s][4 * h + c] == "1":
-                vx(lambda xo=xo, win=win: V.tensor_copy(xo, win), 512, [xk, "P16%d" % p3], ["xg%d" % xb], pr["ga"])
+            win = Xg(4096).indirect(T.P16[:, p3, 16 * c0:16 * (c0 + n)])
+            xo = T.xg[:, 2048 * u2 + a:2048 * u2 + b]
+            if pr["vg"][s][5 * h + c] == "1":
+                cp(xo, win, b - a, xk + ["P16%d" % p3], xn, kind="vg")
             else:
-                act(xo, win, F.Copy, 512, [xk, "P16%d" % p3], ["xg%d" % xb], ind=True)
-            mm(ps[:], [(T.dgb[:, rd, :], xo), (T.zT[:, u2, :], T.E[:, 512 * c:512 * c + 512])], 512,
-               ["dgb%d" % rd, "xg%d" % xb, "zT%d" % u2] + EK, [pk_])
-            no, nk = T.near[:, 8 * u2 + 2 * c:8 * u2 + 2 * c + 2, :], "near%d/%d" % (u2, c)
-            if pr["sv"][s][4 * h + c] == "1":
-                act(T.lv[:, xb, :], ps[:], F.Identity, 512, [pk_], ["lv%d" % xb], bias=CB - C0)
-                ts(no, T.lv[:, xb, :], CB, A.is_equal, None, None, 512, ["lv%d" % xb], [nk], 0.5)
+                act(xo, win, F.Copy, b - a, xk + ["P16%d" % p3], xn, ind=True)
+            mm(ps[:, 0:b - a], [(T.dgb[:, rd, :], xo), (T.zT[:, u2, :], T.E[:, a:b])], b - a, ["dgb%d" % rd, "zT%d" % u2] + xn + EK, [pk_])
+            no, nk = T.near[:, 8 * u2 + c0:8 * u2 + c0 + n, :, 0:16], ["near%d" % (8 * u2 + i) for i in range(c0, c0 + n)]
+            if pr["sv"][s][5 * h + c] == "1":
+                j = chunk[0] % 4
+                chunk[0] += 1
+                act(T.lv[:, j, 0:b - a], ps[:, 0:b - a], F.Identity, b - a, [pk_], ["lv%d" % j], bias=CB - C0)
+                ts(no, T.lv[:, j, 0:b - a], CB, A.is_equal, None, None, b - a, ["lv%d" % j], nk, 0.5)
             else:
-                ts(no, ps[:], CF - C0, A.add, CF, A.is_equal, 512, [pk_], [nk])
+                ts(no, ps[:, 0:b - a], CF - C0, A.add, CF, A.is_equal, b - a, [pk_], nk)
+            c0 += n
         ps, pn = bank()
-        nt = pr["nt"]
-        for c in range(nt):
-            w_ = 8 // nt
-            mm(ps[:, 16 * w_ * c:16 * w_ * (c + 1)],
-               [(T.Z[:, 15 - a:143 - a], T.near[:, 8 * u2 + w_ * c:8 * u2 + w_ * (c + 1), 16 * a:16 * a + 16]) for a in range(16)], 16 * w_,
-               ["Z"] + ["near%d/%d" % (u2, c_) for c_ in range(4 * c // nt, 4 * (c + 1) // nt)], [pn])
-        scan(T.key[:, u2, :], T.d0T[:], ps[:, 0:128], A.add, A.max, 128, ["d0T", pn], ["key%d" % u2])
-        key, kk = T.key[:, u2, 15:128:16], "key%d" % u2
-        ts(sm(1), key, CF, A.add, CF - 64.0, A.subtract, 8, [kk], [k("q")])
+        for c in (0, 4):
+            mm(ps[:, 17 * c:17 * c + 68], [(T.Z[:, 15 - a:143 - a], T.near[:, 8 * u2 + c:8 * u2 + c + 4, a, :]) for a in range(16)], 68,
+               ["Z", "nearz"] + ["near%d" % (8 * u2 + i) for i in range(c, c + 4)], [pn])
+        for i in range(2):
+            scan(T.key[:, 2 * u2 + i, :], T.d0T[:, i, :], ps[:, 0:136], A.add, A.max, 136, ["d0T%d" % i, pn], ["key%d" % (2 * u2 + i)])
+        key, kk = T.key[:, 2 * u2, 16:136:17], "key%d" % (2 * u2)
+        tt(sm(2), key, T.key[:, 2 * u2 + 1, 16:136:17], A.subtract, 8, [kk, "key%d" % (2 * u2 + 1)], [k("xo")])
+        cp(su(1), sm(2), 8, [k("xo")], [k("nu")])
+        m, m1 = T.OM[:, U, 0:8], T.m1[:, U, :]
         if s == 0:
-            ts(sm(2), key, 64.0 * 34816 + 64.0, A.max, None, None, 8, [kk], [k("G")])
+            ts(m, key, M0, A.is_le, BIG, A.mult, 8, [kk, "OM"], [k("m")])
+            dead = (T.ident[:], m, k("m"))
         else:
-            tt(sm(2), key, T.LF[:, li, 8:16], A.max, 8, [kk, k("LL")], [k("G")])
-        tt(sm(3), sm(2), sm(1), A.subtract, 8, [k("G"), k("q")], [k("r")])
-        ts(su(1), sm(3), -48.0, A.min, 64.0, A.add, 8, [k("r")], [k("kl")])
-        vx(lambda: V.tensor_tensor(T.Pm[:, u2, :], T.eye[:, 0:32].indirect(su(1)), T.Pf[:, p3, :], A.mult), 128,
-           ["eye", k("kl"), "Pf%d" % p3], ["Pm%d" % u2], pr["ga"])
-        if pr["mS"]:
-            act(ob(144, 152), sm(3), F.Relu, 8, [k("r")], [k("m")], bias=BIG, scale=BIG / 32)
-        else:
-            ts(ob(144, 152), sm(3), 0.0, A.is_ge, BIG, A.mult, 8, [k("r")], [k("m")])
-        ps, pn = bank()
-        mm(ps[:, 0:128], [(T.ident[:], T.offd[:]), (T.BO[:], T.Pm[:, u2, :])], 128, ["BO", "Pm%d" % u2, "ident", "offd"], [pn], 5)
-        scan(T.nvs[:, u2, :], T.d0N[:, 0:128], ps[:, 0:128], A.add, A.max, 128, ["d0N", pn], ["nvs%d" % u2])
-        ps, pn = bank()
-        mm(ps[:, 0:128], [(T.BO[:], T.Pm[:, u2, :])], 128, ["BO", "Pm%d" % u2], [pn], 4)
-        if pr["eS"][2 * s + h] < 8:
-            ts(T.nvr[:, y, :], ps[:, 0:128], 8192.0, A.add, None, None, 128, [pn], ["nvr%d" % y])
-        if pr["eS"][2 * s + h] > 0:
-            if pr["eS"][2 * s + h] < 8:
-                ps, pn = bank()
-                mm(ps[:, 0:128], [(T.BO[:], T.Pm[:, u2, :])], 128, ["BO", "Pm%d" % u2], [pn], 4)
-            act(T.nvf[:, y, :], ps[:, 0:128], F.Identity, 128, [pn], ["nvf%d" % y], bias=8192.0)
-        nvd = sm(9)
-        tt(nvd, T.nvs[:, u2, 15:128:16], dm, A.min, 8, ["nvs%d" % u2, "dum"], [k("nv")])
-        if s == 0:
-            cp(T.sq[:, 2 * rd + h, :], nvd, 8, [k("nv")], [k("n0")])
-            act(T.zq[:, h, :], Xg[:, 0:4352].indirect(T.sq[:, 2 * rd + h, :]), F.Copy, 128, [xk, xk + "d", k("n0")], ["zq%d" % h], ind=True)
+            tt(m1, T.LF[:, li, 8:16], key, A.is_ge, 8, [kk, k("LL")], [k("m1")])
+            dead = (T.idB[:], m1, k("m1"))
+            if pr["mV"][s] == "1":
+                ts(m, m1, BIG, A.mult, None, None, 8, [k("m1"), "OM"], [k("m")])
+            else:
+                act(m, m1, F.Copy, 8, [k("m1"), "OM"], [k("m")], scale=BIG)
+        act(sm(4), dead[1], F.Identity, 8, [dead[2]], [k("gb")], bias=BIG, scale=-1.0 if s == 0 else -BIG)
+        back = (-1, T.OM[:, U, :], T.LB[:, li, :], "b%d" % U, "LB/%d" % (U - 2))
         if s == 3:
-            cp(su(2), nvd, 8, [k("nv")], [k("nu")])
-            zw, zwk = Xg[:, 0:4352], [xk, xk + "d", k("nu")]
-        else:
-            tt(sm(8), T.cx[:], sm(3), A.subtract, 8, ["cx", k("r")], [k("xo")])
-            cp(su(2), sm(8), 8, [k("xo")], [k("nu")])
-            zw, zwk = T.xg[:, 2048 * u2:2048 * u2 + 2048], ["xg%d" % (4 * u2 + c) for c in range(4)] + [k("nu")]
+            send([back], [k("m")])
+        zw, zwk = T.xg[:, 2048 * u2:2048 * u2 + 2048].indirect(su(1)), ["xg%d" % (8 * u2 + c) for c in range(8)] + [k("nu")]
+        pv, pvk = W(rd, ST + 128 * y, ST + 128 * y + 128), "W%ds%d" % (rd, y)
         if s < 3:
-            act(ob(0, 128), zw.indirect(su(2)), F.Copy, 128, zwk, [k("nz")], ind=True)
-            act(T.pv[:, y, :], ob(0, 128), F.Relu, 128, [k("nz")], ["pv%d" % y], bias=-37.0)
+            if pr["zV"][2 * s + h] == "1":
+                cp(T.OZ[:, lo, :], zw, 128, zwk, [k("nz")], kind="vg")
+            else:
+                act(T.OZ[:, lo, :], zw, F.Copy, 128, zwk, [k("nz")], ind=True)
+            send([(1, T.OZ[:, lo, :], T.LZ[:, lo, :], "t%d" % U, "LF/%d" % (U + 2))], [k("nz")])
+            act(pv, T.OZ[:, lo, :], F.Relu, 128, [k("nz")], [pvk], bias=-37.0)
         else:
-            act(T.pv[:, y, :], zw.indirect(su(2)), F.Relu, 128, zwk, ["pv%d" % y], bias=-37.0, ind=True)
-        if pr["gS"]:
-            act(sm(4), sm(3), F.Relu, 8, [k("r")], [k("gb")], bias=-16 * BIG, scale=-BIG / 2)
-        else:
-            ts(sm(4), sm(3), 0.0, A.is_lt, BIG, A.mult, 8, [k("r")], [k("gb")])
+            act(pv, zw, F.Relu, 128, zwk, [pvk], bias=-37.0, ind=True)
+        tt(T.Pm[:, u2, :], T.eye[:].indirect(su(1)), T.Pf[:, p3, :], A.mult, 128, EYE + [k("nu"), "Pf%d" % p3], ["Pm%d" % u2], 1.0, "vg")
+        ps, pn = bank()
+        mm(ps[:, 0:8], [(T.Z1[:, 15 - a:143 - a], T.Pm[:, u2, a:128:16]) for a in range(16)] + [(T.ident[:], T.half[:, 128:136]), dead[0:2]], 8,
+           ["Z1", "Pm%d" % u2, "ident", "idB", "c4k", dead[2]], [pn])
+        nv = ps[:, 0:8]
+        if s < 3:
+            ts(T.ON[:, lo, :], nv, -2048.0, A.add, 4095.0, A.min, 8, [pn], [k("n16")])
+            send([(1, T.ON[:, lo, :], T.LN[:, lo, :], "n%d" % U, "LN/%d" % (U + 2))], [k("n16")])
         if s == 0:
-            vi_ = 4 * rd + 2 * h
-            tt(T.vri[:, vi_, :], v, T.US[:, rd, 8 * h:8 * h + 8], A.add, 8, [vk, "US%d" % rd], [k("vr0")])
-            ts(T.vri[:, vi_ + 1, :], T.vri[:, vi_, :], 4095, A.bitwise_and, None, None, 8, [k("vr0")], [k("vr")])
-            tt(sm(5), T.vri[:, vi_ + 1, :], sm(4), A.add, 8, [k("vr"), k("gb")], [k("t")])
+            vr = lambda i: T.vr[:, 6 * rd + 3 * h + i, :]
+            tt(vr(0), v, T.ui[:, 2 * rd + 1, 8 * h:8 * h + 8], A.add, 8, [vk, "uj%d" % rd], [k("vr0")])
+            ts(vr(1), vr(0), 4095, A.bitwise_and, None, None, 8, [k("vr0")], [k("vr1")])
+            ts(vr(2), vr(1), 2048.0, A.add, None, None, 8, [k("vr1")], [k("vr")])
+            tt(sm(5), vr(2), sm(4), A.add, 8, [k("vr"), k("gb")], [k("t")])
         else:
             tt(sm(5), v, sm(4), A.add, 8, [vk, k("gb")], [k("t")])
-        tt(ob(128, 136), T.nvs[:, u2, 15:128:16], sm(5), A.min, 8, ["nvs%d" % u2, k("t")], [k("v")])
-        tt(ob(136, 144), sm(1), ob(144, 152), A.max, 8, [k("q"), k("m")], [k("M")])
-        if s > 0:
-            tt(ob(152, 160), dm, sm(4), A.min, 8, ["dum", k("gb")], [k("fb")])
-            back = (-1, ob(144, 160), T.LB[:, li, :], "b%d" % U, "LB/%d" % (U - 2))
+        tt(T.OB[:, U, 0:8], nv, sm(5), A.min, 8, [pn, k("t")], [k("v")])
+        tt(T.OB[:, U, 8:16], key, m, A.max, 8, [kk, k("m")], [k("M")])
         if s < 3:
-            lo = 6 * rd + 2 * s + h
-            on = (1, ob(128, 144), T.LF[:, lo, :], "f%d" % U, "LL/%d" % (U + 2))
-            send([on, back] if s > 0 else [on], [k("v"), k("M")] + ([k("m"), k("fb")] if s > 0 else []))
-            send([(1, ob(0, 128), T.LZ[:, lo, :], "t%d" % U, "LF/%d" % (U + 2))], [k("nz")])
+            tt(sm(6), nv, dm, A.min, 8, [pn, "dum"], [k("nv")])
+            on = (1, T.OB[:, U, :], T.LF[:, lo, :], "f%d" % U, "LL/%d" % (U + 2))
+            send([on, back] if s > 0 else [on], [k("v"), k("M"), k("m")])
         else:
-            send([(1, ob(128, 144), T.LV[:, 2 * rd + h, :], "f%d" % U, "LV/%d" % (2 * rd + h)), back], [k("v"), k("M"), k("m"), k("fb")])
+            tt(keys(st, [h]), nv, dm, A.min, 8, [pn, "dum"], [DK[slot(st, h)]])
+            send([(1, T.OB[:, U, :], T.LV[:, 2 * rd + h, :], "f%d" % U, "LV/%d" % (2 * rd + h))], [k("v"), k("M")])
         if s == 0:
-            tt(T.zs[:, h, :], z, T.zq[:, h, :], A.add, 128, [zk, "zq%d" % h], ["zs%d" % h])
-            ts(T.zs[:, h, :], T.zs[:, h, :], -0.5, A.add, C2, A.add, 128, ["zs%d" % h], ["zs%d" % h])
+            ts(su(5), sm(6), -2048.0, A.add, None, None, 8, [k("nv")], [k("n0")])
+            act(T.zq[:, h, :], Xg(4352).indirect(su(5)), F.Copy, 128, xk + xd + [k("n0")], ["zq%d" % h], ind=True)
+            ps, pn = bank()
+            mm(ps[:, 0:128], [(T.ident[:], z), (T.ident[:], T.zq[:, h, :]), (T.ident[:], T.half[:, 0:128])], 128, [zk, "zq%d" % h, "ident", "half"], [pn])
+            act(T.zs[:, h, :], ps[:, 0:128], F.Identity, 128, [pn], ["zs%d" % h], bias=C2)
             act(T.zr[:, rd, 128 * h:128 * h + 128], T.zs[:, h, :], F.Identity, 128, ["zs%d" % h], ["zr%d/%d" % (rd, h)], bias=-C2 / 2, scale=0.5)
+
+    edits = [0]
+
+    def edit(rd, s, hs):
+        st = 4 * rd + s
+        K = lambda n: ks(n, st, hs)
+        sm = lambda i: sml(st, i, hs)
+        su = lambda i: sul(st, i, hs)
+        n = len(hs)
+        dk = [DK[slot(st, h)] for h in hs]
+        y0 = (2 * st + hs[0]) % 6
+        wk = ["W%do" % rd, "W%dx" % rd, "W%dd" % rd]
         if s < 3:
-            lift[0] = pr["lift"]
-            if pr["wS"]:
-                act(T.wf[:, u2, :], iw.indirect(su(0)), F.Copy, 128, ik + [k("w")], ["wf%d" % u2], ind=True)
-                cp(T.wr[:, u2, :], T.wf[:, u2, :], 128, ["wf%d" % u2], ["wr%d" % u2])
+            li = 6 * rd + 2 * s
+            fb = T.LB[:, li + hs[0], 0:8] if n == 1 else T.LB[:, li:li + 2, 0:8]
+            tt(sm(7), T.wI[:, st, 8 * hs[0]:8 * hs[-1] + 8], fb, A.add, 8, K("w") + K("LB"), K("wm"))
+            tt(keys(st, hs), sm(7), sm(6), A.min, 8, K("wm") + K("nv"), dk)
+            tt(sm(8), sm(7), T.stg[:, 8 * y0:8 * y0 + 8 * n], A.min, 8, K("wm") + ["stg"], K("go"))
+            cp(su(3), sm(8), 8, K("go"), K("g16"))
+            tt(sm(9), sm(2), fb, A.add, 8, K("xo") + K("LB"), K("kx"))
+        cp(su(2), keys(st, hs), 8, dk, K("k16"))
+        ps, pn = bank()
+        es = []
+        for h in hs:
+            e = edits[0] % 4
+            edits[0] += 1
+            es.append(e)
+            row = T.i2k[:].indirect(sul(st, 2, [h]))
+            if pr["kS"][2 * s + h] == "1":
+                act(T.kf[:, e % 2, :], row, F.Copy, 128, IK + ks("k16", st, [h]), ["kf%d" % (e % 2)], ind=True)
+                cp(T.kr[:, e, :], T.kf[:, e % 2, :], 128, ["kf%d" % (e % 2)], ["kr%d" % e])
             else:
-                vx(lambda: V.tensor_copy(T.wr[:, u2, :], iw.indirect(su(0))), 128, ik + [k("w")], ["wr%d" % u2], pr["ga"])
+                cp(T.kr[:, e, :], row, 128, IK + ks("k16", st, [h]), ["kr%d" % e], kind="vg")
             for b in range(8):
-                ts(T.eqe[:, 8 * y + b, :], T.wr[:, u2, :], T.sm[:, NS * st + 7, 8 * h + b:8 * h + b + 1], A.is_equal, None, None, 128,
-                   ["wr%d" % u2, k("wf")], ["eqe%d/%d" % (y, b)], 0.5)
-            if h == 1:
-                ek = lambda h_: (8 * ((2 * st + h_) % 6), ["eqe%d/%d" % ((2 * st + h_) % 6, b) for b in range(8)])
-                first(st, [0, 1], 0, T.eqe, ek, 7, "wf", 16, "oe")
-            lift[0] = 0.0
-
-    def landed(rd, s, hs, a):
-        li = 6 * rd + 2 * s
-        return T.LB[:, li + hs[0], a:a + 8] if len(hs) == 1 else T.LB[:, li:li + 2, a:a + 8]
-
-    def penalty(rd, s, hs):
-        st = 4 * rd + s
-        ki, kn = 9, "nv"
-        e4 = lambda h: (2 * st + h) % 4
-        if s < 3:
-            tt(sml(st, 16, hs), sml(st, 9, hs), landed(rd, s, hs, 8), A.max, 8, ks("nv", st, hs) + ks("LB", st, hs), ks("pk", st, hs))
-            ki, kn = 16, "pk"
-        for h in hs:
-            y = (2 * st + h) % 6
-            for b in range(pr["eS"][2 * s + h]):
-                kc, ab = T.sm[:, NS * st + ki, 8 * h + b:8 * h + b + 1], T.ab[:, b % 4, :]
-                act(ab, T.nvf[:, y, :], F.Abs, 128, ["nvf%d" % y] + ks(kn, st, [h]), ["ab%d" % (b % 4)], bias=kc, scale=-1.0)
-                act(T.eqp[:, 8 * e4(h) + b, :], ab, F.Relu, 128, ["ab%d" % (b % 4)], ["eqp%d/%d" % (e4(h), b)], bias=1.0, scale=-1.0)
-            for b in range(pr["eS"][2 * s + h], 8):
-                ts(T.eqp[:, 8 * e4(h) + b, :], T.nvr[:, y, :], T.sm[:, NS * st + ki, 8 * h + b:8 * h + b + 1], A.is_equal, None, None, 128,
-                   ["nvr%d" % y] + ks(kn, st, [h]), ["eqp%d/%d" % (e4(h), b)], 0.5)
-        first(st, hs, 1, T.eqp, lambda h: (8 * e4(h), ["eqp%d/%d" % (e4(h), b) for b in range(8)]), ki, kn, 0, "op")
-        wk = "X%d" % (rd + 1)
-        for h in hs:
-            y = (2 * st + h) % 6
-            vx(lambda h=h, y=y: V.tensor_copy(X[rd + 1][:, 0:4352].indirect(sul(st, 4, [h])), T.pv[:, y, :]), 128,
-               ks("op", st, [h]) + ["pv%d" % y], [wk, wk + "d"], pr["sc"])
-
-    def exonerate(rd, s, hs):
-        st = 4 * rd + s
-        tt(sml(st, 6, hs), sml(st, 3, hs), landed(rd, s, hs, 0), A.add, 8, ks("r", st, hs) + ks("LB", st, hs), ks("kx", st, hs))
-        uk = "US%d" % rd if s == 0 else "LU/%d" % (2 * rd + s - 1)
-        wk, W = "O%d" % (rd + 1), O[rd + 1]
-        for h in hs:
-            y = (2 * st + h) % 6
+                c = 136 * slot(st, h) + 17 * b + 16
+                ts(T.eq[:, 8 * e + b, :, 0:16], T.kr[:, e, :], T.D[:, c:c + 1], A.is_equal, None, None, 128,
+                   ["kr%d" % e, DK[slot(st, h)]], [EQ[8 * e + b]], 0.5)
+        for i, e in enumerate(es):
+            mm(ps[:, 136 * i:136 * i + 136], [(T.Wl[:, b, :], T.eq[:, 8 * e + b, :, :]) for b in range(8)] + [(T.ident[:], T.thr[:])], 136,
+               WL + EQ[8 * e:8 * e + 8] + ["eqz", "ident", "thr"], [pn])
+        yi = es[0] % 2
+        d0 = 136 * slot(st, hs[0])
+        scan(T.yo[:, yi, 0:136 * n], T.D[:, d0:d0 + 136 * n], ps[:, 0:136 * n], A.max, A.min, 136 * n, dk + [pn], ["yo%d" % yi])
+        cp(su(4), T.yo[:, yi, 16:136 * n:17], 8, ["yo%d" % yi], K("off"))
+        for h, e in zip(hs, es):
+            y, j = (2 * st + h) % 6, e % 2
+            out, ok = W(rd, 0, ST).indirect(sul(st, 4, [h])), ks("off", st, [h])
+            if s == 3:
+                cp(out, W(rd, ST + 128 * y, ST + 128 * y + 128), 128, ok + ["W%ds%d" % (rd, y)], wk, kind="vs")
+                continue
+            uk = "US%d" % rd if s == 0 else "LU/%d" % (2 * rd + s - 1)
             for b in range(8):
                 c = 8 * h + b
                 u = T.US[:, rd, c:c + 1] if s == 0 else T.LU[:, 2 * rd + s - 1, c:c + 1]
-                ts(T.lh[:, c, :], T.iK[:], T.sm[:, NS * st + 6, c:c + 1], A.is_equal, u, A.mult, 128, ["iK", uk] + ks("kx", st, [h]), ["lh%d" % c], 0.5)
-            off, oe = sul(st, 3, [h]), ks("oe", st, [h])
-            act(T.cs[:, h, :], W[:, 2048:4352].indirect(off), F.Copy, 128, [wk, wk + "d"] + oe, ["cs%d" % h], ind=True)
+                ts(T.lh[:, 8 * j + b, :], T.iK[:, b, :], T.sm[:, NS * st + 9, c:c + 1], A.is_equal, u, A.mult, 128,
+                   ["iK%d" % b, uk] + ks("kx", st, [h]), ["lh%d" % (8 * j + b)], 0.5)
+            act(T.cs[:, j, :], W(rd, 0, ST + 128 * y + 128).indirect(sul(st, 3, [h])), F.Identity, 128,
+                wk + ["W%ds%d" % (rd, i) for i in range(y + 1)] + ks("g16", st, [h]), ["cs%d" % j], ind=True, bias=0.5)
             ps, pn = bank()
-            mm(ps[:, 0:128], [(T.lh[:, 8 * h + b, :], T.eqe[:, 8 * y + b, :]) for b in range(8)], 128,
-               ["lh%d" % (8 * h + b) for b in range(8)] + ["eqe%d/%d" % (y, b) for b in range(8)] + oe, [pn])
-            tt(T.nw[:, 2 * h, :], ps[:, 0:128], T.cs[:, h, :], A.add, 128, [pn, "cs%d" % h], ["nw%d" % h], 1.0)
-            ts(T.nw[:, 2 * h + 1, :], T.nw[:, 2 * h, :], 4095, A.bitwise_and, None, None, 128, ["nw%d" % h], ["nx%d" % h])
-            vx(lambda h=h, off=off: V.tensor_copy(W[:, 2048:4352].indirect(off), T.nw[:, 2 * h + 1, :]), 128, oe + ["nx%d" % h], [wk, wk + "d"], pr["sc"])
+            mm(ps[:, 0:128], [(T.lh[:, 8 * j + b, :], T.eq[:, 8 * e + b, :, 0:16]) for b in range(8)], 128,
+               ["lh%d" % (8 * j + b) for b in range(8)] + EQ[8 * e:8 * e + 8], [pn], last=False)
+            mm(ps[:, 0:128], [(T.identF[:], T.cs[:, j, :])], 128, ["identF", "cs%d" % j], [pn], 4, first=False)
+            if pr["hS"][2 * s + h] == "2":
+                ts(T.ys[:, j, :], ps[:, 0:128], -0.5, A.add, None, None, 128, [pn], ["ys%d" % j])
+            else:
+                act(T.ys[:, j, :], ps[:, 0:128], F.Identity, 128, [pn], ["ys%d" % j, pn], bias=-0.5)
+            if pr["hS"][2 * s + h] == "1":
+                act(T.kf[:, 2 + j, :], ps[:, 0:128], F.Identity, 128, [pn], ["hp%d" % j], bias=CM)
+                act(T.hs[:, j, :], T.kf[:, 2 + j, :], F.Identity, 128, ["hp%d" % j], ["hs%d" % j], bias=-CM)
+            else:
+                ts(T.hs[:, j, :], ps[:, 0:128], CM, A.add, CM, A.subtract, 128, [pn], ["hs%d" % j])
+            if s == 2:
+                edit(rd, 3, [h])
+            tt(out, T.ys[:, j, :], T.hs[:, j, :], A.subtract, 128, ok + ["ys%d" % j, "hs%d" % j], wk, 1.0, "vs")
 
     def code(rd):
         zk = ["X0d"] if rd == 0 else ["zr0/0", "zr0/1"]
@@ -464,17 +464,16 @@ def make_ops(g, core, T, topo, rank, banks):
 
     def nearness():
         ts(T.cnt[:, 0:48], T.LF[:, 0:6, 8:16], BIG, A.is_lt, None, None, 48, ["LL/%d" % U for U in range(2, 8)], ["cnt0"])
-        ts(T.cnt[:, 48:96], T.OB[:, 0:6, 16:24], 1.0, A.is_lt, -1.0, A.mult, 48, ["m/%d" % U for U in range(6)], ["cnt1"])
-        ms(T.ta[:, 9, 0:96], -1e6, 96, ["ta9"])
-        scan(T.ta[:, 0, 0:96], T.cnt[:], T.ta[:, 9, 0:96], A.add, A.max, 96, ["cnt0", "cnt1", "ta9"], ["ta0"])
+        ts(T.cnt[:, 48:96], T.OM[:, 0:6, 0:8], 1.0, A.is_lt, -1.0, A.mult, 48, ["m/%d" % U for U in range(6)], ["cnt1"])
+        op("V", lambda: [V.tensor_reduce(col(10), T.cnt[:], AxisListType.X, A.add)], ("v", 96), ["cnt0", "cnt1"], ["c10"])
         ps, pn = bank()
-        mm(ps[:, 0:2], [(T.BO[:], T.ta[:, 0, 94:96])], 2, ["BO", "ta0"], [pn], 4)
-        cp(T.coli[:, 8:9], ps[:, 1:2], 1, [pn], ["A0"])
+        mm(ps[:, 0:2], [(T.BO[:], T.col[:, 9:11])], 2, ["BO", "c9", "c10"], [pn], 4)
+        ts(T.coli[:, 8:9], ps[:, 1:2], 1024.0, A.add, None, None, 1, [pn], ["A0"])
         ts(T.coli[:, 12:13], T.coli[:, 8:9], 3, A.bitwise_and, None, None, 1, ["A0"], ["A1"])
         ts(col(12), T.coli[:, 12:13], 2.0 / 64, A.mult, 49.0 / 64, A.add, 1, ["A1"], ["A2"])
-        op("V", lambda: [V.reciprocal(col(16), col(12))], 250.0, ["A2"], ["A3"])
+        op("V", lambda: [V.reciprocal(col(16), col(12))], ("v", 250), ["A2"], ["A3"])
         cp(T.colb[:, 0:1], col(16), 1, ["A3"], ["A4"])
-        cp(col(20), T.colb[:, 0:1], 1, ["A4"], ["A5"])
+        act(col(20), T.colb[:, 0:1], F.Copy, 1, ["A4"], ["A5"])
         act(T.dgb[:, 1, :], T.ident[:], F.Copy, 128, ["ident", "A5"], ["dgb1"], scale=col(20))
 
     code(0)
@@ -484,32 +483,32 @@ def make_ops(g, core, T, topo, rank, banks):
                 ahead[0] = pr["ahead"][s] * (1 - h)
                 station(rd, s, h)
                 ahead[0] = 0.0
+                if s == 0 and h == 0:
+                    if rd == 0:
+                        dma(W(0, 0, XO), T.O0[:, 2048:4096], 1048576, OK[0] + ["O0t"], ["W0o"])
+                        dma(W(0, XO, SP), T.tracks[:], 2097152, ["LN/2"], ["W0x"], True)
+                    else:
+                        dma(W(1, XO, SP), W(0, XO, SP), 2097152, ["W0x", "LN/10"], ["W1x"])
                 lift[0] = pr["lift"]
-                if s == 3:
-                    penalty(rd, 3, [h])
                 if s > 0 and (s > pr["both"] or h == 1):
-                    hs = [h] if s > pr["both"] else [0, 1]
-                    penalty(rd, s - 1, hs)
-                    lift[0] = pr["lift"] + (pr["last"] if rd == 1 and s == 3 else 0.0)
-                    exonerate(rd, s - 1, hs)
+                    edit(rd, s - 1, [h] if s > pr["both"] else [0, 1])
                 lift[0] = 0.0
             if rd == 0 and s == 0:
                 code(1)
         if rd == 0:
             nearness()
-            act(T.X1[:, 4096:4352], T.zr[:, 0, :], F.Copy, 256, ["zr0/0", "zr0/1"], ["X1d"])
-            dma(T.X2[:, 0:4096], T.X1[:, 0:4096], 1048576, ["X1"], ["X2"])
-            dma(T.O1[:, 0:2048], T.O1[:, 2048:4096], 1048576, ["O1"], ["O1t"])
-            dma(T.O2[:, 2048:4096], T.O1[:, 2048:4096], 1048576, ["O1"], ["O2"])
+            act(W(0, SP, ST), T.zr[:, 0, :], F.Copy, 256, ["zr0/0", "zr0/1"], ["W0d"])
+            dma(T.W1[:, 0:2048], W(0, 0, XO), 1048576, ["W0o"], ["O1t"])
+            dma(W(1, 0, XO), W(0, 0, XO), 1048576, ["W0o", "O1t"], ["W1o"])
     dma(T.yz[:], T.zr[:, 1, :], 65536, ["zr1/0", "zr1/1"], ["yz"])
-    for h in range(2):
-        dma(T.yv[:, 8 * h:8 * h + 8], T.LV[:, 2 + h, 0:8], 30000, ["LV/%d" % (2 + h)], ["yv%d" % h])
-    dma(T.yx[:], T.X2[:, 0:4096], 1048576, ["X2"], ["yx"])
-    for c in range(2):
+    ts(T.vf[:], T.LV[:, 2:4, 0:8], -2048.0, A.add, None, None, 16, ["LV/2", "LV/3"], ["vf"])
+    dma(T.yv[:], T.vf[:], 30000, ["vf"], ["yv"])
+    dma(T.yx[:], W(1, XO, SP), 1048576, ["W1x"], ["yx"], True)
+    for c in range(4):
         ps, pk_ = bank()
-        act(ps[:], T.O2[:, 3072 + 512 * c:3584 + 512 * c], F.Copy, 512, ["O2"], [pk_], scale=4096.0)
-        tt(T.pk[:, 512 * c:512 * c + 512], ps[:], T.O2[:, 2048 + 512 * c:2560 + 512 * c], A.add, 512, [pk_, "O2"], ["pk%d" % c], 1.0)
-        dma(T.yn[:, 512 * c:512 * c + 512], T.pk[:, 512 * c:512 * c + 512], 262144, ["pk%d" % c], ["yn%d" % c])
+        act(ps[:, 0:256], W(1, 1024 + 256 * c, 1280 + 256 * c), F.Identity, 256, ["W1o"], [pk_], scale=4096.0, bias=2048.0 * 4097)
+        tt(T.pk[:, 256 * c:256 * c + 256], ps[:, 0:256], W(1, 256 * c, 256 * c + 256), A.add, 256, [pk_, "W1o"], ["pk%d" % c], 1.0)
+        dma(T.yn[:, 256 * c:256 * c + 256], T.pk[:, 256 * c:256 * c + 256], 131072, ["pk%d" % c], ["yn%d" % c])
     return ops
 
 
@@ -538,24 +537,66 @@ def depend(ops, order, banks):
 
 
 def queue(o):
-    return "G" if o["e"] == "R" else o["e"]
+    return "G" if o["e"] in "RC" else o["e"]
 
 
-def after(o):
-    return PARAM["rem"] if o["e"] == "R" else (2000.0 if o["e"] == "Y" else PARAM["lat"])
+def cost(o, pr):
+    kind, n = o["k"]
+    cyc = pr["cyc"]
+    held = {"v": max(64.0, n) * cyc, "s": max(64.0, n) * cyc + 30.0, "vg": 55.0 + n * pr["ga"] * cyc, "sg": 70.0 + n * pr["ga"] * cyc,
+            "vs": 55.0 + n * pr["sc"] * cyc, "p": n * pr["pe"] + 30.0, "g": 140.0 + 2 * n * cyc, "y": n / pr["bw"], "c": 1000.0, "r": pr["iss"]}[kind]
+    return held, {"r": pr["rem"] + 320.0 * (n - 2), "y": pr["dma"], "c": pr["dma"] + n / pr["bw"]}.get(kind, pr["lat"])
 
 
 def arrange(ops, deps):
     n = len(ops)
     way = [0.0] * n
     succ = [set() for _ in range(n)]
+    cs = [cost(o, PARAM) for o in ops]
     for i in range(n):
         for j, _x in deps[i]:
             succ[j].add(i)
     for i in range(n - 1, -1, -1):
-        way[i] = ops[i]["c"] + after(ops[i]) + max([way[j] for j in succ[i]] + [0.0])
+        way[i] = sum(cs[i]) + max([way[j] for j in succ[i]] + [0.0])
     rank_ = [way[i] + (ops[i]["lift"] or ops[i]["first"]) for i in range(n)]
-    rank_ = [x + PARAM["tie"] * ((i * 7919 + PARAM["mix"]) * (i + PARAM["mix"]) % 1009) / 1009.0 for i, x in enumerate(rank_)]
+    best = sweep(ops, deps, succ, cs, rank_)
+    now = best
+    for _ in range(PARAM["turns"]):
+        late = backward(ops, deps, succ, cs, now[3])
+        rank_ = [late[i] + PARAM["keep"] * (ops[i]["lift"] or ops[i]["first"]) for i in range(n)]
+        now = sweep(ops, deps, succ, cs, rank_)
+        if now[2] < best[2]:
+            best = now
+    return best[0:3]
+
+
+def backward(ops, deps, succ, cs, done):
+    n = len(ops)
+    left = [len(succ[i]) for i in range(n)]
+    ready = [cs[i][1] for i in range(n)]
+    free = {q: 0.0 for q in "VSPGY"}
+    pool = [i for i in range(n) if left[i] == 0]
+    late = [0.0] * n
+    while pool:
+        best = min(pool, key=lambda i: (max(ready[i], free[queue(ops[i])]), -done[i]))
+        q = queue(ops[best])
+        soon = max(ready[best], free[q]) + PARAM["back"] * cs[best][0]
+        for i in pool:
+            if queue(ops[i]) == q and done[i] > done[best] and max(ready[i], free[q]) < soon:
+                best = i
+        pool.remove(best)
+        late[best] = free[q] = max(ready[best], free[q]) + cs[best][0]
+        for j in set(j for j, _x in deps[best]):
+            ready[j] = max(ready[j], late[best] + cs[j][1])
+            left[j] -= 1
+            if left[j] == 0:
+                pool.append(j)
+    return late
+
+
+def sweep(ops, deps, succ, cs, rank_):
+    n = len(ops)
+    ends = [0.0] * n
     left = [len(set(j for j, _x in deps[i])) for i in range(n)]
     ready = [0.0] * n
     free = {q: 0.0 for q in "VSPGY"}
@@ -577,7 +618,7 @@ def arrange(ops, deps):
     while pool:
         best = min(pool, key=lambda i: (start(i), -rank_[i]))
         q = queue(ops[best])
-        soon = start(best) + PARAM["hold" + (q if q in "PS" else "")] * ops[best]["c"]
+        soon = start(best) + PARAM["hold" + (q if q in "PS" else "")] * cs[best][0]
         assert soon < 1e17
         for i in pool:
             if queue(ops[i]) == q and rank_[i] > rank_[best] and start(i) < soon:
@@ -585,9 +626,9 @@ def arrange(ops, deps):
         t0 = start(best)
         pool.remove(best)
         order.append(best)
-        free[q] = t0 + ops[best]["c"]
-        done = free[q] + after(ops[best])
-        ops[best]["t"] = t0
+        free[q] = t0 + cs[best][0]
+        done = free[q] + cs[best][1]
+        ends[best] = done
         x = use[best]
         if x is not None:
             if x not in banks:
@@ -602,7 +643,7 @@ def arrange(ops, deps):
             left[j] -= 1
             if left[j] == 0:
                 pool.append(j)
-    return order, banks, end
+    return order, banks, end, ends
 
 
 def rank_program(g, core, T, topo):
@@ -643,7 +684,7 @@ def rank_program(g, core, T, topo):
             for sem, val in o["sems"].values():
                 count[sem] = val
                 count["sent"] = count.get("sent", 0) + val
-        elif o["e"] == "Y":
+        elif o["e"] in "YC":
             made[0].then_inc(T.sem[o["sems"][""]], 16)
             count[o["sems"][""]] = 16
             mark[i] = (o["sems"][""], 16, dict(known[q]))

from concourse.bass import DstId, RemoteDMATransfer
from concourse.mybir import AluOpType as A, AxisListType, ActivationFunctionType as F

BIG = float(2 ** 23)
CF = float(3 * 2 ** 28)
CB = float(3 * 2 ** 12)
C2 = float(3 * 2 ** 23)
CM = float(3 * 2 ** 34)
C0 = 192.0
S0 = 1.3046875
M0 = 64.0 * 34816
XO, SP, ST, WN = 2048, 6144, 6400, 7168
PARAM = {"sv": ("00000000", "00000000", "00000000", "00000000"), "vg": ("00000000", "00000000", "00000000", "00000000"),
         "kS": "00000000", "hS": "00000000", "pS": "0000", "both": 0, "hold": 0.2, "holdP": 0.5, "holdS": 0.3, "lift": 1.0, "spare": 2, "nt": 2,
         "ahead": (2000.0, 2000.0, 2000.0, 1000.0),
         "cyc": 0.9, "pe": 0.45, "ga": 1.56, "sc": 3.8, "lat": 200.0, "rem": 1800.0, "bw": 250.0, "dma": 1800.0, "iss": 600.0}
PARAM.update({'sv': ('0000000000', '0000000000', '1000010000', '1000011000'), 'vg': ('1000001000', '1000010000', '0000000000', '0000000100'),
              'kS': '01001101', 'ch': ((2, 2, 2, 1, 1),) * 4, 'mV': '0001', 'zV': '000000',
              'hS': '00010010', 'holdS': 0.6, 'spare': 0, 'ahead': (1000.0, 4000.0, 1000.0, 0.0), 'lat': 150.0})
PARAM.update({'sv': ('0011010000', '0000000000', '1000010100', '1001011100'), 'vg': ('1000101000', '1000010010', '0000100000', '0001000100'), 'kS': '00001101', 'hS': '20010010', 'pS': '0000', 'both': 0, 'hold': 0.5, 'holdP': 0.5, 'holdS': 0.6, 'lift': 1.0, 'spare': 1, 'nt': 2, 'ahead': (1000.0, 2000.0, 3000.0, 0.0), 'cyc': 0.83, 'lat': 200.0, 'rem': 2000.0, 'ch': ((2, 2, 1, 2, 1), (2, 2, 2, 1, 1), (2, 2, 1, 2, 1), (2, 2, 2, 1, 1)), 'mV': '1000', 'zV': '100011'})
PARAM.update({'sv': ('0000000000', '0000001001', '1100111000', '1110011110'), 'vg': ('1000010000', '1000010000', '1000000001', '0000010000'), 'kS': '10111111', 'hS': '10110200', 'pS': '0000', 'both': 0, 'hold': 0.5, 'holdP': 0.5, 'holdS': 0.6, 'lift': 1.0, 'spare': 0, 'nt': 2, 'ahead': (2000.0, 2000.0, 4000.0, 0.0), 'cyc': 0.83, 'lat': 200.0, 'rem': 2000.0, 'ch': ((2, 2, 2, 1, 1), (2, 2, 1, 2, 1), (1, 1, 2, 2, 2), (2, 2, 1, 2, 1)), 'mV': '0000', 'zV': '001111', 'turns': 2, 'keep': 0.0, 'back': 0})
NS = 12

SCRATCH = {
    "X0": ("sbuf", [128, 4352], "bfloat16"), "O0": ("sbuf", [128, 4096], "float32"),
    "W1": ("sbuf", [128, 2048 + WN], "float32"), "W2": ("sbuf", [128, WN], "float32"),
    "nbi": ("sbuf", [128, 1024], "int32"), "nbt": ("sbuf", [128, 2048], "int32"), "pk": ("sbuf", [128, 1024], "float32"),
    "vi": ("sbuf", [128, 16], "int32"), "v0": ("sbuf", [128, 16], "int32"), "vf": ("sbuf", [128, 16], "float32"),
    "zr": ("sbuf", [128, 2, 256], "bfloat16"), "zs": ("sbuf", [128, 2, 128], "float32"),
    "LF": ("sbuf", [128, 12, 16], "int32"), "LB": ("sbuf", [128, 12, 32], "bfloat16"), "LV": ("sbuf", [128, 4, 16], "int32"),
    "LN": ("sbuf", [128, 12, 8], "uint16"), "ON": ("sbuf", [128, 12, 8], "uint16"), "m1": ("sbuf", [128, 16, 8], "bfloat16"),
    "idB": ("sbuf", [128, 128], "bfloat16"), "OM": ("sbuf", [128, 16, 32], "bfloat16"),
    "LU": ("sbuf", [128, 4, 16], "float32"), "US": ("sbuf", [128, 2, 16], "float32"), "OB": ("sbuf", [128, 16, 16], "int32"),
    "ui": ("sbuf", [128, 4, 16], "int32"), "vr": ("sbuf", [128, 12, 8], "int32"), "wI": ("sbuf", [128, 8, 16], "int32"),
    "sm": ("sbuf", [128, 8 * NS, 16], "float32"), "su": ("sbuf", [128, 8 * 6, 16], "uint16"),
    "P16": ("sbuf", [128, 3, 128], "uint16"), "Pf": ("sbuf", [128, 3, 128], "float32"), "Pm": ("sbuf", [128, 2, 128], "float16"),
    "OZ": ("sbuf", [128, 12, 128], "bfloat16"), "LZ": ("sbuf", [128, 12, 128], "bfloat16"),
    "zT": ("sbuf", [128, 2, 128], "bfloat16"), "xg": ("sbuf", [128, 4096], "bfloat16"), "cx": ("sbuf", [128, 8], "float32"),
    "zq": ("sbuf", [128, 2, 128], "bfloat16"), "lv": ("sbuf", [128, 4, 512], "bfloat16"),
    "near": ("sbuf", [128, 16, 16, 17], "bfloat16"), "key": ("sbuf", [128, 4, 136], "float32"),
    "kr": ("sbuf", [128, 4, 128], "uint16"), "kf": ("sbuf", [128, 4, 128], "float32"), "D": ("sbuf", [128, 6 * 136], "float32"), "yo": ("sbuf", [128, 2, 272], "float32"),
    "eq": ("sbuf", [128, 32, 8, 17], "float16"), "lh": ("sbuf", [128, 16, 128], "float16"),
    "cs": ("sbuf", [128, 2, 128], "float32"), "ys": ("sbuf", [128, 2, 128], "float32"), "hs": ("sbuf", [128, 2, 128], "float32"),
    "cnt": ("sbuf", [128, 96], "float32"), "col": ("sbuf", [128, 64], "float32"), "coli": ("sbuf", [128, 16], "int32"),
    "colb": ("sbuf", [128, 8], "bfloat16"),
    "iof": ("sbuf", [128, 144], "float32"), "cm": ("sbuf", [128, 256], "float32"), "jg": ("sbuf", [128, 128], "float32"),
    "i2k": ("sbuf", [128, ST], "float32"),
    "ident": ("sbuf", [128, 128], "bfloat16"), "identF": ("sbuf", [128, 128], "float32"), "E": ("sbuf", [128, 2048], "bfloat16"),
    "eye": ("sbuf", [128, 2048], "bfloat16"), "iK": ("sbuf", [128, 8, 128], "float16"),
    "Z": ("sbuf", [128, 144], "bfloat16"), "Zu": ("sbuf", [128, 144], "bfloat16"), "Z1": ("sbuf", [128, 144], "float16"),
    "BO": ("sbuf", [128, 128], "float32"), "Wl": ("sbuf", [128, 8, 128], "bfloat16"), "pw": ("sbuf", [128, 128], "float32"),
    "thr": ("sbuf", [128, 8, 17], "bfloat16"), "half": ("sbuf", [128, 136], "bfloat16"),
    "ta": ("sbuf", [128, 8, 128], "float32"), "d0T": ("sbuf", [128, 2, 136], "float32"),
    "dum": ("sbuf", [128, 16], "float32"), "stg": ("sbuf", [128, 48], "float32"),
    "dgb": ("sbuf", [128, 2, 128], "bfloat16"), "tw": ("sbuf", [128, 3, 128], "float32"),
    "pd0": ("psum", [128, 512], "float32"), "pd1": ("psum", [128, 512], "float32"), "pd2": ("psum", [128, 512], "float32"),
    "pd3": ("psum", [128, 512], "float32"), "pd4": ("psum", [128, 512], "float32"), "pd5": ("psum", [128, 512], "float32"),
    "pd6": ("psum", [128, 512], "float32"), "pd7": ("psum", [128, 512], "float32"),
}
PSUM = tuple("pd%d" % i for i in range(8))
SEMAPHORES = (["cV", "cS", "cP", "cG", "sent"] + ["d%d" % i for i in range(30)] + ["f%d" % i for i in range(16)]
              + ["t%d" % i for i in range(16)] + ["b%d" % i for i in range(16)] + ["n%d" % i for i in range(16)]
              + ["u%d" % i for i in range(4)])
ORDER = {}


def make_ops(g, core, T, topo, rank, banks):
    pr = PARAM
    uses = [0]

    def bank():
        uses[0] += 1
        name = "#%d" % uses[0]
        return T[banks.get(name, PSUM[0])], name

    V, S, PE = g.vector, g.scalar, g.tensor
    ops = []
    ndma = [0]
    lift = [0.0]
    ahead = [0.0]

    def op(eng, fn, cost, r, w, sems=None):
        ops.append({"e": eng, "fn": fn, "k": cost, "r": list(r), "w": list(w), "sems": sems, "lift": lift[0], "first": ahead[0]})

    def ts(out, in0, s1, o0, s2, o1, n, r, w, c=1.0, kind="v"):
        if o1 is None:
            op("V", lambda: [V.tensor_scalar(out, in0, s1, None, o0)], (kind, n * c), r, w)
        else:
            op("V", lambda: [V.tensor_scalar(out, in0, s1, s2, o0, o1)], (kind, n * c), r, w)

    def tt(out, a, b, o, n, r, w, c=2.0, kind="v"):
        op("V", lambda: [V.tensor_tensor(out, a, b, o)], (kind, n * c), r, w)

    def cp(out, a, n, r, w, c=1.0, kind="v"):
        op("V", lambda: [V.tensor_copy(out, a)], (kind, n * c), r, w)

    def scan(out, d0, d1, o0, o1, n, r, w, init=0.0):
        op("V", lambda: [V.tensor_tensor_scan(out, d0, d1, init, o0, o1)], ("v", n), r, w)

    def ms(ap, val, n, w):
        op("V", lambda: [V.memset(ap, val)], ("v", n), [], w)

    def act(out, in_, f, n, r, w, bias=None, scale=None, ind=False):
        kw = {}
        if bias is not None:
            kw["bias"] = bias
        if scale is not None:
            kw["scale"] = scale
        op("S", lambda: [S.activation(out, in_, f, **kw)], ("sg" if ind else "s", n), r, w)

    def mm(out, pairs, n, r, w, passes=0, first=True, last=True):
        def fn():
            return [PE.matmul(out, l, x, first and i == 0, last and i == len(pairs) - 1) for i, (l, x) in enumerate(pairs)]
        op("P", fn, ("p", (passes or len(pairs)) * max(64, n)), r, w)

    def iota(out, pat, base, cm_, n, w, fl=True):
        if fl:
            op("G", lambda: [g.iota(out, pat, base, cm_, allow_small_or_imprecise_dtypes=True)], ("g", n), [], w)
        else:
            op("G", lambda: [g.iota(out, pat, base, cm_)], ("g", n), [], w)

    def dma(out, in_, nbytes, r, w, cast=False):
        name = "d%d" % ndma[0]
        ndma[0] += 1
        if cast:
            op("C", lambda: [g.dma_start(out, in_)], ("c", nbytes), r, w, {"": name})
        else:
            op("Y", lambda: [g.sync.dma_start(out, in_)], ("y", nbytes), r, w, {"": name})

    def send(trs, r):
        n = len(trs)
        cuts = {1: (0, 4), 2: (0, 2, 4), 3: (0, 2, 3, 4)}[n]
        made, sems = [], {}
        for i, (step, src, dst, sem, name) in enumerate(trs):
            to = T.cores[(rank + step) % len(T.cores)]
            en = topo.engines(core, to)
            part = en[cuts[i] * len(en) // 4:cuts[i + 1] * len(en) // 4]
            rid, pid, _se = topo.addr(to)
            made.append((rid, pid, sum(1 << e for e in part), src, dst, sem))
            sems[name] = (sem, len(part))

        def fn():
            if n == 1:
                rid, pid, mask, src, dst, sem = made[0]
                g.remote_dma(dst, src, T.sem[sem], T.sem.sent, pid, rid, mask)
            else:
                g.remote_dma_fused([RemoteDMATransfer(dst_ids=[DstId(rid=rid, pnc=pid)], dma_engine_mask=mask, remote_sem=T.sem[sem],
                                                      src=src, dst=dst) for rid, pid, mask, src, dst, sem in made], local_sem=T.sem.sent)
            return []
        op("R", fn, ("r", n), r, [t[4] for t in trs], sems)

    W = lambda rd, a, b: T.W1[:, 2048 + a:2048 + b] if rd == 0 else T.W2[:, a:b]
    col = lambda i: T.col[:, i:i + 1]
    ta = lambda i: T.ta[:, i, :]

    ahead[0] = 1e6
    for c in range(2):
        dma(T.nbi[:, 512 * c:512 * c + 512], T.nb[:, 512 * c:512 * c + 512], 262144, [], ["nbi%d" % c])
    ahead[0] = 5e5
    dma(T.vi[:], T.v[:], 30000, [], ["vi"])
    dma(T.X0[:, 4096:4352], T.z[:], 65536, [], ["X0d"])
    dma(T.X0[:, 0:4096], T.tracks[:], 1048576, [], ["X0"])
    ahead[0] = 0.0

    iota(T.coli[:, 0:1], [[0, 1]], 0, 1, 1, ["pi"], False)
    iota(T.iof[:], [[1, 144]], 0, 0, 144, ["iof"])
    iota(T.cm[:], [[0, 16], [1, 16]], 0, 0, 256, ["cm"])
    iota(T.jg[:], [[16, 8], [0, 16]], 0, 0, 128, ["jg"])
    iota(T.stg[:], [[16, 48]], ST, 0, 48, ["stg"])
    for c in range(8):
        iota(T.i2k[:, 800 * c:800 * c + 800], [[1, 800]], 800 * c, 0, 800, ["i2k%d" % c])
    IK = ["i2k%d" % c for c in range(8)]
    cm = T.cm[:, 0:128]
    cp(col(0), T.coli[:, 0:1], 1, ["pi"], ["c0"])
    ts(T.coli[:, 4:5], T.coli[:, 0:1], 15, A.bitwise_and, None, None, 1, ["pi"], ["ai"])
    cp(col(1), T.coli[:, 4:5], 1, ["ai"], ["c1"])
    tt(col(2), col(0), col(1), A.subtract, 1, ["c0", "c1"], ["c2"])
    act(col(3), col(2), F.Identity, 1, ["c2"], ["c3"], bias=15.0)
    act(col(4), col(1), F.Identity, 1, ["c1"], ["c4"], bias=4096.0, scale=16.0)
    act(col(5), col(1), F.Identity, 1, ["c1"], ["c5"], bias=1.0, scale=2.0)
    ts(T.ident[:], T.iof[:, 0:128], col(0), A.is_equal, None, None, 128, ["iof", "c0"], ["ident"])
    act(T.identF[:], T.ident[:], F.Copy, 128, ["ident"], ["identF"])
    act(T.dgb[:, 0, :], T.ident[:], F.Copy, 128, ["ident"], ["dgb0"], scale=S0)
    for k in range(16):
        act(T.E[:, k:2048:16], T.ident[:], F.Copy, 128, ["ident"], ["E%d" % k], scale=-1.0)
    EK = ["E%d" % k for k in range(16)]
    ms(ta(0), 0.5, 128, ["ta0"])
    ms(ta(1), 0.0, 128, ["ta1"])
    scan(T.pw[:], ta(0), ta(1), A.mult, A.add, 128, ["ta0", "ta1"], ["pw"], float(2 ** 64))
    ts(ta(2), cm, col(1), A.is_equal, None, None, 128, ["cm", "c1"], ["ta2"])
    tt(ta(3), ta(2), T.pw[:], A.mult, 128, ["ta2", "pw"], ["ta3"])
    op("V", lambda: [V.tensor_reduce(col(7), T.ta[:, 3, 0:16], AxisListType.X, A.add)], ("v", 16), ["ta3"], ["c7"])
    act(col(8), col(7), F.Copy, 1, ["c7"], ["c8"], scale=float(2.0 ** -42))
    ts(T.Z[:], T.iof[:], col(3), A.is_equal, col(8), A.mult, 144, ["iof", "c3", "c8"], ["Z"])
    ts(T.Zu[:], T.iof[:], col(3), A.is_equal, col(5), A.mult, 144, ["iof", "c3", "c5"], ["Zu"])
    ts(T.Z1[:], T.iof[:], col(3), A.is_equal, None, None, 144, ["iof", "c3"], ["Z1"])
    ts(T.BO[:], T.jg[:], col(2), A.is_equal, None, None, 128, ["jg", "c2"], ["BO"])
    for c in range(16):
        act(T.eye[:, 128 * c:128 * c + 128], ta(2), F.Copy, 128, ["ta2"], ["eye%d" % c])
    EYE = ["eye%d" % c for c in range(16)]
    ms(T.tw[:, 0, :], float(2.0 ** -0.75), 128, ["tw0"])
    scan(T.tw[:, 1, :], T.tw[:, 0, :], ta(1), A.mult, A.add, 128, ["tw0", "ta1"], ["tw1"], float(2 ** 90))
    act(T.tw[:, 0, :], ta(2), F.Copy, 128, ["ta2"], ["tw0"], scale=float(2 ** 26))
    tt(T.tw[:, 2, :], T.tw[:, 0, :], T.tw[:, 1, :], A.mult, 128, ["tw0", "tw1"], ["tw2"])
    op("V", lambda: [V.tensor_reduce(col(9), T.tw[:, 2, 0:16], AxisListType.X, A.add)], ("v", 16), ["tw2"], ["c9"])
    act(T.Wl[:, 0, :], T.BO[:], F.Copy, 128, ["BO", "c9"], ["Wl0"], scale=col(9))
    for b in range(1, 8):
        act(T.Wl[:, b, :], T.Wl[:, 0, :], F.Copy, 128, ["Wl0"], ["Wl%d" % b], scale=float(2.0 ** (-12 * b)))
    WL = ["Wl%d" % b for b in range(8)]
    ts(ta(4), cm, col(1), A.not_equal, 1e29, A.mult, 128, ["cm", "c1"], ["ta4"])
    act(ta(5), T.tw[:, 2, :], F.Copy, 128, ["tw2"], ["ta5"], scale=-2.575)
    ms(T.thr[:], 1e29, 68, ["thr"])
    tt(T.thr[:, :, 0:16], ta(4), ta(5), A.add, 128, ["ta4", "ta5", "thr"], ["thr"])
    act(ta(6), cm, F.Identity, 128, ["cm", "c4"], ["ta6"], bias=col(4))
    tt(ta(7), ta(6), T.BO[:], A.mult, 128, ["ta6", "BO"], ["ta7"])
    for b in range(8):
        ts(T.iK[:, b, :], ta(7), 256.0 * b - 4096.0, A.add, None, None, 128, ["ta7"], ["iK%d" % b])
    ts(T.stg[:], T.stg[:], col(1), A.add, None, None, 48, ["stg", "c1"], ["stg"])
    act(T.dum[:], T.stg[:, 0:16], F.Identity, 16, ["stg"], ["dum"], bias=float(SP - ST))
    for i in range(2):
        ms(T.d0T[:, i, :], float(i), 136, ["d0T%d" % i])
        ms(T.d0T[:, i, 0:136:17], -BIG, 8, ["d0T%d" % i])
    act(T.d0T[:, 1, 16:136:17], T.stg[:, 0:8], F.Identity, 8, ["stg"], ["d0T1"], bias=16.0 * ST - 15.0, scale=-16.0)
    ms(T.near[:, :, :, 16:17], -1.0, 128, ["nearz"])
    act(T.idB[:], T.ident[:], F.Copy, 128, ["ident"], ["idB"], scale=BIG)
    DK = ["D%d" % i for i in range(6)]
    ms(T.D[:], -1e29, 816, DK)
    for i in range(3):
        act(T.D[:, 272 * i:272 * i + 272:17], T.dum[:], F.Copy, 16, ["dum"], DK[2 * i:2 * i + 2])
    EQ = ["eq%d/%d" % (e, b) for e in range(4) for b in range(8)]
    ts(T.eq[:, :, :, 16:17], T.cm[:], 0.0, A.mult, None, None, 256, ["cm"], ["eqz"])
    ms(T.half[:, 0:128], -0.5, 64, ["half"])
    ms(T.half[:, 128:136], 4096.0, 8, ["c4k"])
    ms(T.OM[:], 0.0, 256, ["OM"])
    for rd in range(2):
        for c in range(4):
            act(W(rd, SP + 256 * c, SP + 256 * c + 256), T.cm[:], F.Copy, 256, ["cm"],
                ["W%dd" % rd] if c == 0 else ["W%ds%d" % (rd, y) for y in (2 * c - 2, 2 * c - 1)])

    for c in range(2):
        for hi in range(2):
            a = 1024 * hi + 512 * c
            ts(T.nbt[:, a:a + 512], T.nbi[:, 512 * c:512 * c + 512], 12 if hi else 4095, A.logical_shift_right if hi else A.bitwise_and,
               None, None, 512, ["nbi%d" % c], ["nbt%d" % a])
            ts(T.O0[:, 2048 + a:2560 + a], T.nbt[:, a:a + 512], -2048.0, A.add, None, None, 512, ["nbt%d" % a], ["O0/%d" % a])
    OK = [["O0/%d" % a for a in range(0, 2048, 512)], ["W0o"]]
    dma(T.O0[:, 0:2048], T.O0[:, 2048:4096], 1048576, OK[0] + ["X0"], ["O0t"])
    ts(T.v0[:], T.vi[:], 2048.0, A.add, None, None, 16, ["vi"], ["v0"])

    chunk = [0]
    sml = lambda st, i, hs: T.sm[:, NS * st + i, 8 * hs[0]:8 * hs[-1] + 8]
    sul = lambda st, i, hs: T.su[:, 6 * st + i, 8 * hs[0]:8 * hs[-1] + 8]
    ks = lambda n, st, hs: ["%s/%d" % (n, 2 * st + h) for h in hs]
    slot = lambda st, h: (4 if st % 4 == 3 else 2 * (st % 2)) + h
    keys = lambda st, hs: T.D[:, 136 * slot(st, hs[0]) + 16:136 * slot(st, hs[-1]) + 136:17]

    def station(rd, s, h):
        st = 4 * rd + s
        U = 2 * st + h
        k = lambda n: "%s/%d" % (n, U)
        sm = lambda i: sml(st, i, [h])
        su = lambda i: sul(st, i, [h])
        y, p3, u2 = U % 6, U % 3, U % 2
        lo = 6 * rd + 2 * s + h
        li = lo - 2
        Xg = lambda n: T.X0[:, 0:n] if rd == 0 else W(0, XO, XO + n)
        xk, xd = (["X0"], ["X0d"]) if rd == 0 else (["W0x"], ["W0d"])
        dm = T.dum[:, 8 * h:8 * h + 8]
        wI = T.wI[:, st, 8 * h:8 * h + 8]
        if s == 0:
            v, vk = (T.v0[:, 8 * h:8 * h + 8], "v0") if rd == 0 else (T.LV[:, h, 0:8], "LV/%d" % h)
            z, zk = (T.X0[:, 4096 + 128 * h:4224 + 128 * h], "X0d") if rd == 0 else (T.zr[:, 0, 128 * h:128 * h + 128], "zr0/%d" % h)
        else:
            v, vk, z, zk = T.LF[:, li, 0:8], k("LL"), T.LZ[:, li, :], k("LF")
        if s < 3:
            ts(wI, v, 2047, A.bitwise_and, None, None, 8, [vk], [k("w")])
        if s == 0:
            cp(su(0), wI, 8, [k("w")], [k("w16")])
            ow = (T.O0[:, 2048:4096] if rd == 0 else W(0, 0, XO)).indirect(su(0))
            ok = OK[rd] + [k("w16")]
        else:
            ow = (T.O0 if rd == 0 else T.W1)[:, 0:4096].indirect(T.LN[:, li, 0:8])
            ok = OK[rd] + ["O%dt" % rd, k("LN")]
        act(T.Pf[:, p3, :], ow, F.Copy, 128, ok, ["Pf%d" % p3], ind=True)
        if pr["pS"][s] == "1":
            ts(T.P16[:, p3, :], T.Pf[:, p3, :], 2048.0, A.add, None, None, 128, ["Pf%d" % p3], ["P16%d" % p3])
        else:
            ts(T.P16[:, p3, :], ow, 2048.0, A.add, None, None, 128, ok, ["P16%d" % p3], kind="vg")
        ps, pn = bank()
        mm(ps[:, 0:128], [(z, T.dgb[:, rd, :])], 128, [zk, "dgb%d" % rd], [pn])
        act(T.zT[:, u2, :], ps[:, 0:128], F.Identity, 128, [pn], ["zT%d" % u2], bias=-C0)
        c0 = 0
        for c, n in enumerate(pr["ch"][s]):
            a, b = 256 * c0, 256 * (c0 + n)
            xn = ["xg%d" % (8 * u2 + i) for i in range(c0, c0 + n)]
            ps, pk_ = bank()
            win = Xg(4096).indirect(T.P16[:, p3, 16 * c0:16 * (c0 + n)])
            xo = T.xg[:, 2048 * u2 + a:2048 * u2 + b]
            if pr["vg"][s][5 * h + c] == "1":
                cp(xo, win, b - a, xk + ["P16%d" % p3], xn, kind="vg")
            else:
                act(xo, win, F.Copy, b - a, xk + ["P16%d" % p3], xn, ind=True)
            mm(ps[:, 0:b - a], [(T.dgb[:, rd, :], xo), (T.zT[:, u2, :], T.E[:, a:b])], b - a, ["dgb%d" % rd, "zT%d" % u2] + xn + EK, [pk_])
            no, nk = T.near[:, 8 * u2 + c0:8 * u2 + c0 + n, :, 0:16], ["near%d" % (8 * u2 + i) for i in range(c0, c0 + n)]
            if pr["sv"][s][5 * h + c] == "1":
                j = chunk[0] % 4
                chunk[0] += 1
                act(T.lv[:, j, 0:b - a], ps[:, 0:b - a], F.Identity, b - a, [pk_], ["lv%d" % j], bias=CB - C0)
                ts(no, T.lv[:, j, 0:b - a], CB, A.is_equal, None, None, b - a, ["lv%d" % j], nk, 0.5)
            else:
                ts(no, ps[:, 0:b - a], CF - C0, A.add, CF, A.is_equal, b - a, [pk_], nk)
            c0 += n
        ps, pn = bank()
        for c in (0, 4):
            mm(ps[:, 17 * c:17 * c + 68], [(T.Z[:, 15 - a:143 - a], T.near[:, 8 * u2 + c:8 * u2 + c + 4, a, :]) for a in range(16)], 68,
               ["Z", "nearz"] + ["near%d" % (8 * u2 + i) for i in range(c, c + 4)], [pn])
        for i in range(2):
            scan(T.key[:, 2 * u2 + i, :], T.d0T[:, i, :], ps[:, 0:136], A.add, A.max, 136, ["d0T%d" % i, pn], ["key%d" % (2 * u2 + i)])
        key, kk = T.key[:, 2 * u2, 16:136:17], "key%d" % (2 * u2)
        tt(sm(2), key, T.key[:, 2 * u2 + 1, 16:136:17], A.subtract, 8, [kk, "key%d" % (2 * u2 + 1)], [k("xo")])
        cp(su(1), sm(2), 8, [k("xo")], [k("nu")])
        m, m1 = T.OM[:, U, 0:8], T.m1[:, U, :]
        if s == 0:
            ts(m, key, M0, A.is_le, BIG, A.mult, 8, [kk, "OM"], [k("m")])
            dead = (T.ident[:], m, k("m"))
        else:
            tt(m1, T.LF[:, li, 8:16], key, A.is_ge, 8, [kk, k("LL")], [k("m1")])
            dead = (T.idB[:], m1, k("m1"))
            if pr["mV"][s] == "1":
                ts(m, m1, BIG, A.mult, None, None, 8, [k("m1"), "OM"], [k("m")])
            else:
                act(m, m1, F.Copy, 8, [k("m1"), "OM"], [k("m")], scale=BIG)
        act(sm(4), dead[1], F.Identity, 8, [dead[2]], [k("gb")], bias=BIG, scale=-1.0 if s == 0 else -BIG)
        back = (-1, T.OM[:, U, :], T.LB[:, li, :], "b%d" % U, "LB/%d" % (U - 2))
        if s == 3:
            send([back], [k("m")])
        zw, zwk = T.xg[:, 2048 * u2:2048 * u2 + 2048].indirect(su(1)), ["xg%d" % (8 * u2 + c) for c in range(8)] + [k("nu")]
        pv, pvk = W(rd, ST + 128 * y, ST + 128 * y + 128), "W%ds%d" % (rd, y)
        if s < 3:
            if pr["zV"][2 * s + h] == "1":
                cp(T.OZ[:, lo, :], zw, 128, zwk, [k("nz")], kind="vg")
            else:
                act(T.OZ[:, lo, :], zw, F.Copy, 128, zwk, [k("nz")], ind=True)
            send([(1, T.OZ[:, lo, :], T.LZ[:, lo, :], "t%d" % U, "LF/%d" % (U + 2))], [k("nz")])
            act(pv, T.OZ[:, lo, :], F.Relu, 128, [k("nz")], [pvk], bias=-37.0)
        else:
            act(pv, zw, F.Relu, 128, zwk, [pvk], bias=-37.0, ind=True)
        tt(T.Pm[:, u2, :], T.eye[:].indirect(su(1)), T.Pf[:, p3, :], A.mult, 128, EYE + [k("nu"), "Pf%d" % p3], ["Pm%d" % u2], 1.0, "vg")
        ps, pn = bank()
        mm(ps[:, 0:8], [(T.Z1[:, 15 - a:143 - a], T.Pm[:, u2, a:128:16]) for a in range(16)] + [(T.ident[:], T.half[:, 128:136]), dead[0:2]], 8,
           ["Z1", "Pm%d" % u2, "ident", "idB", "c4k", dead[2]], [pn])
        nv = ps[:, 0:8]
        if s < 3:
            ts(T.ON[:, lo, :], nv, -2048.0, A.add, 4095.0, A.min, 8, [pn], [k("n16")])
            send([(1, T.ON[:, lo, :], T.LN[:, lo, :], "n%d" % U, "LN/%d" % (U + 2))], [k("n16")])
        if s == 0:
            vr = lambda i: T.vr[:, 6 * rd + 3 * h + i, :]
            tt(vr(0), v, T.ui[:, 2 * rd + 1, 8 * h:8 * h + 8], A.add, 8, [vk, "uj%d" % rd], [k("vr0")])
            ts(vr(1), vr(0), 4095, A.bitwise_and, None, None, 8, [k("vr0")], [k("vr1")])
            ts(vr(2), vr(1), 2048.0, A.add, None, None, 8, [k("vr1")], [k("vr")])
            tt(sm(5), vr(2), sm(4), A.add, 8, [k("vr"), k("gb")], [k("t")])
        else:
            tt(sm(5), v, sm(4), A.add, 8, [vk, k("gb")], [k("t")])
        tt(T.OB[:, U, 0:8], nv, sm(5), A.min, 8, [pn, k("t")], [k("v")])
        tt(T.OB[:, U, 8:16], key, m, A.max, 8, [kk, k("m")], [k("M")])
        if s < 3:
            tt(sm(6), nv, dm, A.min, 8, [pn, "dum"], [k("nv")])
            on = (1, T.OB[:, U, :], T.LF[:, lo, :], "f%d" % U, "LL/%d" % (U + 2))
            send([on, back] if s > 0 else [on], [k("v"), k("M"), k("m")])
        else:
            tt(keys(st, [h]), nv, dm, A.min, 8, [pn, "dum"], [DK[slot(st, h)]])
            send([(1, T.OB[:, U, :], T.LV[:, 2 * rd + h, :], "f%d" % U, "LV/%d" % (2 * rd + h))], [k("v"), k("M")])
        if s == 0:
            ts(su(5), sm(6), -2048.0, A.add, None, None, 8, [k("nv")], [k("n0")])
            act(T.zq[:, h, :], Xg(4352).indirect(su(5)), F.Copy, 128, xk + xd + [k("n0")], ["zq%d" % h], ind=True)
            ps, pn = bank()
            mm(ps[:, 0:128], [(T.ident[:], z), (T.ident[:], T.zq[:, h, :]), (T.ident[:], T.half[:, 0:128])], 128, [zk, "zq%d" % h, "ident", "half"], [pn])
            act(T.zs[:, h, :], ps[:, 0:128], F.Identity, 128, [pn], ["zs%d" % h], bias=C2)
            act(T.zr[:, rd, 128 * h:128 * h + 128], T.zs[:, h, :], F.Identity, 128, ["zs%d" % h], ["zr%d/%d" % (rd, h)], bias=-C2 / 2, scale=0.5)

    edits = [0]

    def edit(rd, s, hs):
        st = 4 * rd + s
        K = lambda n: ks(n, st, hs)
        sm = lambda i: sml(st, i, hs)
        su = lambda i: sul(st, i, hs)
        n = len(hs)
        dk = [DK[slot(st, h)] for h in hs]
        y0 = (2 * st + hs[0]) % 6
        wk = ["W%do" % rd, "W%dx" % rd, "W%dd" % rd]
        if s < 3:
            li = 6 * rd + 2 * s
            fb = T.LB[:, li + hs[0], 0:8] if n == 1 else T.LB[:, li:li + 2, 0:8]
            tt(sm(7), T.wI[:, st, 8 * hs[0]:8 * hs[-1] + 8], fb, A.add, 8, K("w") + K("LB"), K("wm"))
            tt(keys(st, hs), sm(7), sm(6), A.min, 8, K("wm") + K("nv"), dk)
            tt(sm(8), sm(7), T.stg[:, 8 * y0:8 * y0 + 8 * n], A.min, 8, K("wm") + ["stg"], K("go"))
            cp(su(3), sm(8), 8, K("go"), K("g16"))
            tt(sm(9), sm(2), fb, A.add, 8, K("xo") + K("LB"), K("kx"))
        cp(su(2), keys(st, hs), 8, dk, K("k16"))
        ps, pn = bank()
        es = []
        for h in hs:
            e = edits[0] % 4
            edits[0] += 1
            es.append(e)
            row = T.i2k[:].indirect(sul(st, 2, [h]))
            if pr["kS"][2 * s + h] == "1":
                act(T.kf[:, e % 2, :], row, F.Copy, 128, IK + ks("k16", st, [h]), ["kf%d" % (e % 2)], ind=True)
                cp(T.kr[:, e, :], T.kf[:, e % 2, :], 128, ["kf%d" % (e % 2)], ["kr%d" % e])
            else:
                cp(T.kr[:, e, :], row, 128, IK + ks("k16", st, [h]), ["kr%d" % e], kind="vg")
            for b in range(8):
                c = 136 * slot(st, h) + 17 * b + 16
                ts(T.eq[:, 8 * e + b, :, 0:16], T.kr[:, e, :], T.D[:, c:c + 1], A.is_equal, None, None, 128,
                   ["kr%d" % e, DK[slot(st, h)]], [EQ[8 * e + b]], 0.5)
        for i, e in enumerate(es):
            mm(ps[:, 136 * i:136 * i + 136], [(T.Wl[:, b, :], T.eq[:, 8 * e + b, :, :]) for b in range(8)] + [(T.ident[:], T.thr[:])], 136,
               WL + EQ[8 * e:8 * e + 8] + ["eqz", "ident", "thr"], [pn])
        yi = es[0] % 2
        d0 = 136 * slot(st, hs[0])
        scan(T.yo[:, yi, 0:136 * n], T.D[:, d0:d0 + 136 * n], ps[:, 0:136 * n], A.max, A.min, 136 * n, dk + [pn], ["yo%d" % yi])
        cp(su(4), T.yo[:, yi, 16:136 * n:17], 8, ["yo%d" % yi], K("off"))
        for h, e in zip(hs, es):
            y, j = (2 * st + h) % 6, e % 2
            out, ok = W(rd, 0, ST).indirect(sul(st, 4, [h])), ks("off", st, [h])
            if s == 3:
                cp(out, W(rd, ST + 128 * y, ST + 128 * y + 128), 128, ok + ["W%ds%d" % (rd, y)], wk, kind="vs")
                continue
            uk = "US%d" % rd if s == 0 else "LU/%d" % (2 * rd + s - 1)
            for b in range(8):
                c = 8 * h + b
                u = T.US[:, rd, c:c + 1] if s == 0 else T.LU[:, 2 * rd + s - 1, c:c + 1]
                ts(T.lh[:, 8 * j + b, :], T.iK[:, b, :], T.sm[:, NS * st + 9, c:c + 1], A.is_equal, u, A.mult, 128,
                   ["iK%d" % b, uk] + ks("kx", st, [h]), ["lh%d" % (8 * j + b)], 0.5)
            act(T.cs[:, j, :], W(rd, 0, ST + 128 * y + 128).indirect(sul(st, 3, [h])), F.Identity, 128,
                wk + ["W%ds%d" % (rd, i) for i in range(y + 1)] + ks("g16", st, [h]), ["cs%d" % j], ind=True, bias=0.5)
            ps, pn = bank()
            mm(ps[:, 0:128], [(T.lh[:, 8 * j + b, :], T.eq[:, 8 * e + b, :, 0:16]) for b in range(8)], 128,
               ["lh%d" % (8 * j + b) for b in range(8)] + EQ[8 * e:8 * e + 8], [pn], last=False)
            mm(ps[:, 0:128], [(T.identF[:], T.cs[:, j, :])], 128, ["identF", "cs%d" % j], [pn], 4, first=False)
            if pr["hS"][2 * s + h] == "2":
                ts(T.ys[:, j, :], ps[:, 0:128], -0.5, A.add, None, None, 128, [pn], ["ys%d" % j])
            else:
                act(T.ys[:, j, :], ps[:, 0:128], F.Identity, 128, [pn], ["ys%d" % j, pn], bias=-0.5)
            if pr["hS"][2 * s + h] == "1":
                act(T.kf[:, 2 + j, :], ps[:, 0:128], F.Identity, 128, [pn], ["hp%d" % j], bias=CM)
                act(T.hs[:, j, :], T.kf[:, 2 + j, :], F.Identity, 128, ["hp%d" % j], ["hs%d" % j], bias=-CM)
            else:
                ts(T.hs[:, j, :], ps[:, 0:128], CM, A.add, CM, A.subtract, 128, [pn], ["hs%d" % j])
            if s == 2:
                edit(rd, 3, [h])
            tt(out, T.ys[:, j, :], T.hs[:, j, :], A.subtract, 128, ok + ["ys%d" % j, "hs%d" % j], wk, 1.0, "vs")

    def code(rd):
        zk = ["X0d"] if rd == 0 else ["zr0/0", "zr0/1"]
        col16 = lambda a: T.X0[:, 4096 + a:4352:16] if rd == 0 else T.zr[:, 0, a:256:16]
        ps, pn = bank()
        mm(ps[:, 0:16], [(T.Zu[:, 15 - a:143 - a], col16(a)) for a in range(16)], 16, ["Zu"] + zk, [pn])
        ts(T.ui[:, 2 * rd, :], ps[:, 0:16], 2048.0, A.add, None, None, 16, [pn], ["ui%d" % rd])
        ts(T.ui[:, 2 * rd + 1, :], T.ui[:, 2 * rd, :], 4095, A.bitwise_and, None, None, 16, ["ui%d" % rd], ["uj%d" % rd])
        ts(T.US[:, rd, :], T.ui[:, 2 * rd + 1, :], -2048.0, A.add, None, None, 16, ["uj%d" % rd], ["US%d" % rd])
        send([(i + 1, T.US[:, rd, :], T.LU[:, 2 * rd + i, :], "u%d" % (2 * rd + i), "LU/%d" % (2 * rd + i)) for i in range(2)], ["US%d" % rd])

    def nearness():
        ts(T.cnt[:, 0:48], T.LF[:, 0:6, 8:16], BIG, A.is_lt, None, None, 48, ["LL/%d" % U for U in range(2, 8)], ["cnt0"])
        ts(T.cnt[:, 48:96], T.OM[:, 0:6, 0:8], 1.0, A.is_lt, -1.0, A.mult, 48, ["m/%d" % U for U in range(6)], ["cnt1"])
        op("V", lambda: [V.tensor_reduce(col(10), T.cnt[:], AxisListType.X, A.add)], ("v", 96), ["cnt0", "cnt1"], ["c10"])
        ps, pn = bank()
        mm(ps[:, 0:2], [(T.BO[:], T.col[:, 9:11])], 2, ["BO", "c9", "c10"], [pn], 4)
        ts(T.coli[:, 8:9], ps[:, 1:2], 1024.0, A.add, None, None, 1, [pn], ["A0"])
        ts(T.coli[:, 12:13], T.coli[:, 8:9], 3, A.bitwise_and, None, None, 1, ["A0"], ["A1"])
        ts(col(12), T.coli[:, 12:13], 2.0 / 64, A.mult, 49.0 / 64, A.add, 1, ["A1"], ["A2"])
        op("V", lambda: [V.reciprocal(col(16), col(12))], ("v", 250), ["A2"], ["A3"])
        cp(T.colb[:, 0:1], col(16), 1, ["A3"], ["A4"])
        act(col(20), T.colb[:, 0:1], F.Copy, 1, ["A4"], ["A5"])
        act(T.dgb[:, 1, :], T.ident[:], F.Copy, 128, ["ident", "A5"], ["dgb1"], scale=col(20))

    code(0)
    for rd in range(2):
        for s in range(4):
            for h in range(2):
                ahead[0] = pr["ahead"][s] * (1 - h)
                station(rd, s, h)
                ahead[0] = 0.0
                if s == 0 and h == 0:
                    if rd == 0:
                        dma(W(0, 0, XO), T.O0[:, 2048:4096], 1048576, OK[0] + ["O0t"], ["W0o"])
                        dma(W(0, XO, SP), T.tracks[:], 2097152, ["LN/2"], ["W0x"], True)
                    else:
                        dma(W(1, XO, SP), W(0, XO, SP), 2097152, ["W0x", "LN/10"], ["W1x"])
                lift[0] = pr["lift"]
                if s > 0 and (s > pr["both"] or h == 1):
                    edit(rd, s - 1, [h] if s > pr["both"] else [0, 1])
                lift[0] = 0.0
            if rd == 0 and s == 0:
                code(1)
        if rd == 0:
            nearness()
            act(W(0, SP, ST), T.zr[:, 0, :], F.Copy, 256, ["zr0/0", "zr0/1"], ["W0d"])
            dma(T.W1[:, 0:2048], W(0, 0, XO), 1048576, ["W0o"], ["O1t"])
            dma(W(1, 0, XO), W(0, 0, XO), 1048576, ["W0o", "O1t"], ["W1o"])
    dma(T.yz[:], T.zr[:, 1, :], 65536, ["zr1/0", "zr1/1"], ["yz"])
    ts(T.vf[:], T.LV[:, 2:4, 0:8], -2048.0, A.add, None, None, 16, ["LV/2", "LV/3"], ["vf"])
    dma(T.yv[:], T.vf[:], 30000, ["vf"], ["yv"])
    dma(T.yx[:], W(1, XO, SP), 1048576, ["W1x"], ["yx"], True)
    for c in range(4):
        ps, pk_ = bank()
        act(ps[:, 0:256], W(1, 1024 + 256 * c, 1280 + 256 * c), F.Identity, 256, ["W1o"], [pk_], scale=4096.0, bias=2048.0 * 4097)
        tt(T.pk[:, 256 * c:256 * c + 256], ps[:, 0:256], W(1, 256 * c, 256 * c + 256), A.add, 256, [pk_, "W1o"], ["pk%d" % c], 1.0)
        dma(T.yn[:, 256 * c:256 * c + 256], T.pk[:, 256 * c:256 * c + 256], 131072, ["pk%d" % c], ["yn%d" % c])
    return ops


def depend(ops, order, banks):
    last, readers, deps = {}, {}, {}
    for i in order:
        o = ops[i]
        d = {}
        rs = [banks.get(x, x) for x in o["r"]]
        ws = [banks.get(x, x) for x in o["w"]]
        for x in rs:
            if x in last:
                d[(last[x], x)] = 1
        for x in ws:
            if x in last:
                d[(last[x], x)] = 1
            for j in readers.get(x, []):
                d[(j, x)] = 1
        for x in rs:
            readers.setdefault(x, []).append(i)
        for x in ws:
            last[x] = i
            readers[x] = []
        deps[i] = [e for e in d if e[0] != i]
    return deps


def queue(o):
    return "G" if o["e"] in "RC" else o["e"]


def cost(o, pr):
    kind, n = o["k"]
    cyc = pr["cyc"]
    held = {"v": max(64.0, n) * cyc, "s": max(64.0, n) * cyc + 30.0, "vg": 55.0 + n * pr["ga"] * cyc, "sg": 70.0 + n * pr["ga"] * cyc,
            "vs": 55.0 + n * pr["sc"] * cyc, "p": n * pr["pe"] + 30.0, "g": 140.0 + 2 * n * cyc, "y": n / pr["bw"], "c": 1000.0, "r": pr["iss"]}[kind]
    return held, {"r": pr["rem"] + 320.0 * (n - 2), "y": pr["dma"], "c": pr["dma"] + n / pr["bw"]}.get(kind, pr["lat"])


def arrange(ops, deps):
    n = len(ops)
    way = [0.0] * n
    succ = [set() for _ in range(n)]
    cs = [cost(o, PARAM) for o in ops]
    for i in range(n):
        for j, _x in deps[i]:
            succ[j].add(i)
    for i in range(n - 1, -1, -1):
        way[i] = sum(cs[i]) + max([way[j] for j in succ[i]] + [0.0])
    rank_ = [way[i] + (ops[i]["lift"] or ops[i]["first"]) for i in range(n)]
    best = sweep(ops, deps, succ, cs, rank_)
    now = best
    for _ in range(PARAM["turns"]):
        late = backward(ops, deps, succ, cs, now[3])
        rank_ = [late[i] + PARAM["keep"] * (ops[i]["lift"] or ops[i]["first"]) for i in range(n)]
        now = sweep(ops, deps, succ, cs, rank_)
        if now[2] < best[2]:
            best = now
    return best[0:3]


def backward(ops, deps, succ, cs, done):
    n = len(ops)
    left = [len(succ[i]) for i in range(n)]
    ready = [cs[i][1] for i in range(n)]
    free = {q: 0.0 for q in "VSPGY"}
    pool = [i for i in range(n) if left[i] == 0]
    late = [0.0] * n
    while pool:
        best = min(pool, key=lambda i: (max(ready[i], free[queue(ops[i])]), -done[i]))
        q = queue(ops[best])
        soon = max(ready[best], free[q]) + PARAM["back"] * cs[best][0]
        for i in pool:
            if queue(ops[i]) == q and done[i] > done[best] and max(ready[i], free[q]) < soon:
                best = i
        pool.remove(best)
        late[best] = free[q] = max(ready[best], free[q]) + cs[best][0]
        for j in set(j for j, _x in deps[best]):
            ready[j] = max(ready[j], late[best] + cs[j][1])
            left[j] -= 1
            if left[j] == 0:
                pool.append(j)
    return late


def sweep(ops, deps, succ, cs, rank_):
    n = len(ops)
    ends = [0.0] * n
    left = [len(set(j for j, _x in deps[i])) for i in range(n)]
    ready = [0.0] * n
    free = {q: 0.0 for q in "VSPGY"}
    pool = [i for i in range(n) if left[i] == 0]
    order, end = [], 0.0
    use = [([x for x in o["r"] + o["w"] if x[0] == "#"] + [None])[0] for o in ops]
    open_ = {}
    for x in use:
        open_[x] = open_.get(x, 0) + 1
    banks, idle = {}, {b: 0.0 for b in PSUM}

    def start(i):
        t = max(ready[i], free[queue(ops[i])])
        if use[i] is not None and use[i] not in banks:
            if len(idle) <= (PARAM["spare"] if ops[i]["lift"] else 0):
                return 1e18
            t = max(t, min(idle.values()))
        return t
    while pool:
        best = min(pool, key=lambda i: (start(i), -rank_[i]))
        q = queue(ops[best])
        soon = start(best) + PARAM["hold" + (q if q in "PS" else "")] * cs[best][0]
        assert soon < 1e17
        for i in pool:
            if queue(ops[i]) == q and rank_[i] > rank_[best] and start(i) < soon:
                best = i
        t0 = start(best)
        pool.remove(best)
        order.append(best)
        free[q] = t0 + cs[best][0]
        done = free[q] + cs[best][1]
        ends[best] = done
        x = use[best]
        if x is not None:
            if x not in banks:
                banks[x] = min(idle, key=lambda b: idle[b])
                idle.pop(banks[x])
            open_[x] -= 1
            if open_[x] == 0:
                idle[banks[x]] = done
        end = max(end, done)
        for j in succ[best]:
            ready[j] = max(ready[j], done)
            left[j] -= 1
            if left[j] == 0:
                pool.append(j)
    return order, banks, end, ends


def rank_program(g, core, T, topo):
    rank = T.rank_of(core)
    if rank is None:
        return
    if "o" not in ORDER:
        ops = make_ops(g, core, T, topo, rank, {})
        ORDER["o"], ORDER["banks"], ORDER["end"] = arrange(ops, depend(ops, range(len(ops)), {}))
    ops = make_ops(g, core, T, topo, rank, ORDER["banks"])
    deps = depend(ops, ORDER["o"], ORDER["banks"])
    Q = {"V": g.vector, "S": g.scalar, "P": g.tensor, "G": g, "Y": g.sync}
    known = {q: {} for q in Q}
    count = {}
    mark = {}
    for i in ORDER["o"]:
        o = ops[i]
        q = queue(o)
        need = {}
        for j, x in deps[i]:
            if ops[j]["e"] == "R":
                sem, val = ops[j]["sems"][x]
                seen = {}
            else:
                sem, val, seen = mark[j]
            if val > need.get(sem, (0, None))[0]:
                need[sem] = (val, seen)
        for sem in sorted(need, key=lambda s_: -sum(need[s_][1].values())):
            val, seen = need[sem]
            if known[q].get(sem, 0) < val:
                Q[q].wait_ge(T.sem[sem], val)
                known[q][sem] = val
                for s_, v_ in seen.items():
                    if known[q].get(s_, 0) < v_:
                        known[q][s_] = v_
        made = o["fn"]()
        if o["e"] == "R":
            for sem, val in o["sems"].values():
                count[sem] = val
                count["sent"] = count.get("sent", 0) + val
        elif o["e"] in "YC":
            made[0].then_inc(T.sem[o["sems"][""]], 16)
            count[o["sems"][""]] = 16
            mark[i] = (o["sems"][""], 16, dict(known[q]))
        else:
            sem = "c" + q
            for m in made:
                m.then_inc(T.sem[sem], 1)
            count[sem] = count.get(sem, 0) + len(made)
            mark[i] = (sem, count[sem], dict(known[q]))
    for sem, val in count.items():
        if max(known[q].get(sem, 0) for q in known) < val:
            g.sync.wait_ge(T.sem[sem], val)
